import numpy as np
import ml_dtypes


def mxq(x, axis, fmt="e4m3"):
    dtype, down = {"e4m3": (ml_dtypes.float8_e4m3fn, 7), "e5m2": (ml_dtypes.float8_e5m2, 14)}[fmt]
    v = np.moveaxis(np.asarray(x, np.float32).astype(ml_dtypes.bfloat16).astype(np.float64), axis, -1)
    blocks = v.reshape(v.shape[:-1] + (-1, 32))
    amax = np.abs(blocks).max(-1, keepdims=True)
    byte = np.maximum(np.where(amax > 0, np.frexp(amax)[1] - 1 + 127, 0) - down, 1)
    scale = np.exp2(byte - 127.0)
    codes = (blocks / scale).astype(np.float32).astype(dtype).astype(np.float64)
    return np.moveaxis((codes * scale).reshape(v.shape), -1, axis)


WIDE = False


def mx_kscale(k):
    if not WIDE:
        return np.ones(k)
    levels = np.array([10, -10, 5, -5, 0])
    if k % 512:
        return np.exp2(np.random.permutation(np.resize(levels, k // 32))).repeat(32)
    a = np.empty((k // 512, 16))
    for p in range(k // 512):
        a[p, :8] = np.random.permutation(np.resize(levels, 8))
        for g in range(8):
            far = levels[np.abs(levels - a[p, g]) >= 10]
            a[p, g + 8] = far[np.random.randint(len(far))]
    return np.exp2(a.ravel()).repeat(32)


def f64(x):
    return np.asarray(x).astype(np.float64)


def striped(idx):
    return np.tile(idx.reshape(-1, 16).T, (8, 1)).astype(np.uint16)


def unstriped(offs):
    return offs[:16].T.reshape(-1).astype(np.int64)


E2M1 = np.array([0.0, 0.5, 1.0, 1.5, 2.0, 3.0, 4.0, 6.0, -0.0, -0.5, -1.0, -1.5, -2.0, -3.0, -4.0, -6.0])


def pack_weight(w, fmt):
    k, n = w.shape
    w = f64(np.asarray(w, np.float32).astype(ml_dtypes.bfloat16)).reshape(k // 32, 32, n)
    amax = np.abs(w).max(1)
    if fmt == "e4m3":
        byte = np.frexp(amax)[1] - 1 + 127 - 7
    else:
        mant, ex = np.frexp(amax / 6.0)
        byte = np.where(mant > 0.5, ex, ex - 1) + 127
    byte = np.clip(np.where(amax > 0, byte, 1), 1, 254)
    scaled = (w * np.exp2(127.0 - byte)[:, None, :]).reshape(k, n).astype(np.float32)
    by_word = np.ascontiguousarray(scaled.reshape(k // 512, 128, 4, n).transpose(0, 1, 3, 2))
    if fmt == "e4m3":
        words = by_word.astype(ml_dtypes.float8_e4m3fn).view(np.uint8)
    else:
        c = by_word.astype(ml_dtypes.float4_e2m1fn).view(np.uint8) & 0xF
        words = (c[..., 0::2] | (c[..., 1::2] << 4)).reshape(k // 512, 128, 2 * n)
    return np.ascontiguousarray(words), np.ascontiguousarray(byte.astype(np.uint8).reshape(k // 512, 16, n))


def unpack_weight(words, scales, fmt):
    g, _, n = scales.shape
    words = np.ascontiguousarray(words).reshape(g, 128, n, -1)
    if fmt == "e4m3":
        vals = words.view(ml_dtypes.float8_e4m3fn).astype(np.float64)
    else:
        nib = np.empty((g, 128, n, 4), np.uint8)
        nib[..., 0::2] = words & 0xF
        nib[..., 1::2] = words >> 4
        vals = E2M1[nib]
    vals = vals * np.repeat(np.exp2(scales.astype(np.float64) - 127.0), 8, axis=1)[..., None]
    return vals.transpose(0, 1, 3, 2).reshape(g * 512, n)


K, T, E1, C1, E2, C2, H = 256, 1024, 8, 128, 8, 128, 512
N = 1024


def by_expert(wq, xq, E, C):
    return np.concatenate([wq[e].T @ xq[:, e * C:(e + 1) * C] for e in range(E)], axis=1)


def setup_inputs():
    n = np.random.standard_normal
    v = mx_kscale(N)
    u = mx_kscale(H)
    slots1, slots2 = np.random.permutation(T), np.random.permutation(T)
    dy = pack_weight(n((N, T)) * v[:, None], "e4m3")
    w2t = [pack_weight(m, "e2m1") for m in n((E2, N, H)) / np.sqrt(N) / v[None, :, None] * u]
    w1t = [pack_weight(m, "e2m1") for m in n((E1, H, K)) / np.sqrt(H) / u[None, :, None]]
    return {
        "dy_words": dy[0],
        "dy_scales": dy[1],
        "w2t_words": np.stack([m[0] for m in w2t]),
        "w2t_scales": np.stack([m[1] for m in w2t]),
        "w1t_words": np.stack([m[0] for m in w1t]),
        "w1t_scales": np.stack([m[1] for m in w1t]),
        "gate1": (np.tile(np.random.uniform(0.2, 1.0, T), (128, 1))).astype(np.float32),
        "gate2": (np.tile(np.random.uniform(0.2, 1.0, T), (128, 1))).astype(np.float32),
        "offs": striped(slots1),
        "offs2": striped(slots2),
    }


def reference(dy_words, dy_scales, w2t_words, w2t_scales, w1t_words, w1t_scales, gate1, gate2, offs, offs2):
    w2t = np.stack([unpack_weight(w2t_words[e], w2t_scales[e], "e2m1") for e in range(E2)])
    w1t = np.stack([unpack_weight(w1t_words[e], w1t_scales[e], "e2m1") for e in range(E1)])
    idx, idx2 = unstriped(offs), unstriped(offs2)
    gq = unpack_weight(dy_words, dy_scales, "e4m3")[:, idx2]
    dc = np.zeros((H, T))
    dc[:, idx2] = f64(gate2[:1]) * by_expert(w2t, gq, E2, C2)
    da = f64(gate1[:1]) * dc[:, idx]
    out = np.zeros((K, T))
    out[:, idx] = by_expert(w1t, mxq(da, 0, "e4m3"), E1, C1)
    return out

@@ -1,0 +1,221 @@
+from contextlib import ExitStack
+
+import concourse.mybir as mybir
+from concourse.masks import make_identity
+
+F32 = mybir.dt.float32
+BF16 = mybir.dt.bfloat16
+I32 = mybir.dt.int32
+U32 = mybir.dt.uint32
+U16 = mybir.dt.uint16
+U8 = mybir.dt.uint8
+FP8X4 = mybir.dt.float8_e4m3fn_x4
+FP4X4 = mybir.dt.float4_e2m1fn_x4
+MULT = mybir.AluOpType.mult
+COPY = mybir.ActivationFunctionType.Copy
+
+P = 128
+T = 1024
+EXPERTS = 8
+SLOTS = 128
+H = 512
+K = 256
+PASSES = 2
+PLANES = H // P
+ROW_BLOCKS = K // P
+STRIPE = 16
+
+FLOPS = 2 * T * (PASSES * 512 * H + H * K)
+
+SECOND_GROUPS = ((0, 2), (2, 4), (4, 8))
+PAIR = 2
+
+
+def load_scale_rows(nc, plane, rows):
+    by_place = rows.rearrange("(q r) m w -> r q m w", r=4)
+    for r in range(4):
+        nc.sync.dma_start(out=plane[:].bitcast(I32)[r:P:32], in_=by_place[r])
+
+
+def tile_moe_seb_none_kernel(
+    tc, dy_words, dy_scales, w2t_words, w2t_scales, w1t_words, w1t_scales, gate1, gate2, offs, offs2, out
+):
+    nc = tc.nc
+    with ExitStack() as ctx:
+        keep = ctx.enter_context(tc.tile_pool(name="keep", bufs=1))
+        ring = ctx.enter_context(tc.tile_pool(name="ring", bufs=4))
+        psum = ctx.enter_context(tc.psum_pool(name="psum", bufs=8))
+
+        def list_slice(lst, first, last):
+            return lst[:, first * SLOTS // STRIPE : last * SLOTS // STRIPE]
+
+        list2 = keep.tile([P, T // STRIPE], U16, name="list2")
+        nc.sync.dma_start(list2[:], offs2)
+
+        dy_plane = keep.tile([P, PASSES, T], U8, name="dy_plane", tag="early_plane", align_bytes=64)
+        nc.gpsimd.memset(dy_plane[:].bitcast(I32), 0)
+        load_scale_rows(nc, dy_plane, dy_scales.bitcast(I32).rearrange("s b w -> b s w"))
+
+        dy_codes = []
+        for s in range(PASSES):
+            codes = keep.tile([P, T], U32, name="dy_codes", tag=f"early_codes{s}", align_bytes=64)
+            nc.sync.dma_start(out=codes[:].bitcast(I32), in_=dy_words[s].rearrange("p t d -> p (t d)").bitcast(I32))
+            dy_codes.append(codes)
+
+        def load_w2_codes(group, tag):
+            first, last = SECOND_GROUPS[group]
+            codes = keep.tile([P, (last - first) * PASSES, 2 * H], U8, name="w2_codes", tag=tag, align_bytes=64)
+            nc.sync.dma_start(
+                out=codes[:].bitcast(I32), in_=w2t_words.bitcast(I32)[first:last].rearrange("f s p w -> p (f s) w")
+            )
+            return codes
+
+        w2_codes = [load_w2_codes(0, "w2_first")]
+        w2_plane = keep.tile([P, EXPERTS * PASSES, H], U8, name="w2_plane", align_bytes=64)
+        nc.vector.memset(w2_plane[:].bitcast(I32), 0)
+        load_scale_rows(nc, w2_plane, w2t_scales.bitcast(I32).rearrange("f s b w -> b (f s) w"))
+        gate2_sb = keep.tile([P, T], F32, name="gate2_sb")
+        nc.sync.dma_start(out=gate2_sb[:], in_=gate2)
+
+        list1 = keep.tile([P, T // STRIPE], U16, name="list1")
+        nc.sync.dma_start(list1[:], offs)
+
+        gate1_rows = keep.tile([P, SLOTS], F32, name="gate1_rows")
+        nc.gpsimd.memset(gate1_rows[:], 0.0)
+        nc.sync.dma_start(out=gate1_rows[0:EXPERTS, :], in_=gate1[0].rearrange("(e u) -> e u", u=SLOTS))
+
+        w1_plane = keep.tile([P, EXPERTS, K], U8, name="w1_plane", align_bytes=64)
+        nc.vector.memset(w1_plane[:].bitcast(I32), 0)
+        load_scale_rows(nc, w1_plane, w1t_scales.bitcast(I32).rearrange("e s b w -> b (e s) w"))
+
+        identity = keep.tile([P, P], F32, name="identity")
+        make_identity(nc, identity[:])
+
+        got_codes = [keep.tile([P, T], U32, name=f"got_codes{s}", align_bytes=64) for s in range(PASSES)]
+        got_scales = [keep.tile([P, T], U8, name=f"got_scales{s}", align_bytes=64) for s in range(PASSES)]
+        for first, last in ((0, 4), (4, 8)):
+            cols = slice(first * SLOTS, last * SLOTS)
+            for s in range(PASSES):
+                nc.vector.tensor_copy(got_scales[s][:, cols], dy_plane[:, s, :].indirect(list_slice(list2, first, last)))
+        for first, last in ((0, 2), (2, 8)):
+            cols = slice(first * SLOTS, last * SLOTS)
+            for s in range(PASSES):
+                nc.vector.tensor_copy(got_codes[s][:, cols], dy_codes[s][:].indirect(list_slice(list2, first, last)))
+
+        w2_codes.append(load_w2_codes(1, "early_plane"))
+        w2_codes.append(load_w2_codes(2, "early_codes0"))
+        w1_codes = keep.tile([P, EXPERTS, 2 * K], U8, name="w1_codes", tag="early_codes1", align_bytes=64)
+        nc.sync.dma_start(out=w1_codes[:].bitcast(I32), in_=w1t_words.bitcast(I32).rearrange("e s p w -> p (e s) w"))
+
+        dc = [keep.tile([P, T], F32, name=f"dc{t}") for t in range(PLANES)]
+        for group, (first, last) in enumerate(SECOND_GROUPS):
+            width = (last - first) * SLOTS
+            for t in range(PLANES):
+                sums = psum.tile([P, width], F32, name="sums", tag="bank")
+                for f in range(first, last):
+                    cols = slice(f * SLOTS, (f + 1) * SLOTS)
+                    for s in range(PASSES):
+                        matrix = (f - first) * PASSES + s
+                        nc.tensor.matmul_mx(
+                            out=sums[:, (f - first) * SLOTS : (f - first + 1) * SLOTS],
+                            lhsT=w2_codes[group][:, matrix, 2 * P * t : 2 * P * (t + 1)].bitcast(FP4X4),
+                            lhsT_scale=w2_plane[:, f * PASSES + s, P * t : P * (t + 1)],
+                            rhs=got_codes[s][:, cols].bitcast(FP8X4),
+                            rhs_scale=got_scales[s][:, cols],
+                            start=(s == 0),
+                            stop=(s == PASSES - 1),
+                        )
+                if last == EXPERTS and t == PLANES - 1:
+                    staged = keep.tile([P, width], F32, name="staged", tag="last_staged")
+                else:
+                    staged = ring.tile([P, width], F32, name="staged", tag="staged")
+                nc.scalar.copy(staged[:], sums[:])
+                nc.vector.tensor_tensor(
+                    dc[t][:].indirect(list_slice(list2, first, last)),
+                    staged[:],
+                    gate2_sb[:, first * SLOTS : last * SLOTS],
+                    MULT,
+                )
+
+        turned_gate = psum.tile([P, SLOTS], F32, name="turned_gate", tag="bank")
+        nc.tensor.transpose(turned_gate[:], gate1_rows[:], identity[:])
+        gate1_cols = keep.tile([P, EXPERTS], F32, name="gate1_cols")
+        nc.scalar.copy(gate1_cols[:], turned_gate[:, 0:EXPERTS])
+
+        result = [keep.tile([P, T], F32, name=f"result{b}") for b in range(ROW_BLOCKS)]
+        width = PAIR * SLOTS
+        groups = EXPERTS // PAIR
+
+        def pick(g, picked):
+            for t in range(PLANES):
+                nc.vector.tensor_copy(picked[:, t, :], dc[t][:].indirect(list_slice(list1, g * PAIR, (g + 1) * PAIR)))
+
+        def quantise(g, picked):
+            words = psum.tile([P, PAIR * 2 * SLOTS], F32, name="words", tag="bank")
+            for x in range(PAIR):
+                by_slot = psum.tile([P, H], F32, name="by_slot", tag="bank")
+                for t in range(PLANES):
+                    nc.tensor.transpose(
+                        by_slot[:, t * P : (t + 1) * P], picked[:, t, x * SLOTS : (x + 1) * SLOTS], identity[:]
+                    )
+                rounded = keep.tile([P, H], BF16, name="rounded", tag=f"rounded{g}_{x}")
+                nc.scalar.activation(
+                    rounded[:].rearrange("j (u p d) -> j u p d", u=2, d=2),
+                    by_slot[:].rearrange("j (p u d) -> j u p d", u=2, d=2),
+                    COPY,
+                    scale=gate1_cols[:, g * PAIR + x : g * PAIR + x + 1],
+                )
+                pairs = rounded[:].bitcast(F32)
+                for u in range(2):
+                    at = (2 * x + u) * SLOTS
+                    nc.tensor.transpose(words[:, at : at + SLOTS], pairs[:, u * P : (u + 1) * P], identity[:])
+            grouped = keep.tile([P, 4 * width], BF16, name="grouped", tag=f"grouped{g}", align_bytes=64)
+            nc.scalar.copy(
+                grouped[:].bitcast(F32).rearrange("p (x j u) -> p x j u", x=PAIR, u=2),
+                words[:].rearrange("p (x u j) -> p x j u", x=PAIR, u=2),
+            )
+            da_codes = ring.tile([P, width], U32, name="da_codes", align_bytes=64)
+            da_scales = ring.tile([P, width], U8, name="da_scales", align_bytes=64)
+            nc.vector.quantize_mx(out=da_codes[:].bitcast(FP8X4), scales=da_scales[:], in_=grouped[:])
+            return da_codes, da_scales
+
+        def multiply_and_scatter(g, da_codes, da_scales):
+            sums = psum.tile([P, ROW_BLOCKS * width], F32, name="sums", tag="bank")
+            for b in range(ROW_BLOCKS):
+                for x in range(PAIR):
+                    at = b * width + x * SLOTS
+                    cols = slice(x * SLOTS, (x + 1) * SLOTS)
+                    nc.tensor.matmul_mx(
+                        out=sums[:, at : at + SLOTS],
+                        lhsT=w1_codes[:, g * PAIR + x, 2 * P * b : 2 * P * (b + 1)].bitcast(FP4X4),
+                        lhsT_scale=w1_plane[:, g * PAIR + x, P * b : P * (b + 1)],
+                        rhs=da_codes[:, cols].bitcast(FP8X4),
+                        rhs_scale=da_scales[:, cols],
+                        start=True,
+                        stop=True,
+                    )
+            tag = f"rounded{g + 1}_{PAIR - 1}" if g + 1 < groups else "last_sums"
+            staged = keep.tile([P, ROW_BLOCKS * width], F32, name="staged_out", tag=tag)
+            nc.scalar.copy(staged[:], sums[:])
+            offsets = list_slice(list1, g * PAIR, (g + 1) * PAIR)
+            for b in range(ROW_BLOCKS):
+                nc.vector.tensor_copy(result[b][:].indirect(offsets), staged[:, b * width : (b + 1) * width])
+
+        picked_first = keep.tile([P, PLANES, width], F32, name="picked_first")
+        picked_middle = keep.tile([P, 2 * PLANES, width], F32, name="picked_middle", tag="last_staged")
+        pick(0, picked_first)
+        pick(1, picked_middle[:, 0:PLANES, :])
+        pick(2, picked_middle[:, PLANES : 2 * PLANES, :])
+        da = [quantise(0, picked_first)]
+        picked_last = keep.tile([P, PLANES, width], F32, name="picked_last", tag="grouped0", align_bytes=64)
+        pick(3, picked_last)
+        da.append(quantise(1, picked_middle[:, 0:PLANES, :]))
+        multiply_and_scatter(0, *da[0])
+        da.append(quantise(2, picked_middle[:, PLANES : 2 * PLANES, :]))
+        multiply_and_scatter(1, *da[1])
+        da.append(quantise(3, picked_last))
+        multiply_and_scatter(2, *da[2])
+        multiply_and_scatter(3, *da[3])
+
+        for b in range(ROW_BLOCKS):
+            nc.sync.dma_start(out=out[b * P : (b + 1) * P, :], in_=result[b][:])

@@ -1,7 +1,6 @@
 from contextlib import ExitStack
 
 import concourse.mybir as mybir
-from concourse.masks import make_identity
 
 F32 = mybir.dt.float32
 BF16 = mybir.dt.bfloat16
@@ -29,6 +28,7 @@ FLOPS = 2 * T * (PASSES * 512 * H + H * K)
 
 SECOND_GROUPS = ((0, 2), (2, 4), (4, 8))
 PAIR = 2
+HALF = 4
 
 
 def load_scale_rows(nc, plane, rows):
@@ -52,9 +52,27 @@ def tile_moe_seb_none_kernel(
         list2 = keep.tile([P, T // STRIPE], U16, name="list2")
         nc.sync.dma_start(list2[:], offs2)
 
-        dy_plane = keep.tile([P, PASSES, T], U8, name="dy_plane", tag="early_plane", align_bytes=64)
+        list1 = keep.tile([P, T // STRIPE], U16, name="list1")
+        nc.sync.dma_start(list1[:], offs)
+
+        dy_plane = keep.tile([P, T], U8, name="dy_plane", tag="dy_plane", align_bytes=64)
         nc.gpsimd.memset(dy_plane[:].bitcast(I32), 0)
-        load_scale_rows(nc, dy_plane, dy_scales.bitcast(I32).rearrange("s b w -> b s w"))
+        by_quadrant = dy_scales.bitcast(I32).rearrange("s (q r) w -> q s r w", r=4)
+        for q in range(4):
+            nc.sync.dma_start(out=dy_plane[:].bitcast(I32)[32 * q : 32 * q + 4 * PASSES], in_=by_quadrant[q])
+
+        identity = keep.tile([P, P], F32, name="identity")
+        ones = keep.tile([P, P], F32, name="ones", tag="early_codes1", align_bytes=64)
+        nc.gpsimd.memset(ones[:], 1.0)
+        nc.gpsimd.affine_select(
+            out=identity[:],
+            in_=ones[:],
+            pattern=[[-1, P]],
+            compare_op=mybir.AluOpType.is_equal,
+            fill=0.0,
+            base=0,
+            channel_multiplier=1,
+        )
 
         dy_codes = []
         for s in range(PASSES):
@@ -62,54 +80,54 @@ def tile_moe_seb_none_kernel(
             nc.sync.dma_start(out=codes[:].bitcast(I32), in_=dy_words[s].rearrange("p t d -> p (t d)").bitcast(I32))
             dy_codes.append(codes)
 
-        def load_w2_codes(group, tag):
+        def load_w2_codes(group, pool, tag):
             first, last = SECOND_GROUPS[group]
-            codes = keep.tile([P, (last - first) * PASSES, 2 * H], U8, name="w2_codes", tag=tag, align_bytes=64)
+            codes = pool.tile([P, (last - first) * PASSES, 2 * H], U8, name="w2_codes", tag=tag, align_bytes=64)
             nc.sync.dma_start(
                 out=codes[:].bitcast(I32), in_=w2t_words.bitcast(I32)[first:last].rearrange("f s p w -> p (f s) w")
             )
             return codes
 
-        w2_codes = [load_w2_codes(0, "w2_first")]
-        w2_plane = keep.tile([P, EXPERTS * PASSES, H], U8, name="w2_plane", align_bytes=64)
-        nc.vector.memset(w2_plane[:].bitcast(I32), 0)
-        load_scale_rows(nc, w2_plane, w2t_scales.bitcast(I32).rearrange("f s b w -> b (f s) w"))
-        gate2_sb = keep.tile([P, T], F32, name="gate2_sb")
-        nc.sync.dma_start(out=gate2_sb[:], in_=gate2)
+        def load_w2_scales(first, last):
+            load_scale_rows(nc, weight_plane, w2t_scales.bitcast(I32)[first:last].rearrange("f s b w -> b (f s) w"))
 
-        list1 = keep.tile([P, T // STRIPE], U16, name="list1")
-        nc.sync.dma_start(list1[:], offs)
-
-        gate1_rows = keep.tile([P, SLOTS], F32, name="gate1_rows")
-        nc.gpsimd.memset(gate1_rows[:], 0.0)
-        nc.sync.dma_start(out=gate1_rows[0:EXPERTS, :], in_=gate1[0].rearrange("(e u) -> e u", u=SLOTS))
-
-        w1_plane = keep.tile([P, EXPERTS, K], U8, name="w1_plane", align_bytes=64)
-        nc.vector.memset(w1_plane[:].bitcast(I32), 0)
-        load_scale_rows(nc, w1_plane, w1t_scales.bitcast(I32).rearrange("e s b w -> b (e s) w"))
-
-        identity = keep.tile([P, P], F32, name="identity")
-        make_identity(nc, identity[:])
+        w2_codes = [load_w2_codes(0, keep, "w2_first")]
+        weight_plane = keep.tile([P, HALF * PASSES, H], U8, name="weight_plane", align_bytes=64)
+        nc.vector.memset(weight_plane[:].bitcast(I32), 0)
+        load_w2_scales(0, HALF)
+        lead = SECOND_GROUPS[0][1] * SLOTS
+        gate2_lead = keep.tile([P, lead], F32, name="gate2_lead")
+        nc.gpsimd.dma_start(out=gate2_lead[:], in_=gate2[:, 0:lead])
 
         got_codes = [keep.tile([P, T], U32, name=f"got_codes{s}", align_bytes=64) for s in range(PASSES)]
-        got_scales = [keep.tile([P, T], U8, name=f"got_scales{s}", align_bytes=64) for s in range(PASSES)]
-        for first, last in ((0, 4), (4, 8)):
+        got_plane = keep.tile([P, T], U8, name="got_plane", align_bytes=64)
+        moved_plane = keep.tile([P, T], U8, name="moved_plane", align_bytes=64)
+        nc.gpsimd.memset(moved_plane[:].bitcast(I32), 0)
+        got_scales = [got_plane, moved_plane]
+        for first, last in ((0, 2), (2, 8)):
             cols = slice(first * SLOTS, last * SLOTS)
-            for s in range(PASSES):
-                nc.vector.tensor_copy(got_scales[s][:, cols], dy_plane[:, s, :].indirect(list_slice(list2, first, last)))
+            nc.vector.tensor_copy(got_plane[:, cols], dy_plane[:].indirect(list_slice(list2, first, last)))
+            for q in range(4):
+                nc.scalar.dma_start(
+                    out=moved_plane[32 * q : 32 * q + 4, cols].bitcast(I32),
+                    in_=got_plane[32 * q + 4 : 32 * q + 8, cols].bitcast(I32),
+                )
         for first, last in ((0, 2), (2, 8)):
             cols = slice(first * SLOTS, last * SLOTS)
             for s in range(PASSES):
                 nc.vector.tensor_copy(got_codes[s][:, cols], dy_codes[s][:].indirect(list_slice(list2, first, last)))
 
-        w2_codes.append(load_w2_codes(1, "early_plane"))
-        w2_codes.append(load_w2_codes(2, "early_codes0"))
-        w1_codes = keep.tile([P, EXPERTS, 2 * K], U8, name="w1_codes", tag="early_codes1", align_bytes=64)
-        nc.sync.dma_start(out=w1_codes[:].bitcast(I32), in_=w1t_words.bitcast(I32).rearrange("e s p w -> p (e s) w"))
+        w2_codes.append(load_w2_codes(1, keep, "dy_plane"))
+        w2_codes.append(load_w2_codes(2, keep, "early_codes0"))
+        gate2_rest = keep.tile([P, T - lead], F32, name="gate2_rest", tag="early_codes1", align_bytes=64)
+        nc.sync.dma_start(out=gate2_rest[:], in_=gate2[:, lead:T])
+        gate2_parts = (gate2_lead[:], gate2_rest[:, 0:lead], gate2_rest[:, lead : T - lead])
 
         dc = [keep.tile([P, T], F32, name=f"dc{t}") for t in range(PLANES)]
         for group, (first, last) in enumerate(SECOND_GROUPS):
             width = (last - first) * SLOTS
+            if first == HALF:
+                load_w2_scales(HALF, EXPERTS)
             for t in range(PLANES):
                 sums = psum.tile([P, width], F32, name="sums", tag="bank")
                 for f in range(first, last):
@@ -119,7 +137,7 @@ def tile_moe_seb_none_kernel(
                         nc.tensor.matmul_mx(
                             out=sums[:, (f - first) * SLOTS : (f - first + 1) * SLOTS],
                             lhsT=w2_codes[group][:, matrix, 2 * P * t : 2 * P * (t + 1)].bitcast(FP4X4),
-                            lhsT_scale=w2_plane[:, f * PASSES + s, P * t : P * (t + 1)],
+                            lhsT_scale=weight_plane[:, (f % HALF) * PASSES + s, P * t : P * (t + 1)],
                             rhs=got_codes[s][:, cols].bitcast(FP8X4),
                             rhs_scale=got_scales[s][:, cols],
                             start=(s == 0),
@@ -133,10 +151,17 @@ def tile_moe_seb_none_kernel(
                 nc.vector.tensor_tensor(
                     dc[t][:].indirect(list_slice(list2, first, last)),
                     staged[:],
-                    gate2_sb[:, first * SLOTS : last * SLOTS],
+                    gate2_parts[group],
                     MULT,
                 )
 
+        gate1_rows = keep.tile([P, SLOTS], F32, name="gate1_rows", tag="w2_first", align_bytes=64)
+        nc.gpsimd.memset(gate1_rows[:], 0.0)
+        nc.sync.dma_start(out=gate1_rows[0:EXPERTS, :], in_=gate1[0].rearrange("(e u) -> e u", u=SLOTS))
+        w1_codes = keep.tile([P, EXPERTS, 2 * K], U8, name="w1_codes", tag="dy_plane", align_bytes=64)
+        nc.sync.dma_start(out=w1_codes[:].bitcast(I32), in_=w1t_words.bitcast(I32).rearrange("e s p w -> p (e s) w"))
+        w1_plane = weight_plane[:, :, 0:K]
+        load_scale_rows(nc, w1_plane, w1t_scales.bitcast(I32).rearrange("e s b w -> b (e s) w"))
         turned_gate = psum.tile([P, SLOTS], F32, name="turned_gate", tag="bank")
         nc.tensor.transpose(turned_gate[:], gate1_rows[:], identity[:])
         gate1_cols = keep.tile([P, EXPERTS], F32, name="gate1_cols")

@@ -108,7 +108,7 @@ def tile_moe_seb_none_kernel(
             cols = slice(first * SLOTS, last * SLOTS)
             nc.vector.tensor_copy(got_plane[:, cols], dy_plane[:].indirect(list_slice(list2, first, last)))
             for q in range(4):
-                nc.scalar.dma_start(
+                nc.sync.dma_start(
                     out=moved_plane[32 * q : 32 * q + 4, cols].bitcast(I32),
                     in_=got_plane[32 * q + 4 : 32 * q + 8, cols].bitcast(I32),
                 )
@@ -243,4 +243,6 @@ def tile_moe_seb_none_kernel(
         multiply_and_scatter(3, *da[3])
 
         for b in range(ROW_BLOCKS):
-            nc.sync.dma_start(out=out[b * P : (b + 1) * P, :], in_=result[b][:])
+            rows = slice(b * P, (b + 1) * P)
+            nc.sync.dma_start(out=out[rows, 0 : T // 2], in_=result[b][:, 0 : T // 2])
+            nc.scalar.dma_start(out=out[rows, T // 2 : T], in_=result[b][:, T // 2 : T])

@@ -19,22 +19,30 @@ EXPERTS = 8
 SLOTS = 128
 H = 512
 K = 256
+PACK = 4
 PASSES = 2
-PLANES = H // P
+DC_TILES = H // P
 ROW_BLOCKS = K // P
 STRIPE = 16
+QUADRANTS = 4
+QUADRANT = P // QUADRANTS
+SCALE_ROWS = 4
+FP4_BYTES = 2
 
-FLOPS = 2 * T * (PASSES * 512 * H + H * K)
+FLOPS = 2 * T * (PASSES * P * PACK * H + H * K)
 
-SECOND_GROUPS = ((0, 2), (2, 4), (4, 8))
 PAIR = 2
 HALF = 4
+SECOND_GROUPS = ((0, PAIR), (PAIR, HALF), (HALF, EXPERTS))
+LEAD_AND_REST = ((0, PAIR), (PAIR, EXPERTS))
+PAIRS = EXPERTS // PAIR
+PAIR_SLOTS = PAIR * SLOTS
 
 
 def load_scale_rows(nc, plane, rows):
-    by_place = rows.rearrange("(q r) m w -> r q m w", r=4)
-    for r in range(4):
-        nc.sync.dma_start(out=plane[:].bitcast(I32)[r:P:32], in_=by_place[r])
+    by_place = rows.rearrange("(q r) m w -> r q m w", r=SCALE_ROWS)
+    for r in range(SCALE_ROWS):
+        nc.sync.dma_start(out=plane[:].bitcast(I32)[r:P:QUADRANT], in_=by_place[r])
 
 
 def tile_moe_seb_none_kernel(
@@ -46,8 +54,8 @@ def tile_moe_seb_none_kernel(
         ring = ctx.enter_context(tc.tile_pool(name="ring", bufs=4))
         psum = ctx.enter_context(tc.psum_pool(name="psum", bufs=8))
 
-        def list_slice(lst, first, last):
-            return lst[:, first * SLOTS // STRIPE : last * SLOTS // STRIPE]
+        def entries(list_tile, first, last):
+            return list_tile[:, first * SLOTS // STRIPE : last * SLOTS // STRIPE]
 
         list2 = keep.tile([P, T // STRIPE], U16, name="list2")
         nc.sync.dma_start(list2[:], offs2)
@@ -57,9 +65,10 @@ def tile_moe_seb_none_kernel(
 
         dy_plane = keep.tile([P, T], U8, name="dy_plane", tag="dy_plane", align_bytes=64)
         nc.gpsimd.memset(dy_plane[:].bitcast(I32), 0)
-        by_quadrant = dy_scales.bitcast(I32).rearrange("s (q r) w -> q s r w", r=4)
-        for q in range(4):
-            nc.sync.dma_start(out=dy_plane[:].bitcast(I32)[32 * q : 32 * q + 4 * PASSES], in_=by_quadrant[q])
+        by_quadrant = dy_scales.bitcast(I32).rearrange("s (q r) w -> q s r w", r=SCALE_ROWS)
+        for q in range(QUADRANTS):
+            base = QUADRANT * q
+            nc.sync.dma_start(out=dy_plane[:].bitcast(I32)[base : base + SCALE_ROWS * PASSES], in_=by_quadrant[q])
 
         identity = keep.tile([P, P], F32, name="identity")
         ones = keep.tile([P, P], F32, name="ones", tag="early_codes1", align_bytes=64)
@@ -76,89 +85,97 @@ def tile_moe_seb_none_kernel(
 
         dy_codes = []
         for s in range(PASSES):
-            codes = keep.tile([P, T], U32, name="dy_codes", tag=f"early_codes{s}", align_bytes=64)
-            nc.sync.dma_start(out=codes[:].bitcast(I32), in_=dy_words[s].rearrange("p t d -> p (t d)").bitcast(I32))
-            dy_codes.append(codes)
-
-        def load_w2_codes(group, pool, tag):
-            first, last = SECOND_GROUPS[group]
-            codes = pool.tile([P, (last - first) * PASSES, 2 * H], U8, name="w2_codes", tag=tag, align_bytes=64)
+            pass_codes = keep.tile([P, T], U32, name="dy_codes", tag=f"early_codes{s}", align_bytes=64)
             nc.sync.dma_start(
-                out=codes[:].bitcast(I32), in_=w2t_words.bitcast(I32)[first:last].rearrange("f s p w -> p (f s) w")
+                out=pass_codes[:].bitcast(I32), in_=dy_words[s].rearrange("p t d -> p (t d)").bitcast(I32)
             )
-            return codes
+            dy_codes.append(pass_codes)
+
+        def load_w2_codes(group, tag):
+            first, last = SECOND_GROUPS[group]
+            group_codes = keep.tile(
+                [P, (last - first) * PASSES, FP4_BYTES * H], U8, name="w2_codes", tag=tag, align_bytes=64
+            )
+            nc.sync.dma_start(
+                out=group_codes[:].bitcast(I32),
+                in_=w2t_words.bitcast(I32)[first:last].rearrange("f s p w -> p (f s) w"),
+            )
+            return group_codes
 
         def load_w2_scales(first, last):
             load_scale_rows(nc, weight_plane, w2t_scales.bitcast(I32)[first:last].rearrange("f s b w -> b (f s) w"))
 
-        w2_codes = [load_w2_codes(0, keep, "w2_first")]
+        w2_codes = [load_w2_codes(0, "w2_first")]
         weight_plane = keep.tile([P, HALF * PASSES, H], U8, name="weight_plane", align_bytes=64)
         nc.vector.memset(weight_plane[:].bitcast(I32), 0)
         load_w2_scales(0, HALF)
-        lead = SECOND_GROUPS[0][1] * SLOTS
-        gate2_lead = keep.tile([P, lead], F32, name="gate2_lead")
-        nc.gpsimd.dma_start(out=gate2_lead[:], in_=gate2[:, 0:lead])
+        gate2_lead = keep.tile([P, PAIR_SLOTS], F32, name="gate2_lead", tag="gate2_lead")
+        nc.gpsimd.dma_start(out=gate2_lead[:], in_=gate2[:, 0:PAIR_SLOTS])
 
         got_codes = [keep.tile([P, T], U32, name=f"got_codes{s}", align_bytes=64) for s in range(PASSES)]
         got_plane = keep.tile([P, T], U8, name="got_plane", align_bytes=64)
         moved_plane = keep.tile([P, T], U8, name="moved_plane", align_bytes=64)
         nc.gpsimd.memset(moved_plane[:].bitcast(I32), 0)
         got_scales = [got_plane, moved_plane]
-        for first, last in ((0, 2), (2, 8)):
+        for first, last in LEAD_AND_REST:
             cols = slice(first * SLOTS, last * SLOTS)
-            nc.vector.tensor_copy(got_plane[:, cols], dy_plane[:].indirect(list_slice(list2, first, last)))
-            for q in range(4):
+            nc.vector.tensor_copy(got_plane[:, cols], dy_plane[:].indirect(entries(list2, first, last)))
+            for q in range(QUADRANTS):
+                base = QUADRANT * q
                 nc.sync.dma_start(
-                    out=moved_plane[32 * q : 32 * q + 4, cols].bitcast(I32),
-                    in_=got_plane[32 * q + 4 : 32 * q + 8, cols].bitcast(I32),
+                    out=moved_plane[base : base + SCALE_ROWS, cols].bitcast(I32),
+                    in_=got_plane[base + SCALE_ROWS : base + 2 * SCALE_ROWS, cols].bitcast(I32),
                 )
-        for first, last in ((0, 2), (2, 8)):
+        for first, last in LEAD_AND_REST:
             cols = slice(first * SLOTS, last * SLOTS)
             for s in range(PASSES):
-                nc.vector.tensor_copy(got_codes[s][:, cols], dy_codes[s][:].indirect(list_slice(list2, first, last)))
+                nc.vector.tensor_copy(got_codes[s][:, cols], dy_codes[s][:].indirect(entries(list2, first, last)))
 
-        w2_codes.append(load_w2_codes(1, keep, "dy_plane"))
-        w2_codes.append(load_w2_codes(2, keep, "early_codes0"))
-        gate2_rest = keep.tile([P, T - lead], F32, name="gate2_rest", tag="early_codes1", align_bytes=64)
-        nc.sync.dma_start(out=gate2_rest[:], in_=gate2[:, lead:T])
-        gate2_parts = (gate2_lead[:], gate2_rest[:, 0:lead], gate2_rest[:, lead : T - lead])
+        w2_codes.append(load_w2_codes(1, "dy_plane"))
+        gate2_rest = keep.tile([P, T - PAIR_SLOTS], F32, name="gate2_rest", tag="early_codes1", align_bytes=64)
+        nc.sync.dma_start(out=gate2_rest[:], in_=gate2[:, PAIR_SLOTS:T])
+        gate2_parts = (gate2_lead[:], gate2_rest[:, 0:PAIR_SLOTS], gate2_rest[:, PAIR_SLOTS : T - PAIR_SLOTS])
 
-        dc = [keep.tile([P, T], F32, name=f"dc{t}") for t in range(PLANES)]
+        dc = [keep.tile([P, T], F32, name=f"dc{t}") for t in range(DC_TILES)]
         for group, (first, last) in enumerate(SECOND_GROUPS):
-            width = (last - first) * SLOTS
+            group_slots = (last - first) * SLOTS
+            if first == PAIR:
+                w2_codes.append(load_w2_codes(2, "w2_first"))
             if first == HALF:
                 load_w2_scales(HALF, EXPERTS)
-            for t in range(PLANES):
-                sums = psum.tile([P, width], F32, name="sums", tag="bank")
+            for t in range(DC_TILES):
+                dc_sums = psum.tile([P, group_slots], F32, name="sums", tag="bank")
                 for f in range(first, last):
                     cols = slice(f * SLOTS, (f + 1) * SLOTS)
                     for s in range(PASSES):
-                        matrix = (f - first) * PASSES + s
+                        words_at = FP4_BYTES * P * t
                         nc.tensor.matmul_mx(
-                            out=sums[:, (f - first) * SLOTS : (f - first + 1) * SLOTS],
-                            lhsT=w2_codes[group][:, matrix, 2 * P * t : 2 * P * (t + 1)].bitcast(FP4X4),
+                            out=dc_sums[:, (f - first) * SLOTS : (f - first + 1) * SLOTS],
+                            lhsT=w2_codes[group][
+                                :, (f - first) * PASSES + s, words_at : words_at + FP4_BYTES * P
+                            ].bitcast(FP4X4),
                             lhsT_scale=weight_plane[:, (f % HALF) * PASSES + s, P * t : P * (t + 1)],
                             rhs=got_codes[s][:, cols].bitcast(FP8X4),
                             rhs_scale=got_scales[s][:, cols],
                             start=(s == 0),
                             stop=(s == PASSES - 1),
                         )
-                if last == EXPERTS and t == PLANES - 1:
-                    staged = keep.tile([P, width], F32, name="staged", tag="last_staged")
+                if last == EXPERTS and t == DC_TILES - 1:
+                    dc_staged = keep.tile([P, group_slots], F32, name="staged", tag="last_staged")
                 else:
-                    staged = ring.tile([P, width], F32, name="staged", tag="staged")
-                nc.scalar.copy(staged[:], sums[:])
+                    dc_staged = ring.tile([P, group_slots], F32, name="staged", tag="staged")
+                nc.scalar.copy(dc_staged[:], dc_sums[:])
                 nc.vector.tensor_tensor(
-                    dc[t][:].indirect(list_slice(list2, first, last)),
-                    staged[:],
+                    dc[t][:].indirect(entries(list2, first, last)),
+                    dc_staged[:],
                     gate2_parts[group],
                     MULT,
                 )
 
-        gate1_rows = keep.tile([P, SLOTS], F32, name="gate1_rows", tag="w2_first", align_bytes=64)
+        gate1_rows = keep.tile([P, SLOTS], F32, name="gate1_rows", tag="gate2_lead")
         nc.gpsimd.memset(gate1_rows[:], 0.0)
         nc.sync.dma_start(out=gate1_rows[0:EXPERTS, :], in_=gate1[0].rearrange("(e u) -> e u", u=SLOTS))
-        w1_codes = keep.tile([P, EXPERTS, 2 * K], U8, name="w1_codes", tag="dy_plane", align_bytes=64)
+        w1_codes = keep.tile([P, EXPERTS, FP4_BYTES * K], U8, name="w1_codes", tag="dy_plane", align_bytes=64)
         nc.sync.dma_start(out=w1_codes[:].bitcast(I32), in_=w1t_words.bitcast(I32).rearrange("e s p w -> p (e s) w"))
         w1_plane = weight_plane[:, :, 0:K]
         load_scale_rows(nc, w1_plane, w1t_scales.bitcast(I32).rearrange("e s b w -> b (e s) w"))
@@ -168,18 +185,16 @@ def tile_moe_seb_none_kernel(
         nc.scalar.copy(gate1_cols[:], turned_gate[:, 0:EXPERTS])
 
         result = [keep.tile([P, T], F32, name=f"result{b}") for b in range(ROW_BLOCKS)]
-        width = PAIR * SLOTS
-        groups = EXPERTS // PAIR
 
         def pick(g, picked):
-            for t in range(PLANES):
-                nc.vector.tensor_copy(picked[:, t, :], dc[t][:].indirect(list_slice(list1, g * PAIR, (g + 1) * PAIR)))
+            for t in range(DC_TILES):
+                nc.vector.tensor_copy(picked[:, t, :], dc[t][:].indirect(entries(list1, g * PAIR, (g + 1) * PAIR)))
 
         def quantise(g, picked):
-            words = psum.tile([P, PAIR * 2 * SLOTS], F32, name="words", tag="bank")
+            turned_pairs = psum.tile([P, PAIR * 2 * SLOTS], F32, name="words", tag="bank")
             for x in range(PAIR):
                 by_slot = psum.tile([P, H], F32, name="by_slot", tag="bank")
-                for t in range(PLANES):
+                for t in range(DC_TILES):
                     nc.tensor.transpose(
                         by_slot[:, t * P : (t + 1) * P], picked[:, t, x * SLOTS : (x + 1) * SLOTS], identity[:]
                     )
@@ -190,57 +205,62 @@ def tile_moe_seb_none_kernel(
                     COPY,
                     scale=gate1_cols[:, g * PAIR + x : g * PAIR + x + 1],
                 )
-                pairs = rounded[:].bitcast(F32)
+                value_pairs = rounded[:].bitcast(F32)
                 for u in range(2):
                     at = (2 * x + u) * SLOTS
-                    nc.tensor.transpose(words[:, at : at + SLOTS], pairs[:, u * P : (u + 1) * P], identity[:])
-            grouped = keep.tile([P, 4 * width], BF16, name="grouped", tag=f"grouped{g}", align_bytes=64)
+                    nc.tensor.transpose(
+                        turned_pairs[:, at : at + SLOTS], value_pairs[:, u * P : (u + 1) * P], identity[:]
+                    )
+            grouped = keep.tile([P, PACK * PAIR_SLOTS], BF16, name="grouped", tag=f"grouped{g}", align_bytes=64)
             nc.scalar.copy(
                 grouped[:].bitcast(F32).rearrange("p (x j u) -> p x j u", x=PAIR, u=2),
-                words[:].rearrange("p (x u j) -> p x j u", x=PAIR, u=2),
+                turned_pairs[:].rearrange("p (x u j) -> p x j u", x=PAIR, u=2),
             )
-            da_codes = ring.tile([P, width], U32, name="da_codes", align_bytes=64)
-            da_scales = ring.tile([P, width], U8, name="da_scales", align_bytes=64)
+            da_codes = ring.tile([P, PAIR_SLOTS], U32, name="da_codes", align_bytes=64)
+            da_scales = ring.tile([P, PAIR_SLOTS], U8, name="da_scales", align_bytes=64)
             nc.vector.quantize_mx(out=da_codes[:].bitcast(FP8X4), scales=da_scales[:], in_=grouped[:])
             return da_codes, da_scales
 
         def multiply_and_scatter(g, da_codes, da_scales):
-            sums = psum.tile([P, ROW_BLOCKS * width], F32, name="sums", tag="bank")
+            out_sums = psum.tile([P, ROW_BLOCKS * PAIR_SLOTS], F32, name="sums", tag="bank")
             for b in range(ROW_BLOCKS):
                 for x in range(PAIR):
-                    at = b * width + x * SLOTS
+                    at = b * PAIR_SLOTS + x * SLOTS
                     cols = slice(x * SLOTS, (x + 1) * SLOTS)
                     nc.tensor.matmul_mx(
-                        out=sums[:, at : at + SLOTS],
-                        lhsT=w1_codes[:, g * PAIR + x, 2 * P * b : 2 * P * (b + 1)].bitcast(FP4X4),
+                        out=out_sums[:, at : at + SLOTS],
+                        lhsT=w1_codes[:, g * PAIR + x, FP4_BYTES * P * b : FP4_BYTES * P * (b + 1)].bitcast(FP4X4),
                         lhsT_scale=w1_plane[:, g * PAIR + x, P * b : P * (b + 1)],
                         rhs=da_codes[:, cols].bitcast(FP8X4),
                         rhs_scale=da_scales[:, cols],
                         start=True,
                         stop=True,
                     )
-            tag = f"rounded{g + 1}_{PAIR - 1}" if g + 1 < groups else "last_sums"
-            staged = keep.tile([P, ROW_BLOCKS * width], F32, name="staged_out", tag=tag)
-            nc.scalar.copy(staged[:], sums[:])
-            offsets = list_slice(list1, g * PAIR, (g + 1) * PAIR)
+            tag = f"rounded{g + 1}_{PAIR - 1}" if g + 1 < PAIRS else "last_sums"
+            out_staged = keep.tile([P, ROW_BLOCKS * PAIR_SLOTS], F32, name="staged_out", tag=tag)
+            nc.scalar.copy(out_staged[:], out_sums[:])
+            offsets = entries(list1, g * PAIR, (g + 1) * PAIR)
             for b in range(ROW_BLOCKS):
-                nc.vector.tensor_copy(result[b][:].indirect(offsets), staged[:, b * width : (b + 1) * width])
+                nc.vector.tensor_copy(
+                    result[b][:].indirect(offsets), out_staged[:, b * PAIR_SLOTS : (b + 1) * PAIR_SLOTS]
+                )
 
-        picked_first = keep.tile([P, PLANES, width], F32, name="picked_first")
-        picked_middle = keep.tile([P, 2 * PLANES, width], F32, name="picked_middle", tag="last_staged")
-        pick(0, picked_first)
-        pick(1, picked_middle[:, 0:PLANES, :])
-        pick(2, picked_middle[:, PLANES : 2 * PLANES, :])
+        picked_first = keep.tile([P, DC_TILES, PAIR_SLOTS], F32, name="picked_first")
+        picked_middle = keep.tile(
+            [P, (PAIRS - 2) * DC_TILES, PAIR_SLOTS], F32, name="picked_middle", tag="last_staged"
+        )
+        picked_pairs = [picked_first]
+        picked_pairs.extend([picked_middle[:, m * DC_TILES : (m + 1) * DC_TILES, :] for m in range(PAIRS - 2)])
+        for g in range(PAIRS - 1):
+            pick(g, picked_pairs[g])
         da = [quantise(0, picked_first)]
-        picked_last = keep.tile([P, PLANES, width], F32, name="picked_last", tag="grouped0", align_bytes=64)
-        pick(3, picked_last)
-        da.append(quantise(1, picked_middle[:, 0:PLANES, :]))
-        multiply_and_scatter(0, *da[0])
-        da.append(quantise(2, picked_middle[:, PLANES : 2 * PLANES, :]))
-        multiply_and_scatter(1, *da[1])
-        da.append(quantise(3, picked_last))
-        multiply_and_scatter(2, *da[2])
-        multiply_and_scatter(3, *da[3])
+        picked_last = keep.tile([P, DC_TILES, PAIR_SLOTS], F32, name="picked_last", tag="grouped0", align_bytes=64)
+        picked_pairs.append(picked_last)
+        pick(PAIRS - 1, picked_last)
+        for g in range(1, PAIRS):
+            da.append(quantise(g, picked_pairs[g]))
+            multiply_and_scatter(g - 1, *da[g - 1])
+        multiply_and_scatter(PAIRS - 1, *da[PAIRS - 1])
 
         for b in range(ROW_BLOCKS):
             rows = slice(b * P, (b + 1) * P)

@@ -31,18 +31,20 @@ FP4_BYTES = 2
 
 FLOPS = 2 * T * (PASSES * P * PACK * H + H * K)
 
+LEAD = 2
 PAIR = 2
-HALF = 4
-SECOND_GROUPS = ((0, PAIR), (PAIR, HALF), (HALF, EXPERTS))
-LEAD_AND_REST = ((0, PAIR), (PAIR, EXPERTS))
-PAIRS = EXPERTS // PAIR
-PAIR_SLOTS = PAIR * SLOTS
+LEAD_SLOTS = LEAD * SLOTS
+BANK = 512
+WIDE_GATHER = 1376
+WIDE_SCATTER = 1536
+PASS_BYTES = T * PACK
+A, B, C = (0, 2), (2, 4), (4, 8)
 
 
 def load_scale_rows(nc, plane, rows):
     by_place = rows.rearrange("(q r) m w -> r q m w", r=SCALE_ROWS)
     for r in range(SCALE_ROWS):
-        nc.sync.dma_start(out=plane[:].bitcast(I32)[r:P:QUADRANT], in_=by_place[r])
+        nc.sync.dma_start(out=plane[r:P:QUADRANT], in_=by_place[r])
 
 
 def tile_moe_seb_none_kernel(
@@ -51,27 +53,59 @@ def tile_moe_seb_none_kernel(
     nc = tc.nc
     with ExitStack() as ctx:
         keep = ctx.enter_context(tc.tile_pool(name="keep", bufs=1))
-        ring = ctx.enter_context(tc.tile_pool(name="ring", bufs=4))
-        psum = ctx.enter_context(tc.psum_pool(name="psum", bufs=8))
+        early = ctx.enter_context(tc.tile_pool(name="early", bufs=1))
+        psum = ctx.enter_context(tc.psum_pool(name="psum", bufs=1))
+
+        def bank(number, width):
+            return psum.tile([P, width], F32, name="bank", tag=f"bank{number}")
 
         def entries(list_tile, first, last):
             return list_tile[:, first * SLOTS // STRIPE : last * SLOTS // STRIPE]
 
+        def slots(first, last):
+            return slice(first * SLOTS, last * SLOTS)
+
         list2 = keep.tile([P, T // STRIPE], U16, name="list2")
         nc.sync.dma_start(list2[:], offs2)
 
-        list1 = keep.tile([P, T // STRIPE], U16, name="list1")
-        nc.sync.dma_start(list1[:], offs)
+        def load_w2_codes(first, last, group_codes):
+            nc.sync.dma_start(
+                out=group_codes[:].bitcast(I32),
+                in_=w2t_words.bitcast(I32)[first:last].rearrange("f s p w -> p (f s) w"),
+            )
+
+        def load_w2_scales(first, last, plane):
+            load_scale_rows(
+                nc,
+                plane[:].bitcast(I32).rearrange("p (m w) -> p m w", m=(last - first) * PASSES),
+                w2t_scales.bitcast(I32)[first:last].rearrange("f s b w -> b (f s) w"),
+            )
 
         dy_plane = keep.tile([P, T], U8, name="dy_plane", tag="dy_plane", align_bytes=64)
         nc.gpsimd.memset(dy_plane[:].bitcast(I32), 0)
         by_quadrant = dy_scales.bitcast(I32).rearrange("s (q r) w -> q s r w", r=SCALE_ROWS)
         for q in range(QUADRANTS):
             base = QUADRANT * q
-            nc.sync.dma_start(out=dy_plane[:].bitcast(I32)[base : base + SCALE_ROWS * PASSES], in_=by_quadrant[q])
+            queue = nc.sync if q % 2 == 0 else nc.scalar
+            queue.dma_start(out=dy_plane[:].bitcast(I32)[base : base + SCALE_ROWS * PASSES], in_=by_quadrant[q])
+
+        dy_codes = []
+        for s, (width, offset) in enumerate(((WIDE_GATHER, PASS_BYTES), (T, 0))):
+            pass_codes = early.tile([P, width], U32, name=f"dy_codes{s}", offset=offset, align_bytes=64)
+            nc.sync.dma_start(
+                out=pass_codes[:, 0:T].bitcast(I32), in_=dy_words[s].rearrange("p t d -> p (t d)").bitcast(I32)
+            )
+            dy_codes.append(pass_codes)
+        lead_plane = keep.tile([P, LEAD * PASSES * H], U8, name="lead_plane", align_bytes=64)
+        nc.vector.memset(lead_plane[:].bitcast(I32), 0)
+        load_w2_scales(0, LEAD, lead_plane)
+        w2_lead = keep.tile([P, LEAD * PASSES, FP4_BYTES * H], U8, name="w2_lead", tag="w2_lead", align_bytes=64)
+        load_w2_codes(0, LEAD, w2_lead)
+        gate2_lead = keep.tile([P, LEAD_SLOTS], F32, name="gate2_lead", tag="gate2_lead", align_bytes=64)
+        nc.sync.dma_start(out=gate2_lead[:], in_=gate2[:, 0:LEAD_SLOTS])
 
         identity = keep.tile([P, P], F32, name="identity")
-        ones = keep.tile([P, P], F32, name="ones", tag="early_codes1", align_bytes=64)
+        ones = keep.tile([P, P], F32, name="ones")
         nc.gpsimd.memset(ones[:], 1.0)
         nc.gpsimd.affine_select(
             out=identity[:],
@@ -83,42 +117,19 @@ def tile_moe_seb_none_kernel(
             channel_multiplier=1,
         )
 
-        dy_codes = []
-        for s in range(PASSES):
-            pass_codes = keep.tile([P, T], U32, name="dy_codes", tag=f"early_codes{s}", align_bytes=64)
-            nc.sync.dma_start(
-                out=pass_codes[:].bitcast(I32), in_=dy_words[s].rearrange("p t d -> p (t d)").bitcast(I32)
-            )
-            dy_codes.append(pass_codes)
-
-        def load_w2_codes(group, tag):
-            first, last = SECOND_GROUPS[group]
-            group_codes = keep.tile(
-                [P, (last - first) * PASSES, FP4_BYTES * H], U8, name="w2_codes", tag=tag, align_bytes=64
-            )
-            nc.sync.dma_start(
-                out=group_codes[:].bitcast(I32),
-                in_=w2t_words.bitcast(I32)[first:last].rearrange("f s p w -> p (f s) w"),
-            )
-            return group_codes
-
-        def load_w2_scales(first, last):
-            load_scale_rows(nc, weight_plane, w2t_scales.bitcast(I32)[first:last].rearrange("f s b w -> b (f s) w"))
-
-        w2_codes = [load_w2_codes(0, "w2_first")]
-        weight_plane = keep.tile([P, HALF * PASSES, H], U8, name="weight_plane", align_bytes=64)
-        nc.vector.memset(weight_plane[:].bitcast(I32), 0)
-        load_w2_scales(0, HALF)
-        gate2_lead = keep.tile([P, PAIR_SLOTS], F32, name="gate2_lead", tag="gate2_lead")
-        nc.gpsimd.dma_start(out=gate2_lead[:], in_=gate2[:, 0:PAIR_SLOTS])
-
-        got_codes = [keep.tile([P, T], U32, name=f"got_codes{s}", align_bytes=64) for s in range(PASSES)]
-        got_plane = keep.tile([P, T], U8, name="got_plane", align_bytes=64)
         moved_plane = keep.tile([P, T], U8, name="moved_plane", align_bytes=64)
-        nc.gpsimd.memset(moved_plane[:].bitcast(I32), 0)
+        nc.vector.memset(moved_plane[:].bitcast(I32), 0)
+
+        list1 = keep.tile([P, T // STRIPE], U16, name="list1")
+        nc.sync.dma_start(list1[:], offs)
+
+        got_codes = [
+            keep.tile([P, T], U32, name=f"got_codes{s}", tag=f"got_codes{s}", align_bytes=64) for s in range(PASSES)
+        ]
+        got_plane = keep.tile([P, T], U8, name="got_plane", align_bytes=64)
         got_scales = [got_plane, moved_plane]
-        for first, last in LEAD_AND_REST:
-            cols = slice(first * SLOTS, last * SLOTS)
+        for first, last in ((0, LEAD), (LEAD, EXPERTS)):
+            cols = slots(first, last)
             nc.vector.tensor_copy(got_plane[:, cols], dy_plane[:].indirect(entries(list2, first, last)))
             for q in range(QUADRANTS):
                 base = QUADRANT * q
@@ -126,141 +137,185 @@ def tile_moe_seb_none_kernel(
                     out=moved_plane[base : base + SCALE_ROWS, cols].bitcast(I32),
                     in_=got_plane[base + SCALE_ROWS : base + 2 * SCALE_ROWS, cols].bitcast(I32),
                 )
-        for first, last in LEAD_AND_REST:
-            cols = slice(first * SLOTS, last * SLOTS)
-            for s in range(PASSES):
-                nc.vector.tensor_copy(got_codes[s][:, cols], dy_codes[s][:].indirect(entries(list2, first, last)))
+        nc.vector.tensor_copy(got_codes[0][:], dy_codes[0][:].indirect(list2[:]))
+        for first, last in ((0, LEAD), (LEAD, EXPERTS)):
+            nc.vector.tensor_copy(
+                got_codes[1][:, slots(first, last)], dy_codes[1][:].indirect(entries(list2, first, last))
+            )
 
-        w2_codes.append(load_w2_codes(1, "dy_plane"))
-        gate2_rest = keep.tile([P, T - PAIR_SLOTS], F32, name="gate2_rest", tag="early_codes1", align_bytes=64)
-        nc.sync.dma_start(out=gate2_rest[:], in_=gate2[:, PAIR_SLOTS:T])
-        gate2_parts = (gate2_lead[:], gate2_rest[:, 0:PAIR_SLOTS], gate2_rest[:, PAIR_SLOTS : T - PAIR_SLOTS])
+        w2_rest = keep.tile(
+            [P, (EXPERTS - LEAD) * PASSES, FP4_BYTES * H], U8, name="w2_rest", tag="dy_plane", align_bytes=64
+        )
+        load_w2_codes(LEAD, EXPERTS, w2_rest)
+        rest_plane = early.tile([P, (EXPERTS - LEAD) * PASSES * H], U8, name="rest_plane", offset=0, align_bytes=64)
+        load_w2_scales(LEAD, EXPERTS, rest_plane)
+        gate2_rest = keep.tile([P, T - LEAD_SLOTS], F32, name="gate2_rest", tag="w2_lead", align_bytes=64)
+        nc.sync.dma_start(out=gate2_rest[:], in_=gate2[:, LEAD_SLOTS:T])
 
-        dc = [keep.tile([P, T], F32, name=f"dc{t}") for t in range(DC_TILES)]
-        for group, (first, last) in enumerate(SECOND_GROUPS):
-            group_slots = (last - first) * SLOTS
-            if first == PAIR:
-                w2_codes.append(load_w2_codes(2, "w2_first"))
-            if first == HALF:
-                load_w2_scales(HALF, EXPERTS)
-            for t in range(DC_TILES):
-                dc_sums = psum.tile([P, group_slots], F32, name="sums", tag="bank")
-                for f in range(first, last):
-                    cols = slice(f * SLOTS, (f + 1) * SLOTS)
+        dc = [keep.tile([P, WIDE_SCATTER], F32, name=f"dc{t}") for t in range(DC_TILES)]
+
+        def second_layer(t, first, last, w2_codes, plane, banks):
+            staged = keep.tile([P, (last - first) * SLOTS], F32, name="staged", tag=f"staged{first}_{t}")
+            half = (last - first) // len(banks)
+            for number, low in zip(banks, range(first, last, half)):
+                dc_sums = bank(number, half * SLOTS)
+                for f in range(low, low + half):
                     for s in range(PASSES):
+                        matrix = (f - first) * PASSES + s
                         words_at = FP4_BYTES * P * t
                         nc.tensor.matmul_mx(
-                            out=dc_sums[:, (f - first) * SLOTS : (f - first + 1) * SLOTS],
-                            lhsT=w2_codes[group][
-                                :, (f - first) * PASSES + s, words_at : words_at + FP4_BYTES * P
-                            ].bitcast(FP4X4),
-                            lhsT_scale=weight_plane[:, (f % HALF) * PASSES + s, P * t : P * (t + 1)],
-                            rhs=got_codes[s][:, cols].bitcast(FP8X4),
-                            rhs_scale=got_scales[s][:, cols],
+                            out=dc_sums[:, slots(f - low, f - low + 1)],
+                            lhsT=w2_codes[:, matrix, words_at : words_at + FP4_BYTES * P].bitcast(FP4X4),
+                            lhsT_scale=plane[:, matrix * H + P * t : matrix * H + P * (t + 1)],
+                            rhs=got_codes[s][:, slots(f, f + 1)].bitcast(FP8X4),
+                            rhs_scale=got_scales[s][:, slots(f, f + 1)],
                             start=(s == 0),
                             stop=(s == PASSES - 1),
                         )
-                if last == EXPERTS and t == DC_TILES - 1:
-                    dc_staged = keep.tile([P, group_slots], F32, name="staged", tag="last_staged")
-                else:
-                    dc_staged = ring.tile([P, group_slots], F32, name="staged", tag="staged")
-                nc.scalar.copy(dc_staged[:], dc_sums[:])
-                nc.vector.tensor_tensor(
-                    dc[t][:].indirect(entries(list2, first, last)),
-                    dc_staged[:],
-                    gate2_parts[group],
-                    MULT,
-                )
+                nc.scalar.copy(staged[:, slots(low - first, low - first + half)], dc_sums[:])
+            return staged
 
-        gate1_rows = keep.tile([P, SLOTS], F32, name="gate1_rows", tag="gate2_lead")
-        nc.gpsimd.memset(gate1_rows[:], 0.0)
+        def scatter_dc(t, first, last, staged, gate):
+            nc.vector.tensor_tensor(dc[t][:].indirect(entries(list2, first, last)), staged[:], gate[:], MULT)
+
+        for t in range(DC_TILES):
+            lead_staged = second_layer(t, 0, LEAD, w2_lead, lead_plane, [t])
+            scatter_dc(t, 0, LEAD, lead_staged, gate2_lead)
+        for t, banks in enumerate(([4, 5], [6, 7], [0, 1])):
+            scatter_dc(t, LEAD, EXPERTS, second_layer(t, LEAD, EXPERTS, w2_rest, rest_plane, banks), gate2_rest)
+        last_staged = second_layer(DC_TILES - 1, LEAD, EXPERTS, w2_rest, rest_plane, [2, 3])
+
+        gate1_rows = keep.tile([P, SLOTS], F32, name="gate1_rows", tag="staged0_0")
         nc.sync.dma_start(out=gate1_rows[0:EXPERTS, :], in_=gate1[0].rearrange("(e u) -> e u", u=SLOTS))
-        w1_codes = keep.tile([P, EXPERTS, FP4_BYTES * K], U8, name="w1_codes", tag="dy_plane", align_bytes=64)
+        w1_codes = keep.tile([P, EXPERTS, FP4_BYTES * K], U8, name="w1_codes", tag="gate2_lead", align_bytes=64)
         nc.sync.dma_start(out=w1_codes[:].bitcast(I32), in_=w1t_words.bitcast(I32).rearrange("e s p w -> p (e s) w"))
-        w1_plane = weight_plane[:, :, 0:K]
-        load_scale_rows(nc, w1_plane, w1t_scales.bitcast(I32).rearrange("e s b w -> b (e s) w"))
-        turned_gate = psum.tile([P, SLOTS], F32, name="turned_gate", tag="bank")
+        load_scale_rows(
+            nc,
+            lead_plane[:].bitcast(I32).rearrange("p (m w) -> p m w", m=EXPERTS),
+            w1t_scales.bitcast(I32).rearrange("e s b w -> b (e s) w"),
+        )
+        turned_gate = bank(1, SLOTS)
         nc.tensor.transpose(turned_gate[:], gate1_rows[:], identity[:])
         gate1_cols = keep.tile([P, EXPERTS], F32, name="gate1_cols")
         nc.scalar.copy(gate1_cols[:], turned_gate[:, 0:EXPERTS])
 
         result = [keep.tile([P, T], F32, name=f"result{b}") for b in range(ROW_BLOCKS)]
+        rounded = [keep.tile([P, H], BF16, name="rounded", tag=f"rounded{e}") for e in range(EXPERTS)]
 
-        def pick(g, picked):
-            for t in range(DC_TILES):
-                nc.vector.tensor_copy(picked[:, t, :], dc[t][:].indirect(entries(list1, g * PAIR, (g + 1) * PAIR)))
+        def pick(t, first, last, tag):
+            picked = keep.tile([P, (last - first) * SLOTS], F32, name="picked", tag=tag, align_bytes=64)
+            width = WIDE_GATHER if last - first == EXPERTS else T
+            nc.vector.tensor_copy(picked[:], dc[t][:, 0:width].indirect(entries(list1, first, last)))
+            return picked, first
 
-        def quantise(g, picked):
-            turned_pairs = psum.tile([P, PAIR * 2 * SLOTS], F32, name="words", tag="bank")
-            for x in range(PAIR):
-                by_slot = psum.tile([P, H], F32, name="by_slot", tag="bank")
-                for t in range(DC_TILES):
-                    nc.tensor.transpose(
-                        by_slot[:, t * P : (t + 1) * P], picked[:, t, x * SLOTS : (x + 1) * SLOTS], identity[:]
-                    )
-                rounded = keep.tile([P, H], BF16, name="rounded", tag=f"rounded{g}_{x}")
-                nc.scalar.activation(
-                    rounded[:].rearrange("j (u p d) -> j u p d", u=2, d=2),
-                    by_slot[:].rearrange("j (p u d) -> j u p d", u=2, d=2),
-                    COPY,
-                    scale=gate1_cols[:, g * PAIR + x : g * PAIR + x + 1],
+        def turn(source, first, last, number):
+            picked, offset = source
+            by_slot = bank(number, (last - first) * P)
+            for e in range(first, last):
+                nc.tensor.transpose(
+                    by_slot[:, slots(e - first, e - first + 1)],
+                    picked[:, slots(e - offset, e - offset + 1)],
+                    identity[:],
                 )
-                value_pairs = rounded[:].bitcast(F32)
+            return by_slot, first
+
+        def round_tile(t, turned, first, last):
+            by_slot, offset = turned
+            for e in range(first, last):
+                nc.scalar.activation(
+                    rounded[e][:].rearrange("j (u p d) -> j u p d", u=2, d=2)[
+                        :, :, t * QUADRANT : (t + 1) * QUADRANT, :
+                    ],
+                    by_slot[:, slots(e - offset, e - offset + 1)].rearrange("j (p u d) -> j u p d", u=2, d=2),
+                    COPY,
+                    scale=gate1_cols[:, e : e + 1],
+                )
+
+        def turn_and_round(t, source, first, last, number):
+            round_tile(t, turn(source, first, last, number), first, last)
+
+        def turn_back(first, last, number, grouped, at):
+            count = last - first
+            turned_pairs = bank(number, count * 2 * SLOTS)
+            for x in range(count):
+                value_pairs = rounded[first + x][:].bitcast(F32)
                 for u in range(2):
-                    at = (2 * x + u) * SLOTS
                     nc.tensor.transpose(
-                        turned_pairs[:, at : at + SLOTS], value_pairs[:, u * P : (u + 1) * P], identity[:]
+                        turned_pairs[:, slots(2 * x + u, 2 * x + u + 1)],
+                        value_pairs[:, u * P : (u + 1) * P],
+                        identity[:],
                     )
-            grouped = keep.tile([P, PACK * PAIR_SLOTS], BF16, name="grouped", tag=f"grouped{g}", align_bytes=64)
             nc.scalar.copy(
-                grouped[:].bitcast(F32).rearrange("p (x j u) -> p x j u", x=PAIR, u=2),
-                turned_pairs[:].rearrange("p (x u j) -> p x j u", x=PAIR, u=2),
+                grouped[:]
+                .bitcast(F32)[:, slots(2 * at, 2 * (at + count))]
+                .rearrange("p (x j u) -> p x j u", x=count, u=2),
+                turned_pairs[:].rearrange("p (x u j) -> p x j u", x=count, u=2),
             )
-            da_codes = ring.tile([P, PAIR_SLOTS], U32, name="da_codes", align_bytes=64)
-            da_scales = ring.tile([P, PAIR_SLOTS], U8, name="da_scales", align_bytes=64)
+
+        def new_grouped(first, last):
+            return keep.tile(
+                [P, PACK * (last - first) * SLOTS], BF16, name="grouped", tag=f"grouped{first}", align_bytes=64
+            )
+
+        def quantise(first, last, grouped):
+            da_codes = keep.tile([P, (last - first) * SLOTS], U32, name=f"da_codes{first}", align_bytes=64)
+            da_scales = keep.tile([P, (last - first) * SLOTS], U8, name=f"da_scales{first}", align_bytes=64)
             nc.vector.quantize_mx(out=da_codes[:].bitcast(FP8X4), scales=da_scales[:], in_=grouped[:])
             return da_codes, da_scales
 
-        def multiply_and_scatter(g, da_codes, da_scales):
-            out_sums = psum.tile([P, ROW_BLOCKS * PAIR_SLOTS], F32, name="sums", tag="bank")
-            for b in range(ROW_BLOCKS):
-                for x in range(PAIR):
-                    at = b * PAIR_SLOTS + x * SLOTS
-                    cols = slice(x * SLOTS, (x + 1) * SLOTS)
-                    nc.tensor.matmul_mx(
-                        out=out_sums[:, at : at + SLOTS],
-                        lhsT=w1_codes[:, g * PAIR + x, FP4_BYTES * P * b : FP4_BYTES * P * (b + 1)].bitcast(FP4X4),
-                        lhsT_scale=w1_plane[:, g * PAIR + x, P * b : P * (b + 1)],
-                        rhs=da_codes[:, cols].bitcast(FP8X4),
-                        rhs_scale=da_scales[:, cols],
-                        start=True,
-                        stop=True,
-                    )
-            tag = f"rounded{g + 1}_{PAIR - 1}" if g + 1 < PAIRS else "last_sums"
-            out_staged = keep.tile([P, ROW_BLOCKS * PAIR_SLOTS], F32, name="staged_out", tag=tag)
-            nc.scalar.copy(out_staged[:], out_sums[:])
-            offsets = entries(list1, g * PAIR, (g + 1) * PAIR)
-            for b in range(ROW_BLOCKS):
-                nc.vector.tensor_copy(
-                    result[b][:].indirect(offsets), out_staged[:, b * PAIR_SLOTS : (b + 1) * PAIR_SLOTS]
+        def first_layer(b, first, last, da, number, tag):
+            da_codes, da_scales = da
+            out_sums = bank(number, (last - first) * SLOTS)
+            for e in range(first, last):
+                cols = slots(e - first, e - first + 1)
+                nc.tensor.matmul_mx(
+                    out=out_sums[:, cols],
+                    lhsT=w1_codes[:, e, FP4_BYTES * P * b : FP4_BYTES * P * (b + 1)].bitcast(FP4X4),
+                    lhsT_scale=lead_plane[:, e * K + P * b : e * K + P * (b + 1)],
+                    rhs=da_codes[:, cols].bitcast(FP8X4),
+                    rhs_scale=da_scales[:, cols],
+                    start=True,
+                    stop=True,
                 )
+            out_staged = keep.tile([P, (last - first) * SLOTS], F32, name="staged_out", tag=tag)
+            nc.scalar.copy(out_staged[:], out_sums[:])
+            nc.vector.tensor_copy(result[b][:].indirect(entries(list1, first, last)), out_staged[:])
 
-        picked_first = keep.tile([P, DC_TILES, PAIR_SLOTS], F32, name="picked_first")
-        picked_middle = keep.tile(
-            [P, (PAIRS - 2) * DC_TILES, PAIR_SLOTS], F32, name="picked_middle", tag="last_staged"
-        )
-        picked_pairs = [picked_first]
-        picked_pairs.extend([picked_middle[:, m * DC_TILES : (m + 1) * DC_TILES, :] for m in range(PAIRS - 2)])
-        for g in range(PAIRS - 1):
-            pick(g, picked_pairs[g])
-        da = [quantise(0, picked_first)]
-        picked_last = keep.tile([P, DC_TILES, PAIR_SLOTS], F32, name="picked_last", tag="grouped0", align_bytes=64)
-        picked_pairs.append(picked_last)
-        pick(PAIRS - 1, picked_last)
-        for g in range(1, PAIRS):
-            da.append(quantise(g, picked_pairs[g]))
-            multiply_and_scatter(g - 1, *da[g - 1])
-        multiply_and_scatter(PAIRS - 1, *da[PAIRS - 1])
+        picked0 = pick(0, 0, EXPERTS, "got_codes0")
+        picked1ab = pick(1, A[0], B[1], "got_codes1")
+        scatter_dc(DC_TILES - 1, LEAD, EXPERTS, last_staged, gate2_rest)
+        turn_and_round(0, picked0, 0, 4, 4)
+        turn_and_round(0, picked0, 4, 8, 5)
+        turn_and_round(1, picked1ab, 0, 4, 6)
+        picked2ab = pick(2, A[0], B[1], "picked2ab")
+        turn_and_round(2, picked2ab, *A, 0)
+        picked3a = pick(3, *A, "picked3a")
+        turn_and_round(3, picked3a, *A, 1)
+        grouped_a = new_grouped(*A)
+        turn_back(0, 1, 2, grouped_a, 0)
+        turn_back(1, 2, 3, grouped_a, 1)
+        picked3bc = pick(3, B[0], C[1], "picked3bc")
+        picked2c = pick(2, *C, "picked2c")
+        da_a = quantise(*A, grouped_a)
+        picked1c = pick(1, *C, "grouped0")
+        first_layer(0, *A, da_a, 4, "out0a")
+        turn_and_round(2, picked2ab, *B, 2)
+        turn_and_round(3, picked3bc, *B, 3)
+        grouped_b = new_grouped(*B)
+        turn_back(*B, 4, grouped_b, 0)
+        da_b = quantise(*B, grouped_b)
+        first_layer(1, *A, da_a, 5, "rounded3")
+        first_layer(0, *B, da_b, 6, "out0b")
+        turn_and_round(3, picked3bc, *C, 2)
+        turn_and_round(2, picked2c, *C, 3)
+        turn_and_round(1, picked1c, *C, 4)
+        grouped_c = new_grouped(*C)
+        turn_back(4, 6, 7, grouped_c, 0)
+        turn_back(6, 8, 0, grouped_c, 2)
+        da_c = quantise(*C, grouped_c)
+        first_layer(1, *B, da_b, 1, "rounded7")
+        first_layer(0, *C, da_c, 5, "out0c")
+        first_layer(1, *C, da_c, 6, "out1c")
 
         for b in range(ROW_BLOCKS):
             rows = slice(b * P, (b + 1) * P)

@@ -38,7 +38,9 @@ BANK = 512
 WIDE_GATHER = 1376
 WIDE_SCATTER = 1536
 PASS_BYTES = T * PACK
-A, B, C = (0, 2), (2, 4), (4, 8)
+BANKS = 8
+PAIRS = EXPERTS // PAIR
+PAIR_SLOTS = PAIR * SLOTS
 
 
 def load_scale_rows(nc, plane, rows):
@@ -54,6 +56,7 @@ def tile_moe_seb_none_kernel(
     with ExitStack() as ctx:
         keep = ctx.enter_context(tc.tile_pool(name="keep", bufs=1))
         early = ctx.enter_context(tc.tile_pool(name="early", bufs=1))
+        ring = ctx.enter_context(tc.tile_pool(name="ring", bufs=4))
         psum = ctx.enter_context(tc.psum_pool(name="psum", bufs=1))
 
         def bank(number, width):
@@ -199,123 +202,90 @@ def tile_moe_seb_none_kernel(
         gate1_cols = keep.tile([P, EXPERTS], F32, name="gate1_cols")
         nc.scalar.copy(gate1_cols[:], turned_gate[:, 0:EXPERTS])
 
+        scatter_dc(DC_TILES - 1, LEAD, EXPERTS, last_staged, gate2_rest)
+        handed_out = []
+
+        def next_bank(width):
+            handed_out.append(width)
+            return bank((len(handed_out) + 3) % BANKS, width)
+
         result = [keep.tile([P, T], F32, name=f"result{b}") for b in range(ROW_BLOCKS)]
-        rounded = [keep.tile([P, H], BF16, name="rounded", tag=f"rounded{e}") for e in range(EXPERTS)]
 
-        def pick(t, first, last, tag):
-            picked = keep.tile([P, (last - first) * SLOTS], F32, name="picked", tag=tag, align_bytes=64)
-            width = WIDE_GATHER if last - first == EXPERTS else T
-            nc.vector.tensor_copy(picked[:], dc[t][:, 0:width].indirect(entries(list1, first, last)))
-            return picked, first
+        def pick(g, picked):
+            for t in range(DC_TILES):
+                nc.vector.tensor_copy(picked[:, t, :], dc[t][:, 0:T].indirect(entries(list1, g * PAIR, (g + 1) * PAIR)))
 
-        def turn(source, first, last, number):
-            picked, offset = source
-            by_slot = bank(number, (last - first) * P)
-            for e in range(first, last):
-                nc.tensor.transpose(
-                    by_slot[:, slots(e - first, e - first + 1)],
-                    picked[:, slots(e - offset, e - offset + 1)],
-                    identity[:],
-                )
-            return by_slot, first
-
-        def round_tile(t, turned, first, last):
-            by_slot, offset = turned
-            for e in range(first, last):
-                nc.scalar.activation(
-                    rounded[e][:].rearrange("j (u p d) -> j u p d", u=2, d=2)[
-                        :, :, t * QUADRANT : (t + 1) * QUADRANT, :
-                    ],
-                    by_slot[:, slots(e - offset, e - offset + 1)].rearrange("j (p u d) -> j u p d", u=2, d=2),
-                    COPY,
-                    scale=gate1_cols[:, e : e + 1],
-                )
-
-        def turn_and_round(t, source, first, last, number):
-            round_tile(t, turn(source, first, last, number), first, last)
-
-        def turn_back(first, last, number, grouped, at):
-            count = last - first
-            turned_pairs = bank(number, count * 2 * SLOTS)
-            for x in range(count):
-                value_pairs = rounded[first + x][:].bitcast(F32)
-                for u in range(2):
+        def quantise(g, picked):
+            turned_pairs = next_bank(PAIR * 2 * SLOTS)
+            for x in range(PAIR):
+                by_slot = next_bank(H)
+                for t in range(DC_TILES):
                     nc.tensor.transpose(
-                        turned_pairs[:, slots(2 * x + u, 2 * x + u + 1)],
-                        value_pairs[:, u * P : (u + 1) * P],
-                        identity[:],
+                        by_slot[:, t * P : (t + 1) * P], picked[:, t, x * SLOTS : (x + 1) * SLOTS], identity[:]
                     )
+                rounded = keep.tile([P, H], BF16, name="rounded", tag=f"rounded{g}_{x}")
+                nc.scalar.activation(
+                    rounded[:].rearrange("j (u p d) -> j u p d", u=2, d=2),
+                    by_slot[:].rearrange("j (p u d) -> j u p d", u=2, d=2),
+                    COPY,
+                    scale=gate1_cols[:, g * PAIR + x : g * PAIR + x + 1],
+                )
+                value_pairs = rounded[:].bitcast(F32)
+                for u in range(2):
+                    at = (2 * x + u) * SLOTS
+                    nc.tensor.transpose(
+                        turned_pairs[:, at : at + SLOTS], value_pairs[:, u * P : (u + 1) * P], identity[:]
+                    )
+            grouped = keep.tile([P, PACK * PAIR_SLOTS], BF16, name="grouped", tag=f"grouped{g}", align_bytes=64)
             nc.scalar.copy(
-                grouped[:]
-                .bitcast(F32)[:, slots(2 * at, 2 * (at + count))]
-                .rearrange("p (x j u) -> p x j u", x=count, u=2),
-                turned_pairs[:].rearrange("p (x u j) -> p x j u", x=count, u=2),
+                grouped[:].bitcast(F32).rearrange("p (x j u) -> p x j u", x=PAIR, u=2),
+                turned_pairs[:].rearrange("p (x u j) -> p x j u", x=PAIR, u=2),
             )
-
-        def new_grouped(first, last):
-            return keep.tile(
-                [P, PACK * (last - first) * SLOTS], BF16, name="grouped", tag=f"grouped{first}", align_bytes=64
-            )
-
-        def quantise(first, last, grouped):
-            da_codes = keep.tile([P, (last - first) * SLOTS], U32, name=f"da_codes{first}", align_bytes=64)
-            da_scales = keep.tile([P, (last - first) * SLOTS], U8, name=f"da_scales{first}", align_bytes=64)
+            da_codes = ring.tile([P, PAIR_SLOTS], U32, name="da_codes", align_bytes=64)
+            da_scales = ring.tile([P, PAIR_SLOTS], U8, name="da_scales", align_bytes=64)
             nc.vector.quantize_mx(out=da_codes[:].bitcast(FP8X4), scales=da_scales[:], in_=grouped[:])
             return da_codes, da_scales
 
-        def first_layer(b, first, last, da, number, tag):
-            da_codes, da_scales = da
-            out_sums = bank(number, (last - first) * SLOTS)
-            for e in range(first, last):
-                cols = slots(e - first, e - first + 1)
-                nc.tensor.matmul_mx(
-                    out=out_sums[:, cols],
-                    lhsT=w1_codes[:, e, FP4_BYTES * P * b : FP4_BYTES * P * (b + 1)].bitcast(FP4X4),
-                    lhsT_scale=lead_plane[:, e * K + P * b : e * K + P * (b + 1)],
-                    rhs=da_codes[:, cols].bitcast(FP8X4),
-                    rhs_scale=da_scales[:, cols],
-                    start=True,
-                    stop=True,
-                )
-            out_staged = keep.tile([P, (last - first) * SLOTS], F32, name="staged_out", tag=tag)
+        def multiply_and_scatter(g, da_codes, da_scales):
+            out_sums = next_bank(ROW_BLOCKS * PAIR_SLOTS)
+            for b in range(ROW_BLOCKS):
+                for x in range(PAIR):
+                    at = b * PAIR_SLOTS + x * SLOTS
+                    cols = slice(x * SLOTS, (x + 1) * SLOTS)
+                    nc.tensor.matmul_mx(
+                        out=out_sums[:, at : at + SLOTS],
+                        lhsT=w1_codes[:, g * PAIR + x, FP4_BYTES * P * b : FP4_BYTES * P * (b + 1)].bitcast(FP4X4),
+                        lhsT_scale=lead_plane[:, (g * PAIR + x) * K + P * b : (g * PAIR + x) * K + P * (b + 1)],
+                        rhs=da_codes[:, cols].bitcast(FP8X4),
+                        rhs_scale=da_scales[:, cols],
+                        start=True,
+                        stop=True,
+                    )
+            tag = f"rounded{g + 1}_{PAIR - 1}" if g + 1 < PAIRS else "last_sums"
+            out_staged = keep.tile([P, ROW_BLOCKS * PAIR_SLOTS], F32, name="staged_out", tag=tag)
             nc.scalar.copy(out_staged[:], out_sums[:])
-            nc.vector.tensor_copy(result[b][:].indirect(entries(list1, first, last)), out_staged[:])
+            offsets = entries(list1, g * PAIR, (g + 1) * PAIR)
+            for b in range(ROW_BLOCKS):
+                nc.vector.tensor_copy(
+                    result[b][:].indirect(offsets), out_staged[:, b * PAIR_SLOTS : (b + 1) * PAIR_SLOTS]
+                )
 
-        picked0 = pick(0, 0, EXPERTS, "got_codes0")
-        picked1ab = pick(1, A[0], B[1], "got_codes1")
-        scatter_dc(DC_TILES - 1, LEAD, EXPERTS, last_staged, gate2_rest)
-        turn_and_round(0, picked0, 0, 4, 4)
-        turn_and_round(0, picked0, 4, 8, 5)
-        turn_and_round(1, picked1ab, 0, 4, 6)
-        picked2ab = pick(2, A[0], B[1], "picked2ab")
-        turn_and_round(2, picked2ab, *A, 0)
-        picked3a = pick(3, *A, "picked3a")
-        turn_and_round(3, picked3a, *A, 1)
-        grouped_a = new_grouped(*A)
-        turn_back(0, 1, 2, grouped_a, 0)
-        turn_back(1, 2, 3, grouped_a, 1)
-        picked3bc = pick(3, B[0], C[1], "picked3bc")
-        picked2c = pick(2, *C, "picked2c")
-        da_a = quantise(*A, grouped_a)
-        picked1c = pick(1, *C, "grouped0")
-        first_layer(0, *A, da_a, 4, "out0a")
-        turn_and_round(2, picked2ab, *B, 2)
-        turn_and_round(3, picked3bc, *B, 3)
-        grouped_b = new_grouped(*B)
-        turn_back(*B, 4, grouped_b, 0)
-        da_b = quantise(*B, grouped_b)
-        first_layer(1, *A, da_a, 5, "rounded3")
-        first_layer(0, *B, da_b, 6, "out0b")
-        turn_and_round(3, picked3bc, *C, 2)
-        turn_and_round(2, picked2c, *C, 3)
-        turn_and_round(1, picked1c, *C, 4)
-        grouped_c = new_grouped(*C)
-        turn_back(4, 6, 7, grouped_c, 0)
-        turn_back(6, 8, 0, grouped_c, 2)
-        da_c = quantise(*C, grouped_c)
-        first_layer(1, *B, da_b, 1, "rounded7")
-        first_layer(0, *C, da_c, 5, "out0c")
-        first_layer(1, *C, da_c, 6, "out1c")
+        picked_first = keep.tile([P, DC_TILES, PAIR_SLOTS], F32, name="picked_first")
+        picked_middle = keep.tile(
+            [P, (PAIRS - 2) * DC_TILES, PAIR_SLOTS], F32, name="picked_middle", tag=f"staged{LEAD}_{DC_TILES - 1}"
+        )
+        picked_pairs = [picked_first]
+        picked_pairs.extend([picked_middle[:, m * DC_TILES : (m + 1) * DC_TILES, :] for m in range(PAIRS - 2)])
+        for g in range(PAIRS - 1):
+            pick(g, picked_pairs[g])
+        da = [quantise(0, picked_first)]
+        picked_last = keep.tile([P, DC_TILES, PAIR_SLOTS], F32, name="picked_last", tag="grouped0", align_bytes=64)
+        picked_pairs.append(picked_last)
+        pick(PAIRS - 1, picked_last)
+        for g in range(1, PAIRS):
+            da.append(quantise(g, picked_pairs[g]))
+            multiply_and_scatter(g - 1, *da[g - 1])
+        multiply_and_scatter(PAIRS - 1, *da[PAIRS - 1])
 
         for b in range(ROW_BLOCKS):
             rows = slice(b * P, (b + 1) * P)

@@ -38,7 +38,15 @@ BANK = 512
 WIDE_GATHER = 1376
 WIDE_SCATTER = 1536
 PASS_BYTES = T * PACK
+LIVE_ROWS = P - QUADRANT + SCALE_ROWS
+SLOT_BANKS = ((4, 5), (6, 7), (0, 1), (2, 4))
+WORD_BANKS = ((6, 7), (0, 1), (2, 4), (5, 6))
+OUT_BANKS = (7, 1, 4, 7)
+LATER = 3
+PLANE_BYTES = LATER * PASSES * H
+CODES_BYTES = FP4_BYTES * PLANE_BYTES
 BANKS = 8
+GROUPS = ((0, LEAD), (LEAD, 5), (5, EXPERTS))
 PAIRS = EXPERTS // PAIR
 PAIR_SLOTS = PAIR * SLOTS
 
@@ -55,8 +63,8 @@ def tile_moe_seb_none_kernel(
     nc = tc.nc
     with ExitStack() as ctx:
         keep = ctx.enter_context(tc.tile_pool(name="keep", bufs=1))
-        early = ctx.enter_context(tc.tile_pool(name="early", bufs=1))
         ring = ctx.enter_context(tc.tile_pool(name="ring", bufs=4))
+        placed = ctx.enter_context(tc.tile_pool(name="placed", bufs=1))
         psum = ctx.enter_context(tc.psum_pool(name="psum", bufs=1))
 
         def bank(number, width):
@@ -84,21 +92,21 @@ def tile_moe_seb_none_kernel(
                 w2t_scales.bitcast(I32)[first:last].rearrange("f s b w -> b (f s) w"),
             )
 
-        dy_plane = keep.tile([P, T], U8, name="dy_plane", tag="dy_plane", align_bytes=64)
-        nc.gpsimd.memset(dy_plane[:].bitcast(I32), 0)
+        zeroed = placed.tile([P, T + PLANE_BYTES], U8, name="zeroed", offset=CODES_BYTES - T, align_bytes=64)
+        dy_plane = zeroed[:, 0:T]
+        nc.gpsimd.memset(dy_plane.bitcast(I32), 0)
         by_quadrant = dy_scales.bitcast(I32).rearrange("s (q r) w -> q s r w", r=SCALE_ROWS)
         for q in range(QUADRANTS):
             base = QUADRANT * q
             queue = nc.sync if q % 2 == 0 else nc.scalar
-            queue.dma_start(out=dy_plane[:].bitcast(I32)[base : base + SCALE_ROWS * PASSES], in_=by_quadrant[q])
+            queue.dma_start(out=dy_plane.bitcast(I32)[base : base + SCALE_ROWS * PASSES], in_=by_quadrant[q])
 
-        dy_codes = []
-        for s, (width, offset) in enumerate(((WIDE_GATHER, PASS_BYTES), (T, 0))):
-            pass_codes = early.tile([P, width], U32, name=f"dy_codes{s}", offset=offset, align_bytes=64)
+        dy_codes = keep.tile([P, PASSES * T], U32, name="dy_codes", tag="dy_codes", align_bytes=64)
+        for s in range(PASSES):
             nc.sync.dma_start(
-                out=pass_codes[:, 0:T].bitcast(I32), in_=dy_words[s].rearrange("p t d -> p (t d)").bitcast(I32)
+                out=dy_codes[:, s * T : (s + 1) * T].bitcast(I32),
+                in_=dy_words[s].rearrange("p t d -> p (t d)").bitcast(I32),
             )
-            dy_codes.append(pass_codes)
         lead_plane = keep.tile([P, LEAD * PASSES * H], U8, name="lead_plane", align_bytes=64)
         nc.vector.memset(lead_plane[:].bitcast(I32), 0)
         load_w2_scales(0, LEAD, lead_plane)
@@ -123,6 +131,8 @@ def tile_moe_seb_none_kernel(
         moved_plane = keep.tile([P, T], U8, name="moved_plane", align_bytes=64)
         nc.vector.memset(moved_plane[:].bitcast(I32), 0)
 
+        nc.vector.memset(zeroed[:, T:].bitcast(I32), 0)
+
         list1 = keep.tile([P, T // STRIPE], U16, name="list1")
         nc.sync.dma_start(list1[:], offs)
 
@@ -133,32 +143,37 @@ def tile_moe_seb_none_kernel(
         got_scales = [got_plane, moved_plane]
         for first, last in ((0, LEAD), (LEAD, EXPERTS)):
             cols = slots(first, last)
-            nc.vector.tensor_copy(got_plane[:, cols], dy_plane[:].indirect(entries(list2, first, last)))
-            for q in range(QUADRANTS):
-                base = QUADRANT * q
-                nc.sync.dma_start(
-                    out=moved_plane[base : base + SCALE_ROWS, cols].bitcast(I32),
-                    in_=got_plane[base + SCALE_ROWS : base + 2 * SCALE_ROWS, cols].bitcast(I32),
-                )
-        nc.vector.tensor_copy(got_codes[0][:], dy_codes[0][:].indirect(list2[:]))
-        for first, last in ((0, LEAD), (LEAD, EXPERTS)):
-            nc.vector.tensor_copy(
-                got_codes[1][:, slots(first, last)], dy_codes[1][:].indirect(entries(list2, first, last))
+            nc.vector.tensor_copy(got_plane[:, cols], dy_plane.indirect(entries(list2, first, last)))
+            queue = nc.scalar if first == 0 else nc.sync
+            queue.dma_start(
+                out=moved_plane[0:LIVE_ROWS, cols].bitcast(I32),
+                in_=got_plane[SCALE_ROWS : SCALE_ROWS + LIVE_ROWS, cols].bitcast(I32),
             )
+        for first, last in ((0, LEAD), (LEAD, EXPERTS)):
+            for s in range(PASSES):
+                nc.vector.tensor_copy(
+                    got_codes[s][:, slots(first, last)], dy_codes[:, s * T :].indirect(entries(list2, first, last))
+                )
 
-        w2_rest = keep.tile(
-            [P, (EXPERTS - LEAD) * PASSES, FP4_BYTES * H], U8, name="w2_rest", tag="dy_plane", align_bytes=64
+        w2_codes, planes = [w2_lead], [lead_plane]
+
+        def load_group(first, last, group_codes, group_plane):
+            load_w2_codes(first, last, group_codes)
+            load_w2_scales(first, last, group_plane)
+            w2_codes.append(group_codes)
+            planes.append(group_plane)
+
+        codes_shape = [P, LATER * PASSES, FP4_BYTES * H]
+        load_group(
+            *GROUPS[1],
+            placed.tile(codes_shape, U8, name="w2_middle", offset=0, align_bytes=64),
+            placed.tile([P, PLANE_BYTES], U8, name="middle_plane", offset=CODES_BYTES, align_bytes=64),
         )
-        load_w2_codes(LEAD, EXPERTS, w2_rest)
-        rest_plane = early.tile([P, (EXPERTS - LEAD) * PASSES * H], U8, name="rest_plane", offset=0, align_bytes=64)
-        load_w2_scales(LEAD, EXPERTS, rest_plane)
-        gate2_rest = keep.tile([P, T - LEAD_SLOTS], F32, name="gate2_rest", tag="w2_lead", align_bytes=64)
-        nc.sync.dma_start(out=gate2_rest[:], in_=gate2[:, LEAD_SLOTS:T])
 
-        dc = [keep.tile([P, WIDE_SCATTER], F32, name=f"dc{t}") for t in range(DC_TILES)]
+        dc = [keep.tile([P, T], F32, name=f"dc{t}") for t in range(DC_TILES)]
 
         def second_layer(t, first, last, w2_codes, plane, banks):
-            staged = keep.tile([P, (last - first) * SLOTS], F32, name="staged", tag=f"staged{first}_{t}")
+            staged = keep.tile([P, (last - first) * SLOTS], F32, name="staged", tag=f"staged{first}_{t}", align_bytes=64)
             half = (last - first) // len(banks)
             for number, low in zip(banks, range(first, last, half)):
                 dc_sums = bank(number, half * SLOTS)
@@ -179,75 +194,86 @@ def tile_moe_seb_none_kernel(
             return staged
 
         def scatter_dc(t, first, last, staged, gate):
-            nc.vector.tensor_tensor(dc[t][:].indirect(entries(list2, first, last)), staged[:], gate[:], MULT)
+            nc.vector.tensor_tensor(dc[t][:].indirect(entries(list2, first, last)), staged[:], gate, MULT)
 
         for t in range(DC_TILES):
-            lead_staged = second_layer(t, 0, LEAD, w2_lead, lead_plane, [t])
-            scatter_dc(t, 0, LEAD, lead_staged, gate2_lead)
-        for t, banks in enumerate(([4, 5], [6, 7], [0, 1])):
-            scatter_dc(t, LEAD, EXPERTS, second_layer(t, LEAD, EXPERTS, w2_rest, rest_plane, banks), gate2_rest)
-        last_staged = second_layer(DC_TILES - 1, LEAD, EXPERTS, w2_rest, rest_plane, [2, 3])
+            scatter_dc(t, 0, LEAD, second_layer(t, 0, LEAD, w2_lead, lead_plane, [t]), gate2_lead[:])
+        gate2_rest = keep.tile([P, T - LEAD_SLOTS], F32, name="gate2_rest", tag="w2_lead", align_bytes=64)
+        nc.sync.dma_start(out=gate2_rest[:], in_=gate2[:, LEAD_SLOTS:T])
+        load_group(
+            *GROUPS[2],
+            keep.tile(codes_shape, U8, name="w2_last", tag="staged0_0", align_bytes=64),
+            keep.tile([P, PLANE_BYTES], U8, name="last_plane", tag="dy_codes", align_bytes=64),
+        )
+        for group in (1, 2):
+            first, last = GROUPS[group]
+            for t in range(DC_TILES):
+                last_staged = second_layer(t, first, last, w2_codes[group], planes[group], [(4 * group + t) % BANKS])
+                scatter_dc(t, first, last, last_staged, gate2_rest[:, slots(first - LEAD, last - LEAD)])
 
-        gate1_rows = keep.tile([P, SLOTS], F32, name="gate1_rows", tag="staged0_0")
+        gate1_rows = keep.tile([P, SLOTS], F32, name="gate1_rows", tag="staged0_1", align_bytes=64)
         nc.sync.dma_start(out=gate1_rows[0:EXPERTS, :], in_=gate1[0].rearrange("(e u) -> e u", u=SLOTS))
         w1_codes = keep.tile([P, EXPERTS, FP4_BYTES * K], U8, name="w1_codes", tag="gate2_lead", align_bytes=64)
         nc.sync.dma_start(out=w1_codes[:].bitcast(I32), in_=w1t_words.bitcast(I32).rearrange("e s p w -> p (e s) w"))
         load_scale_rows(
             nc,
-            lead_plane[:].bitcast(I32).rearrange("p (m w) -> p m w", m=EXPERTS),
+            planes[1][:, 0 : EXPERTS * K].bitcast(I32).rearrange("p (m w) -> p m w", m=EXPERTS),
             w1t_scales.bitcast(I32).rearrange("e s b w -> b (e s) w"),
         )
-        turned_gate = bank(1, SLOTS)
+        turned_gate = bank(DC_TILES - 1, SLOTS)
         nc.tensor.transpose(turned_gate[:], gate1_rows[:], identity[:])
         gate1_cols = keep.tile([P, EXPERTS], F32, name="gate1_cols")
         nc.scalar.copy(gate1_cols[:], turned_gate[:, 0:EXPERTS])
-
-        scatter_dc(DC_TILES - 1, LEAD, EXPERTS, last_staged, gate2_rest)
-        handed_out = []
-
-        def next_bank(width):
-            handed_out.append(width)
-            return bank((len(handed_out) + 3) % BANKS, width)
 
         result = [keep.tile([P, T], F32, name=f"result{b}") for b in range(ROW_BLOCKS)]
 
         def pick(g, picked):
             for t in range(DC_TILES):
-                nc.vector.tensor_copy(picked[:, t, :], dc[t][:, 0:T].indirect(entries(list1, g * PAIR, (g + 1) * PAIR)))
+                nc.vector.tensor_copy(picked[t], dc[t][:].indirect(entries(list1, g * PAIR, (g + 1) * PAIR)))
 
         def quantise(g, picked):
-            turned_pairs = next_bank(PAIR * 2 * SLOTS)
-            for x in range(PAIR):
-                by_slot = next_bank(H)
-                for t in range(DC_TILES):
-                    nc.tensor.transpose(
-                        by_slot[:, t * P : (t + 1) * P], picked[:, t, x * SLOTS : (x + 1) * SLOTS], identity[:]
-                    )
-                rounded = keep.tile([P, H], BF16, name="rounded", tag=f"rounded{g}_{x}")
-                nc.scalar.activation(
-                    rounded[:].rearrange("j (u p d) -> j u p d", u=2, d=2),
-                    by_slot[:].rearrange("j (p u d) -> j u p d", u=2, d=2),
-                    COPY,
-                    scale=gate1_cols[:, g * PAIR + x : g * PAIR + x + 1],
-                )
-                value_pairs = rounded[:].bitcast(F32)
-                for u in range(2):
-                    at = (2 * x + u) * SLOTS
-                    nc.tensor.transpose(
-                        turned_pairs[:, at : at + SLOTS], value_pairs[:, u * P : (u + 1) * P], identity[:]
-                    )
             grouped = keep.tile([P, PACK * PAIR_SLOTS], BF16, name="grouped", tag=f"grouped{g}", align_bytes=64)
-            nc.scalar.copy(
-                grouped[:].bitcast(F32).rearrange("p (x j u) -> p x j u", x=PAIR, u=2),
-                turned_pairs[:].rearrange("p (x u j) -> p x j u", x=PAIR, u=2),
-            )
+            rounded_pair = []
+            for x in range(PAIR):
+                by_slot = bank(SLOT_BANKS[g][x], H)
+                rounded = keep.tile([P, H], BF16, name="rounded", tag=f"rounded{g}_{x}")
+                steps = ((0, 2), (2, DC_TILES)) if g == 0 else ((0, DC_TILES),)
+                for low, high in steps:
+                    for t in range(low, high):
+                        nc.tensor.transpose(
+                            by_slot[:, t * P : (t + 1) * P], picked[t][:, x * SLOTS : (x + 1) * SLOTS], identity[:]
+                        )
+                    nc.scalar.activation(
+                        rounded[:].rearrange("j (u p d) -> j u p d", u=2, d=2)[:, :, low * QUADRANT : high * QUADRANT, :],
+                        by_slot[:, low * P : high * P].rearrange("j (p u d) -> j u p d", u=2, d=2),
+                        COPY,
+                        scale=gate1_cols[:, g * PAIR + x : g * PAIR + x + 1],
+                    )
+                rounded_pair.append(rounded)
+            count = PAIR // len(WORD_BANKS[g])
+            for low, number in zip(range(0, PAIR, count), WORD_BANKS[g]):
+                turned_pairs = bank(number, count * 2 * SLOTS)
+                for x in range(count):
+                    value_pairs = rounded_pair[low + x][:].bitcast(F32)
+                    for u in range(2):
+                        nc.tensor.transpose(
+                            turned_pairs[:, slots(2 * x + u, 2 * x + u + 1)],
+                            value_pairs[:, u * P : (u + 1) * P],
+                            identity[:],
+                        )
+                nc.scalar.copy(
+                    grouped[:]
+                    .bitcast(F32)[:, slots(2 * low, 2 * (low + count))]
+                    .rearrange("p (x j u) -> p x j u", x=count, u=2),
+                    turned_pairs[:].rearrange("p (x u j) -> p x j u", x=count, u=2),
+                )
             da_codes = ring.tile([P, PAIR_SLOTS], U32, name="da_codes", align_bytes=64)
             da_scales = ring.tile([P, PAIR_SLOTS], U8, name="da_scales", align_bytes=64)
             nc.vector.quantize_mx(out=da_codes[:].bitcast(FP8X4), scales=da_scales[:], in_=grouped[:])
             return da_codes, da_scales
 
         def multiply_and_scatter(g, da_codes, da_scales):
-            out_sums = next_bank(ROW_BLOCKS * PAIR_SLOTS)
+            out_sums = bank(OUT_BANKS[g], ROW_BLOCKS * PAIR_SLOTS)
             for b in range(ROW_BLOCKS):
                 for x in range(PAIR):
                     at = b * PAIR_SLOTS + x * SLOTS
@@ -255,7 +281,7 @@ def tile_moe_seb_none_kernel(
                     nc.tensor.matmul_mx(
                         out=out_sums[:, at : at + SLOTS],
                         lhsT=w1_codes[:, g * PAIR + x, FP4_BYTES * P * b : FP4_BYTES * P * (b + 1)].bitcast(FP4X4),
-                        lhsT_scale=lead_plane[:, (g * PAIR + x) * K + P * b : (g * PAIR + x) * K + P * (b + 1)],
+                        lhsT_scale=planes[1][:, (g * PAIR + x) * K + P * b : (g * PAIR + x) * K + P * (b + 1)],
                         rhs=da_codes[:, cols].bitcast(FP8X4),
                         rhs_scale=da_scales[:, cols],
                         start=True,
@@ -270,18 +296,21 @@ def tile_moe_seb_none_kernel(
                     result[b][:].indirect(offsets), out_staged[:, b * PAIR_SLOTS : (b + 1) * PAIR_SLOTS]
                 )
 
-        picked_first = keep.tile([P, DC_TILES, PAIR_SLOTS], F32, name="picked_first")
+        picked_first = [
+            keep.tile([P, PAIR_SLOTS], F32, name="picked_first", tag=tag, align_bytes=64)[:]
+            for tag in ("got_codes0", "got_codes1", "staged0_1", "picked_first")
+        ]
         picked_middle = keep.tile(
-            [P, (PAIRS - 2) * DC_TILES, PAIR_SLOTS], F32, name="picked_middle", tag=f"staged{LEAD}_{DC_TILES - 1}"
+            [P, (PAIRS - 2) * DC_TILES, PAIR_SLOTS], F32, name="picked_middle", tag=f"staged{GROUPS[2][0]}_{DC_TILES - 1}", align_bytes=64
         )
         picked_pairs = [picked_first]
-        picked_pairs.extend([picked_middle[:, m * DC_TILES : (m + 1) * DC_TILES, :] for m in range(PAIRS - 2)])
+        picked_pairs.extend([[picked_middle[:, m * DC_TILES + t, :] for t in range(DC_TILES)] for m in range(PAIRS - 2)])
         for g in range(PAIRS - 1):
             pick(g, picked_pairs[g])
         da = [quantise(0, picked_first)]
         picked_last = keep.tile([P, DC_TILES, PAIR_SLOTS], F32, name="picked_last", tag="grouped0", align_bytes=64)
-        picked_pairs.append(picked_last)
-        pick(PAIRS - 1, picked_last)
+        picked_pairs.append([picked_last[:, t, :] for t in range(DC_TILES)])
+        pick(PAIRS - 1, picked_pairs[PAIRS - 1])
         for g in range(1, PAIRS):
             da.append(quantise(g, picked_pairs[g]))
             multiply_and_scatter(g - 1, *da[g - 1])

@@ -28,33 +28,43 @@ QUADRANTS = 4
 QUADRANT = P // QUADRANTS
 SCALE_ROWS = 4
 FP4_BYTES = 2
+BANKS = 8
+ALIGN = 64
 
 FLOPS = 2 * T * (PASSES * P * PACK * H + H * K)
 
 LEAD = 2
+LATER = (EXPERTS - LEAD) // 2
+GROUPS = ((0, LEAD), (LEAD, LEAD + LATER), (LEAD + LATER, EXPERTS))
+LEAD_AND_REST = ((0, LEAD), (LEAD, EXPERTS))
+LATER_CODE_BYTES = LATER * PASSES * H * FP4_BYTES
+
 PAIR = 2
-LEAD_SLOTS = LEAD * SLOTS
-BANK = 512
-WIDE_GATHER = 1376
-WIDE_SCATTER = 1536
-PASS_BYTES = T * PACK
-LIVE_ROWS = P - QUADRANT + SCALE_ROWS
-SLOT_BANKS = ((4, 5), (6, 7), (0, 1), (2, 4))
-WORD_BANKS = ((6, 7), (0, 1), (2, 4), (5, 6))
-OUT_BANKS = (7, 1, 4, 7)
-LATER = 3
-PLANE_BYTES = LATER * PASSES * H
-CODES_BYTES = FP4_BYTES * PLANE_BYTES
-BANKS = 8
-GROUPS = ((0, LEAD), (LEAD, 5), (5, EXPERTS))
 PAIRS = EXPERTS // PAIR
 PAIR_SLOTS = PAIR * SLOTS
 
+IDLE_ROWS = QUADRANT - PASSES * SCALE_ROWS
+LIVE_ROWS = P - QUADRANT + SCALE_ROWS
 
-def load_scale_rows(nc, plane, rows):
+
+def slots(first, last):
+    return slice(first * SLOTS, last * SLOTS)
+
+
+def entries(list_tile, first, last):
+    return list_tile[:, first * SLOTS // STRIPE : last * SLOTS // STRIPE]
+
+
+def pair_banks(step):
+    first = (DC_TILES + PAIR * step) % BANKS
+    return range(first, first + PAIR)
+
+
+def load_scale_rows(nc, plane, rows, matrices):
+    by_matrix = plane.bitcast(I32).rearrange("p (m w) -> p m w", m=matrices)
     by_place = rows.rearrange("(q r) m w -> r q m w", r=SCALE_ROWS)
     for r in range(SCALE_ROWS):
-        nc.sync.dma_start(out=plane[r:P:QUADRANT], in_=by_place[r])
+        nc.sync.dma_start(out=by_matrix[r:P:QUADRANT], in_=by_place[r])
 
 
 def tile_moe_seb_none_kernel(
@@ -63,57 +73,48 @@ def tile_moe_seb_none_kernel(
     nc = tc.nc
     with ExitStack() as ctx:
         keep = ctx.enter_context(tc.tile_pool(name="keep", bufs=1))
-        ring = ctx.enter_context(tc.tile_pool(name="ring", bufs=4))
         placed = ctx.enter_context(tc.tile_pool(name="placed", bufs=1))
         psum = ctx.enter_context(tc.psum_pool(name="psum", bufs=1))
 
         def bank(number, width):
             return psum.tile([P, width], F32, name="bank", tag=f"bank{number}")
 
-        def entries(list_tile, first, last):
-            return list_tile[:, first * SLOTS // STRIPE : last * SLOTS // STRIPE]
+        def load_w2_codes(first, last, codes):
+            nc.sync.dma_start(
+                out=codes[:].bitcast(I32), in_=w2t_words.bitcast(I32)[first:last].rearrange("f s p w -> p (f s) w")
+            )
 
-        def slots(first, last):
-            return slice(first * SLOTS, last * SLOTS)
+        def load_w2_scales(first, last, plane):
+            rows = w2t_scales.bitcast(I32)[first:last].rearrange("f s b w -> b (f s) w")
+            load_scale_rows(nc, plane[:], rows, (last - first) * PASSES)
 
         list2 = keep.tile([P, T // STRIPE], U16, name="list2")
         nc.sync.dma_start(list2[:], offs2)
 
-        def load_w2_codes(first, last, group_codes):
-            nc.sync.dma_start(
-                out=group_codes[:].bitcast(I32),
-                in_=w2t_words.bitcast(I32)[first:last].rearrange("f s p w -> p (f s) w"),
-            )
-
-        def load_w2_scales(first, last, plane):
-            load_scale_rows(
-                nc,
-                plane[:].bitcast(I32).rearrange("p (m w) -> p m w", m=(last - first) * PASSES),
-                w2t_scales.bitcast(I32)[first:last].rearrange("f s b w -> b (f s) w"),
-            )
-
-        zeroed = placed.tile([P, T + PLANE_BYTES], U8, name="zeroed", offset=CODES_BYTES - T, align_bytes=64)
-        dy_plane = zeroed[:, 0:T]
-        nc.gpsimd.memset(dy_plane.bitcast(I32), 0)
+        dy_bytes = placed.tile([P, T], U8, name="dy_bytes", offset=LATER_CODE_BYTES - T // 2, align_bytes=ALIGN)
+        for q in range(QUADRANTS):
+            nc.vector.memset(dy_bytes[:].bitcast(I32)[QUADRANT * q : QUADRANT * q + IDLE_ROWS], 0)
         by_quadrant = dy_scales.bitcast(I32).rearrange("s (q r) w -> q s r w", r=SCALE_ROWS)
         for q in range(QUADRANTS):
-            base = QUADRANT * q
             queue = nc.sync if q % 2 == 0 else nc.scalar
-            queue.dma_start(out=dy_plane.bitcast(I32)[base : base + SCALE_ROWS * PASSES], in_=by_quadrant[q])
+            queue.dma_start(
+                out=dy_bytes[:].bitcast(I32)[QUADRANT * q + IDLE_ROWS : QUADRANT * (q + 1)], in_=by_quadrant[q]
+            )
 
-        dy_codes = keep.tile([P, PASSES * T], U32, name="dy_codes", tag="dy_codes", align_bytes=64)
+        dy_codes = keep.tile([P, PASSES * T], U32, name="dy_codes", tag="dy_codes", align_bytes=ALIGN)
         for s in range(PASSES):
             nc.sync.dma_start(
                 out=dy_codes[:, s * T : (s + 1) * T].bitcast(I32),
                 in_=dy_words[s].rearrange("p t d -> p (t d)").bitcast(I32),
             )
-        lead_plane = keep.tile([P, LEAD * PASSES * H], U8, name="lead_plane", align_bytes=64)
-        nc.vector.memset(lead_plane[:].bitcast(I32), 0)
+        lead_plane = keep.tile([P, LEAD * PASSES * H], U8, name="lead_plane", align_bytes=ALIGN)
         load_w2_scales(0, LEAD, lead_plane)
-        w2_lead = keep.tile([P, LEAD * PASSES, FP4_BYTES * H], U8, name="w2_lead", tag="w2_lead", align_bytes=64)
-        load_w2_codes(0, LEAD, w2_lead)
-        gate2_lead = keep.tile([P, LEAD_SLOTS], F32, name="gate2_lead", tag="gate2_lead", align_bytes=64)
-        nc.sync.dma_start(out=gate2_lead[:], in_=gate2[:, 0:LEAD_SLOTS])
+        lead_codes = keep.tile(
+            [P, LEAD * PASSES, FP4_BYTES * H], U8, name="lead_codes", tag="lead_codes", align_bytes=ALIGN
+        )
+        load_w2_codes(0, LEAD, lead_codes)
+        gate2_lead = keep.tile([P, LEAD * SLOTS], F32, name="gate2_lead", tag="gate2_lead", align_bytes=ALIGN)
+        nc.sync.dma_start(out=gate2_lead[:], in_=gate2[:, slots(0, LEAD)])
 
         identity = keep.tile([P, P], F32, name="identity")
         ones = keep.tile([P, P], F32, name="ones")
@@ -128,98 +129,83 @@ def tile_moe_seb_none_kernel(
             channel_multiplier=1,
         )
 
-        moved_plane = keep.tile([P, T], U8, name="moved_plane", align_bytes=64)
-        nc.vector.memset(moved_plane[:].bitcast(I32), 0)
-
-        nc.vector.memset(zeroed[:, T:].bitcast(I32), 0)
-
         list1 = keep.tile([P, T // STRIPE], U16, name="list1")
         nc.sync.dma_start(list1[:], offs)
 
+        got_bytes = keep.tile([P, T], U8, name="got_bytes", align_bytes=ALIGN)
+        got_planes = keep.tile([P, PASSES * T], U8, name="got_planes", align_bytes=ALIGN)
+        got_scales = [got_planes[:, s * T : (s + 1) * T] for s in range(PASSES)]
         got_codes = [
-            keep.tile([P, T], U32, name=f"got_codes{s}", tag=f"got_codes{s}", align_bytes=64) for s in range(PASSES)
+            keep.tile([P, T], U32, name="got_codes", tag=f"got_codes{s}", align_bytes=ALIGN) for s in range(PASSES)
         ]
-        got_plane = keep.tile([P, T], U8, name="got_plane", align_bytes=64)
-        got_scales = [got_plane, moved_plane]
-        for first, last in ((0, LEAD), (LEAD, EXPERTS)):
-            cols = slots(first, last)
-            nc.vector.tensor_copy(got_plane[:, cols], dy_plane.indirect(entries(list2, first, last)))
-            queue = nc.scalar if first == 0 else nc.sync
-            queue.dma_start(
-                out=moved_plane[0:LIVE_ROWS, cols].bitcast(I32),
-                in_=got_plane[SCALE_ROWS : SCALE_ROWS + LIVE_ROWS, cols].bitcast(I32),
-            )
-        for first, last in ((0, LEAD), (LEAD, EXPERTS)):
+
+        def move_down(queue, first, last):
+            for s in range(PASSES):
+                down = IDLE_ROWS + s * SCALE_ROWS
+                queue.dma_start(
+                    out=got_scales[s][0:LIVE_ROWS, slots(first, last)].bitcast(I32),
+                    in_=got_bytes[down : down + LIVE_ROWS, slots(first, last)].bitcast(I32),
+                )
+
+        for first, last in LEAD_AND_REST:
+            nc.vector.tensor_copy(got_bytes[:, slots(first, last)], dy_bytes[:].indirect(entries(list2, first, last)))
+        move_down(nc.scalar, 0, LEAD)
+        later_codes_shape = [P, LATER * PASSES, FP4_BYTES * H]
+        later_plane_shape = [P, LATER * PASSES * H]
+        middle_codes = placed.tile(later_codes_shape, U8, name="middle_codes", offset=0, align_bytes=ALIGN)
+        load_w2_codes(*GROUPS[1], middle_codes)
+        move_down(nc.sync, LEAD, EXPERTS)
+        middle_plane = placed.tile(
+            later_plane_shape, U8, name="middle_plane", offset=LATER_CODE_BYTES, align_bytes=ALIGN
+        )
+        load_w2_scales(*GROUPS[1], middle_plane)
+
+        for first, last in LEAD_AND_REST:
             for s in range(PASSES):
                 nc.vector.tensor_copy(
                     got_codes[s][:, slots(first, last)], dy_codes[:, s * T :].indirect(entries(list2, first, last))
                 )
 
-        w2_codes, planes = [w2_lead], [lead_plane]
-
-        def load_group(first, last, group_codes, group_plane):
-            load_w2_codes(first, last, group_codes)
-            load_w2_scales(first, last, group_plane)
-            w2_codes.append(group_codes)
-            planes.append(group_plane)
-
-        codes_shape = [P, LATER * PASSES, FP4_BYTES * H]
-        load_group(
-            *GROUPS[1],
-            placed.tile(codes_shape, U8, name="w2_middle", offset=0, align_bytes=64),
-            placed.tile([P, PLANE_BYTES], U8, name="middle_plane", offset=CODES_BYTES, align_bytes=64),
-        )
-
         dc = [keep.tile([P, T], F32, name=f"dc{t}") for t in range(DC_TILES)]
 
-        def second_layer(t, first, last, w2_codes, plane, banks):
-            staged = keep.tile([P, (last - first) * SLOTS], F32, name="staged", tag=f"staged{first}_{t}", align_bytes=64)
-            half = (last - first) // len(banks)
-            for number, low in zip(banks, range(first, last, half)):
-                dc_sums = bank(number, half * SLOTS)
-                for f in range(low, low + half):
+        def second_layer(group, codes, plane, gate):
+            first, last = GROUPS[group]
+            for t in range(DC_TILES):
+                dc_sums = bank((DC_TILES * group + t) % BANKS, (last - first) * SLOTS)
+                for f in range(first, last):
                     for s in range(PASSES):
                         matrix = (f - first) * PASSES + s
-                        words_at = FP4_BYTES * P * t
                         nc.tensor.matmul_mx(
-                            out=dc_sums[:, slots(f - low, f - low + 1)],
-                            lhsT=w2_codes[:, matrix, words_at : words_at + FP4_BYTES * P].bitcast(FP4X4),
+                            out=dc_sums[:, slots(f - first, f - first + 1)],
+                            lhsT=codes[:, matrix, FP4_BYTES * P * t : FP4_BYTES * P * (t + 1)].bitcast(FP4X4),
                             lhsT_scale=plane[:, matrix * H + P * t : matrix * H + P * (t + 1)],
                             rhs=got_codes[s][:, slots(f, f + 1)].bitcast(FP8X4),
                             rhs_scale=got_scales[s][:, slots(f, f + 1)],
                             start=(s == 0),
                             stop=(s == PASSES - 1),
                         )
-                nc.scalar.copy(staged[:, slots(low - first, low - first + half)], dc_sums[:])
-            return staged
+                dc_staged = keep.tile(
+                    [P, (last - first) * SLOTS], F32, name="dc_staged", tag=f"staged{group}_{t}", align_bytes=ALIGN
+                )
+                nc.scalar.copy(dc_staged[:], dc_sums[:])
+                nc.vector.tensor_tensor(dc[t][:].indirect(entries(list2, first, last)), dc_staged[:], gate, MULT)
 
-        def scatter_dc(t, first, last, staged, gate):
-            nc.vector.tensor_tensor(dc[t][:].indirect(entries(list2, first, last)), staged[:], gate, MULT)
+        second_layer(0, lead_codes, lead_plane, gate2_lead[:])
+        gate2_rest = keep.tile([P, T - LEAD * SLOTS], F32, name="gate2_rest", tag="lead_codes", align_bytes=ALIGN)
+        nc.sync.dma_start(out=gate2_rest[:], in_=gate2[:, slots(LEAD, EXPERTS)])
+        last_codes = keep.tile(later_codes_shape, U8, name="last_codes", tag="staged0_0", align_bytes=ALIGN)
+        load_w2_codes(*GROUPS[2], last_codes)
+        last_plane = keep.tile(later_plane_shape, U8, name="last_plane", tag="dy_codes", align_bytes=ALIGN)
+        load_w2_scales(*GROUPS[2], last_plane)
+        second_layer(1, middle_codes, middle_plane, gate2_rest[:, slots(0, LATER)])
+        second_layer(2, last_codes, last_plane, gate2_rest[:, slots(LATER, 2 * LATER)])
 
-        for t in range(DC_TILES):
-            scatter_dc(t, 0, LEAD, second_layer(t, 0, LEAD, w2_lead, lead_plane, [t]), gate2_lead[:])
-        gate2_rest = keep.tile([P, T - LEAD_SLOTS], F32, name="gate2_rest", tag="w2_lead", align_bytes=64)
-        nc.sync.dma_start(out=gate2_rest[:], in_=gate2[:, LEAD_SLOTS:T])
-        load_group(
-            *GROUPS[2],
-            keep.tile(codes_shape, U8, name="w2_last", tag="staged0_0", align_bytes=64),
-            keep.tile([P, PLANE_BYTES], U8, name="last_plane", tag="dy_codes", align_bytes=64),
-        )
-        for group in (1, 2):
-            first, last = GROUPS[group]
-            for t in range(DC_TILES):
-                last_staged = second_layer(t, first, last, w2_codes[group], planes[group], [(4 * group + t) % BANKS])
-                scatter_dc(t, first, last, last_staged, gate2_rest[:, slots(first - LEAD, last - LEAD)])
-
-        gate1_rows = keep.tile([P, SLOTS], F32, name="gate1_rows", tag="staged0_1", align_bytes=64)
+        gate1_rows = keep.tile([P, SLOTS], F32, name="gate1_rows", tag="staged0_1", align_bytes=ALIGN)
         nc.sync.dma_start(out=gate1_rows[0:EXPERTS, :], in_=gate1[0].rearrange("(e u) -> e u", u=SLOTS))
-        w1_codes = keep.tile([P, EXPERTS, FP4_BYTES * K], U8, name="w1_codes", tag="gate2_lead", align_bytes=64)
+        w1_codes = keep.tile([P, EXPERTS, FP4_BYTES * K], U8, name="w1_codes", tag="gate2_lead", align_bytes=ALIGN)
         nc.sync.dma_start(out=w1_codes[:].bitcast(I32), in_=w1t_words.bitcast(I32).rearrange("e s p w -> p (e s) w"))
-        load_scale_rows(
-            nc,
-            planes[1][:, 0 : EXPERTS * K].bitcast(I32).rearrange("p (m w) -> p m w", m=EXPERTS),
-            w1t_scales.bitcast(I32).rearrange("e s b w -> b (e s) w"),
-        )
+        w1_plane = middle_plane[:, 0 : EXPERTS * K]
+        load_scale_rows(nc, w1_plane, w1t_scales.bitcast(I32).rearrange("e s b w -> b (e s) w"), EXPERTS)
         turned_gate = bank(DC_TILES - 1, SLOTS)
         nc.tensor.transpose(turned_gate[:], gate1_rows[:], identity[:])
         gate1_cols = keep.tile([P, EXPERTS], F32, name="gate1_cols")
@@ -232,84 +218,71 @@ def tile_moe_seb_none_kernel(
                 nc.vector.tensor_copy(picked[t], dc[t][:].indirect(entries(list1, g * PAIR, (g + 1) * PAIR)))
 
         def quantise(g, picked):
-            grouped = keep.tile([P, PACK * PAIR_SLOTS], BF16, name="grouped", tag=f"grouped{g}", align_bytes=64)
-            rounded_pair = []
-            for x in range(PAIR):
-                by_slot = bank(SLOT_BANKS[g][x], H)
-                rounded = keep.tile([P, H], BF16, name="rounded", tag=f"rounded{g}_{x}")
-                steps = ((0, 2), (2, DC_TILES)) if g == 0 else ((0, DC_TILES),)
-                for low, high in steps:
+            tile_runs = ((0, DC_TILES // 2), (DC_TILES // 2, DC_TILES)) if g == 0 else ((0, DC_TILES),)
+            rounded = []
+            for x, number in enumerate(pair_banks(g)):
+                by_slot = bank(number, H)
+                rounded.append(keep.tile([P, H], BF16, name="rounded", tag=f"rounded{g}_{x}"))
+                for low, high in tile_runs:
                     for t in range(low, high):
-                        nc.tensor.transpose(
-                            by_slot[:, t * P : (t + 1) * P], picked[t][:, x * SLOTS : (x + 1) * SLOTS], identity[:]
-                        )
+                        nc.tensor.transpose(by_slot[:, t * P : (t + 1) * P], picked[t][:, slots(x, x + 1)], identity[:])
+                    by_word = rounded[x][:].rearrange("j (u p d) -> j u p d", u=2, d=2)
                     nc.scalar.activation(
-                        rounded[:].rearrange("j (u p d) -> j u p d", u=2, d=2)[:, :, low * QUADRANT : high * QUADRANT, :],
+                        by_word[:, :, low * P // PACK : high * P // PACK, :],
                         by_slot[:, low * P : high * P].rearrange("j (p u d) -> j u p d", u=2, d=2),
                         COPY,
                         scale=gate1_cols[:, g * PAIR + x : g * PAIR + x + 1],
                     )
-                rounded_pair.append(rounded)
-            count = PAIR // len(WORD_BANKS[g])
-            for low, number in zip(range(0, PAIR, count), WORD_BANKS[g]):
-                turned_pairs = bank(number, count * 2 * SLOTS)
-                for x in range(count):
-                    value_pairs = rounded_pair[low + x][:].bitcast(F32)
-                    for u in range(2):
-                        nc.tensor.transpose(
-                            turned_pairs[:, slots(2 * x + u, 2 * x + u + 1)],
-                            value_pairs[:, u * P : (u + 1) * P],
-                            identity[:],
-                        )
+            grouped = keep.tile([P, PACK * PAIR_SLOTS], BF16, name=f"grouped{g}", align_bytes=ALIGN)
+            for x, number in enumerate(pair_banks(g + 1)):
+                turned_words = bank(number, 2 * SLOTS)
+                for u in range(2):
+                    nc.tensor.transpose(
+                        turned_words[:, slots(u, u + 1)], rounded[x][:].bitcast(F32)[:, u * P : (u + 1) * P], identity[:]
+                    )
                 nc.scalar.copy(
-                    grouped[:]
-                    .bitcast(F32)[:, slots(2 * low, 2 * (low + count))]
-                    .rearrange("p (x j u) -> p x j u", x=count, u=2),
-                    turned_pairs[:].rearrange("p (x u j) -> p x j u", x=count, u=2),
+                    grouped[:].bitcast(F32)[:, slots(2 * x, 2 * x + 2)].rearrange("p (j u) -> p j u", u=2),
+                    turned_words[:].rearrange("p (u j) -> p j u", u=2),
                 )
-            da_codes = ring.tile([P, PAIR_SLOTS], U32, name="da_codes", align_bytes=64)
-            da_scales = ring.tile([P, PAIR_SLOTS], U8, name="da_scales", align_bytes=64)
+            da_codes = keep.tile([P, PAIR_SLOTS], U32, name=f"da_codes{g}", align_bytes=ALIGN)
+            da_scales = keep.tile([P, PAIR_SLOTS], U8, name=f"da_scales{g}", align_bytes=ALIGN)
             nc.vector.quantize_mx(out=da_codes[:].bitcast(FP8X4), scales=da_scales[:], in_=grouped[:])
             return da_codes, da_scales
 
         def multiply_and_scatter(g, da_codes, da_scales):
-            out_sums = bank(OUT_BANKS[g], ROW_BLOCKS * PAIR_SLOTS)
+            out_sums = bank(pair_banks(g + 1)[PAIR - 1], ROW_BLOCKS * PAIR_SLOTS)
             for b in range(ROW_BLOCKS):
                 for x in range(PAIR):
-                    at = b * PAIR_SLOTS + x * SLOTS
-                    cols = slice(x * SLOTS, (x + 1) * SLOTS)
+                    e = g * PAIR + x
                     nc.tensor.matmul_mx(
-                        out=out_sums[:, at : at + SLOTS],
-                        lhsT=w1_codes[:, g * PAIR + x, FP4_BYTES * P * b : FP4_BYTES * P * (b + 1)].bitcast(FP4X4),
-                        lhsT_scale=planes[1][:, (g * PAIR + x) * K + P * b : (g * PAIR + x) * K + P * (b + 1)],
-                        rhs=da_codes[:, cols].bitcast(FP8X4),
-                        rhs_scale=da_scales[:, cols],
+                        out=out_sums[:, slots(b * PAIR + x, b * PAIR + x + 1)],
+                        lhsT=w1_codes[:, e, FP4_BYTES * P * b : FP4_BYTES * P * (b + 1)].bitcast(FP4X4),
+                        lhsT_scale=w1_plane[:, e * K + P * b : e * K + P * (b + 1)],
+                        rhs=da_codes[:, slots(x, x + 1)].bitcast(FP8X4),
+                        rhs_scale=da_scales[:, slots(x, x + 1)],
                         start=True,
                         stop=True,
                     )
             tag = f"rounded{g + 1}_{PAIR - 1}" if g + 1 < PAIRS else "last_sums"
-            out_staged = keep.tile([P, ROW_BLOCKS * PAIR_SLOTS], F32, name="staged_out", tag=tag)
+            out_staged = keep.tile([P, ROW_BLOCKS * PAIR_SLOTS], F32, name="out_staged", tag=tag)
             nc.scalar.copy(out_staged[:], out_sums[:])
             offsets = entries(list1, g * PAIR, (g + 1) * PAIR)
             for b in range(ROW_BLOCKS):
-                nc.vector.tensor_copy(
-                    result[b][:].indirect(offsets), out_staged[:, b * PAIR_SLOTS : (b + 1) * PAIR_SLOTS]
-                )
+                nc.vector.tensor_copy(result[b][:].indirect(offsets), out_staged[:, slots(b * PAIR, (b + 1) * PAIR)])
 
-        picked_first = [
-            keep.tile([P, PAIR_SLOTS], F32, name="picked_first", tag=tag, align_bytes=64)[:]
-            for tag in ("got_codes0", "got_codes1", "staged0_1", "picked_first")
+        picked_pairs = [
+            [
+                keep.tile([P, PAIR_SLOTS], F32, name="picked_first", tag=tag, align_bytes=ALIGN)[:]
+                for tag in ("got_codes0", "got_codes1", "staged0_1", "picked_first")
+            ]
         ]
-        picked_middle = keep.tile(
-            [P, (PAIRS - 2) * DC_TILES, PAIR_SLOTS], F32, name="picked_middle", tag=f"staged{GROUPS[2][0]}_{DC_TILES - 1}", align_bytes=64
-        )
-        picked_pairs = [picked_first]
-        picked_pairs.extend([[picked_middle[:, m * DC_TILES + t, :] for t in range(DC_TILES)] for m in range(PAIRS - 2)])
+        last_source = f"staged{len(GROUPS) - 1}_{DC_TILES - 1}"
+        for tag in (last_source, "lead_codes", last_source):
+            picked = keep.tile([P, DC_TILES * PAIR_SLOTS], F32, name="picked", tag=tag, align_bytes=ALIGN)
+            picked_pairs.append([picked[:, slots(t * PAIR, (t + 1) * PAIR)] for t in range(DC_TILES)])
         for g in range(PAIRS - 1):
             pick(g, picked_pairs[g])
-        da = [quantise(0, picked_first)]
-        picked_last = keep.tile([P, DC_TILES, PAIR_SLOTS], F32, name="picked_last", tag="grouped0", align_bytes=64)
-        picked_pairs.append([picked_last[:, t, :] for t in range(DC_TILES)])
+        da = [quantise(0, picked_pairs[0])]
         pick(PAIRS - 1, picked_pairs[PAIRS - 1])
         for g in range(1, PAIRS):
             da.append(quantise(g, picked_pairs[g]))

@@ -43,8 +43,8 @@ PAIR = 2
 PAIRS = EXPERTS // PAIR
 PAIR_SLOTS = PAIR * SLOTS
 
-IDLE_ROWS = QUADRANT - PASSES * SCALE_ROWS
-LIVE_ROWS = P - QUADRANT + SCALE_ROWS
+BLOCKS = QUADRANTS * SCALE_ROWS
+IDLE_ROWS = P - PASSES * BLOCKS
 
 
 def slots(first, last):
@@ -91,15 +91,11 @@ def tile_moe_seb_none_kernel(
         list2 = keep.tile([P, T // STRIPE], U16, name="list2")
         nc.sync.dma_start(list2[:], offs2)
 
-        dy_bytes = placed.tile([P, T], U8, name="dy_bytes", offset=LATER_CODE_BYTES - T // 2, align_bytes=ALIGN)
-        for q in range(QUADRANTS):
-            nc.vector.memset(dy_bytes[:].bitcast(I32)[QUADRANT * q : QUADRANT * q + IDLE_ROWS], 0)
-        by_quadrant = dy_scales.bitcast(I32).rearrange("s (q r) w -> q s r w", r=SCALE_ROWS)
-        for q in range(QUADRANTS):
-            queue = nc.sync if q % 2 == 0 else nc.scalar
-            queue.dma_start(
-                out=dy_bytes[:].bitcast(I32)[QUADRANT * q + IDLE_ROWS : QUADRANT * (q + 1)], in_=by_quadrant[q]
-            )
+        dy_bytes = placed.tile([P, 2 * T], U8, name="dy_bytes", offset=LATER_CODE_BYTES - ALIGN, align_bytes=ALIGN)
+        nc.vector.memset(dy_bytes[0:IDLE_ROWS, 0:T].bitcast(I32), 0)
+        nc.scalar.dma_start(
+            out=dy_bytes[IDLE_ROWS:P, 0:T].bitcast(I32), in_=dy_scales.bitcast(I32).rearrange("s b w -> (s b) w")
+        )
 
         dy_codes = keep.tile([P, PASSES * T], U32, name="dy_codes", tag="dy_codes", align_bytes=ALIGN)
         for s in range(PASSES):
@@ -113,8 +109,6 @@ def tile_moe_seb_none_kernel(
             [P, LEAD * PASSES, FP4_BYTES * H], U8, name="lead_codes", tag="lead_codes", align_bytes=ALIGN
         )
         load_w2_codes(0, LEAD, lead_codes)
-        gate2_lead = keep.tile([P, LEAD * SLOTS], F32, name="gate2_lead", tag="gate2_lead", align_bytes=ALIGN)
-        nc.sync.dma_start(out=gate2_lead[:], in_=gate2[:, slots(0, LEAD)])
 
         identity = keep.tile([P, P], F32, name="identity")
         ones = keep.tile([P, P], F32, name="ones")
@@ -139,24 +133,22 @@ def tile_moe_seb_none_kernel(
             keep.tile([P, T], U32, name="got_codes", tag=f"got_codes{s}", align_bytes=ALIGN) for s in range(PASSES)
         ]
 
-        def move_down(queue, first, last):
-            for s in range(PASSES):
-                down = IDLE_ROWS + s * SCALE_ROWS
-                queue.dma_start(
-                    out=got_scales[s][0:LIVE_ROWS, slots(first, last)].bitcast(I32),
-                    in_=got_bytes[down : down + LIVE_ROWS, slots(first, last)].bitcast(I32),
+        nc.vector.tensor_copy(got_bytes[:], dy_bytes[:].indirect(list2[:]))
+        for s in range(PASSES):
+            for q in range(QUADRANTS):
+                source = IDLE_ROWS + s * BLOCKS + q * SCALE_ROWS
+                nc.sync.dma_start(
+                    out=got_scales[s][q * QUADRANT : q * QUADRANT + SCALE_ROWS].bitcast(I32),
+                    in_=got_bytes[source : source + SCALE_ROWS].bitcast(I32),
                 )
-
-        for first, last in LEAD_AND_REST:
-            nc.vector.tensor_copy(got_bytes[:, slots(first, last)], dy_bytes[:].indirect(entries(list2, first, last)))
-        move_down(nc.scalar, 0, LEAD)
+        gate2_lead = placed.tile([P, LEAD * SLOTS], F32, name="gate2_lead", offset=LATER_CODE_BYTES, align_bytes=ALIGN)
+        nc.sync.dma_start(out=gate2_lead[:], in_=gate2[:, slots(0, LEAD)])
         later_codes_shape = [P, LATER * PASSES, FP4_BYTES * H]
         later_plane_shape = [P, LATER * PASSES * H]
         middle_codes = placed.tile(later_codes_shape, U8, name="middle_codes", offset=0, align_bytes=ALIGN)
         load_w2_codes(*GROUPS[1], middle_codes)
-        move_down(nc.sync, LEAD, EXPERTS)
         middle_plane = placed.tile(
-            later_plane_shape, U8, name="middle_plane", offset=LATER_CODE_BYTES, align_bytes=ALIGN
+            later_plane_shape, U8, name="middle_plane", offset=LATER_CODE_BYTES + T, align_bytes=ALIGN
         )
         load_w2_scales(*GROUPS[1], middle_plane)
 
@@ -202,7 +194,7 @@ def tile_moe_seb_none_kernel(
 
         gate1_rows = keep.tile([P, SLOTS], F32, name="gate1_rows", tag="staged0_1", align_bytes=ALIGN)
         nc.sync.dma_start(out=gate1_rows[0:EXPERTS, :], in_=gate1[0].rearrange("(e u) -> e u", u=SLOTS))
-        w1_codes = keep.tile([P, EXPERTS, FP4_BYTES * K], U8, name="w1_codes", tag="gate2_lead", align_bytes=ALIGN)
+        w1_codes = keep.tile([P, EXPERTS, FP4_BYTES * K], U8, name="w1_codes", tag="staged0_3", align_bytes=ALIGN)
         nc.sync.dma_start(out=w1_codes[:].bitcast(I32), in_=w1t_words.bitcast(I32).rearrange("e s p w -> p (e s) w"))
         w1_plane = middle_plane[:, 0 : EXPERTS * K]
         load_scale_rows(nc, w1_plane, w1t_scales.bitcast(I32).rearrange("e s b w -> b (e s) w"), EXPERTS)

@@ -33,15 +33,10 @@ ALIGN = 64
 
 FLOPS = 2 * T * (PASSES * P * PACK * H + H * K)
 
-LEAD = 2
-LATER = (EXPERTS - LEAD) // 2
-GROUPS = ((0, LEAD), (LEAD, LEAD + LATER), (LEAD + LATER, EXPERTS))
-LEAD_AND_REST = ((0, LEAD), (LEAD, EXPERTS))
-LATER_CODE_BYTES = LATER * PASSES * H * FP4_BYTES
-
 PAIR = 2
 PAIRS = EXPERTS // PAIR
 PAIR_SLOTS = PAIR * SLOTS
+PAIR_CODE_BYTES = PAIR * PASSES * H * FP4_BYTES
 
 BLOCKS = QUADRANTS * SCALE_ROWS
 IDLE_ROWS = P - PASSES * BLOCKS
@@ -53,11 +48,6 @@ def slots(first, last):
 
 def entries(list_tile, first, last):
     return list_tile[:, first * SLOTS // STRIPE : last * SLOTS // STRIPE]
-
-
-def pair_banks(step):
-    first = (DC_TILES + PAIR * step) % BANKS
-    return range(first, first + PAIR)
 
 
 def load_scale_rows(nc, plane, rows, matrices):
@@ -91,11 +81,13 @@ def tile_moe_seb_none_kernel(
         list2 = keep.tile([P, T // STRIPE], U16, name="list2")
         nc.sync.dma_start(list2[:], offs2)
 
-        dy_bytes = placed.tile([P, 2 * T], U8, name="dy_bytes", offset=LATER_CODE_BYTES - ALIGN, align_bytes=ALIGN)
+        dy_bytes = placed.tile([P, 2 * T], U8, name="dy_bytes", offset=PAIR_CODE_BYTES - ALIGN, align_bytes=ALIGN)
         nc.vector.memset(dy_bytes[0:IDLE_ROWS, 0:T].bitcast(I32), 0)
         nc.scalar.dma_start(
-            out=dy_bytes[IDLE_ROWS:P, 0:T].bitcast(I32), in_=dy_scales.bitcast(I32).rearrange("s b w -> (s b) w")
+            out=dy_bytes[IDLE_ROWS:P, 0:T].bitcast(I32), in_=dy_scales.bitcast(I32).rearrange("s b w -> b s w")
         )
+        gate2_rows = keep.tile([P, SLOTS], F32, name="gate2_rows")
+        nc.sync.dma_start(out=gate2_rows[0:EXPERTS, :], in_=gate2[0].rearrange("(e u) -> e u", u=SLOTS))
 
         dy_codes = keep.tile([P, PASSES * T], U32, name="dy_codes", tag="dy_codes", align_bytes=ALIGN)
         for s in range(PASSES):
@@ -103,12 +95,12 @@ def tile_moe_seb_none_kernel(
                 out=dy_codes[:, s * T : (s + 1) * T].bitcast(I32),
                 in_=dy_words[s].rearrange("p t d -> p (t d)").bitcast(I32),
             )
-        lead_plane = keep.tile([P, LEAD * PASSES * H], U8, name="lead_plane", align_bytes=ALIGN)
-        load_w2_scales(0, LEAD, lead_plane)
+        lead_plane = keep.tile([P, PAIR * PASSES * H], U8, name="lead_plane", tag="lead_plane", align_bytes=ALIGN)
+        load_w2_scales(0, PAIR, lead_plane)
         lead_codes = keep.tile(
-            [P, LEAD * PASSES, FP4_BYTES * H], U8, name="lead_codes", tag="lead_codes", align_bytes=ALIGN
+            [P, PAIR * PASSES, FP4_BYTES * H], U8, name="lead_codes", tag="lead_codes", align_bytes=ALIGN
         )
-        load_w2_codes(0, LEAD, lead_codes)
+        load_w2_codes(0, PAIR, lead_codes)
 
         identity = keep.tile([P, P], F32, name="identity")
         ones = keep.tile([P, P], F32, name="ones")
@@ -126,113 +118,163 @@ def tile_moe_seb_none_kernel(
         list1 = keep.tile([P, T // STRIPE], U16, name="list1")
         nc.sync.dma_start(list1[:], offs)
 
+        def gate_columns(rows, number, name):
+            turned_gate = bank(number, SLOTS)
+            nc.tensor.transpose(turned_gate[:], rows[:], identity[:])
+            cols = keep.tile([P, EXPERTS], F32, name=name)
+            nc.scalar.copy(cols[:], turned_gate[:, 0:EXPERTS])
+            return cols
+
+        gate2_cols = gate_columns(gate2_rows, 6, "gate2_cols")
+        gate2_all = keep.tile([P, T], F32, name="gate2_all")
+        for half in range(2):
+            spread = bank(4 + half, T // 2)
+            for x in range(EXPERTS // 2):
+                f = half * EXPERTS // 2 + x
+                nc.tensor.transpose(
+                    spread[:, slots(x, x + 1)], gate2_cols[:, f : f + 1].to_broadcast([P, P]), identity[:]
+                )
+            nc.scalar.copy(gate2_all[:, half * T // 2 : (half + 1) * T // 2], spread[:])
+
         got_bytes = keep.tile([P, T], U8, name="got_bytes", align_bytes=ALIGN)
         got_planes = keep.tile([P, PASSES * T], U8, name="got_planes", align_bytes=ALIGN)
-        got_scales = [got_planes[:, s * T : (s + 1) * T] for s in range(PASSES)]
-        got_codes = [
-            keep.tile([P, T], U32, name="got_codes", tag=f"got_codes{s}", align_bytes=ALIGN) for s in range(PASSES)
-        ]
-
         nc.vector.tensor_copy(got_bytes[:], dy_bytes[:].indirect(list2[:]))
-        for s in range(PASSES):
-            for q in range(QUADRANTS):
-                source = IDLE_ROWS + s * BLOCKS + q * SCALE_ROWS
-                nc.sync.dma_start(
-                    out=got_scales[s][q * QUADRANT : q * QUADRANT + SCALE_ROWS].bitcast(I32),
-                    in_=got_bytes[source : source + SCALE_ROWS].bitcast(I32),
-                )
-        gate2_lead = placed.tile([P, LEAD * SLOTS], F32, name="gate2_lead", offset=LATER_CODE_BYTES, align_bytes=ALIGN)
-        nc.sync.dma_start(out=gate2_lead[:], in_=gate2[:, slots(0, LEAD)])
-        later_codes_shape = [P, LATER * PASSES, FP4_BYTES * H]
-        later_plane_shape = [P, LATER * PASSES * H]
-        middle_codes = placed.tile(later_codes_shape, U8, name="middle_codes", offset=0, align_bytes=ALIGN)
-        load_w2_codes(*GROUPS[1], middle_codes)
+        for q in range(QUADRANTS):
+            source = IDLE_ROWS + q * PASSES * SCALE_ROWS
+            nc.sync.dma_start(
+                out=got_planes[q * QUADRANT : q * QUADRANT + SCALE_ROWS].bitcast(I32).rearrange("r (s w) -> r s w", s=PASSES),
+                in_=got_bytes[source : source + PASSES * SCALE_ROWS].bitcast(I32),
+            )
+        middle_codes = placed.tile([P, PAIR * PASSES, FP4_BYTES * H], U8, name="middle_codes", offset=0, align_bytes=ALIGN)
+        load_w2_codes(PAIR, 2 * PAIR, middle_codes)
         middle_plane = placed.tile(
-            later_plane_shape, U8, name="middle_plane", offset=LATER_CODE_BYTES + T, align_bytes=ALIGN
+            [P, PAIR * PASSES * H], U8, name="middle_plane", offset=PAIR_CODE_BYTES + T, align_bytes=ALIGN
         )
-        load_w2_scales(*GROUPS[1], middle_plane)
+        load_w2_scales(PAIR, 2 * PAIR, middle_plane)
 
-        for first, last in LEAD_AND_REST:
-            for s in range(PASSES):
-                nc.vector.tensor_copy(
-                    got_codes[s][:, slots(first, last)], dy_codes[:, s * T :].indirect(entries(list2, first, last))
-                )
+        def gather_words(first, last, s, tag):
+            words = keep.tile([P, (last - first) * SLOTS], U32, name="got_words", tag=tag, align_bytes=ALIGN)
+            nc.vector.tensor_copy(words[:], dy_codes[:, s * T :].indirect(entries(list2, first, last)))
+            return words
+
+        lead_words = [gather_words(0, PAIR, s, f"lead_words{s}") for s in range(PASSES)]
+        middle_words = [gather_words(PAIR, 2 * PAIR, s, f"middle_words{s}") for s in range(PASSES)]
+        late_words = [gather_words(2 * PAIR, EXPERTS, 0, "late_words0")]
 
         dc = [keep.tile([P, T], F32, name=f"dc{t}") for t in range(DC_TILES)]
+        TILE_SETS = ((1, 3), (0, 2))
 
-        def second_layer(group, codes, plane, gate):
-            first, last = GROUPS[group]
-            for t in range(DC_TILES):
-                dc_sums = bank((DC_TILES * group + t) % BANKS, (last - first) * SLOTS)
-                for f in range(first, last):
-                    for s in range(PASSES):
-                        matrix = (f - first) * PASSES + s
-                        nc.tensor.matmul_mx(
-                            out=dc_sums[:, slots(f - first, f - first + 1)],
-                            lhsT=codes[:, matrix, FP4_BYTES * P * t : FP4_BYTES * P * (t + 1)].bitcast(FP4X4),
-                            lhsT_scale=plane[:, matrix * H + P * t : matrix * H + P * (t + 1)],
-                            rhs=got_codes[s][:, slots(f, f + 1)].bitcast(FP8X4),
-                            rhs_scale=got_scales[s][:, slots(f, f + 1)],
-                            start=(s == 0),
-                            stop=(s == PASSES - 1),
-                        )
-                dc_staged = keep.tile(
-                    [P, (last - first) * SLOTS], F32, name="dc_staged", tag=f"staged{group}_{t}", align_bytes=ALIGN
+        def products(g, codes, plane, words, base):
+            sums = []
+            for side, tiles in enumerate(TILE_SETS):
+                dc_sums = bank(2 * g + side, 2 * PAIR_SLOTS)
+                sums.append(dc_sums)
+                for place, t in enumerate(tiles):
+                    for x in range(PAIR):
+                        f = g * PAIR + x
+                        for s in range(PASSES):
+                            matrix = (f - base) * PASSES + s
+                            nc.tensor.matmul_mx(
+                                out=dc_sums[:, slots(place * PAIR + x, place * PAIR + x + 1)],
+                                lhsT=codes[:, matrix, FP4_BYTES * P * t : FP4_BYTES * P * (t + 1)].bitcast(FP4X4),
+                                lhsT_scale=plane[:, matrix * H + P * t : matrix * H + P * (t + 1)],
+                                rhs=words[s][:, slots(f - base, f - base + 1)].bitcast(FP8X4),
+                                rhs_scale=got_planes[:, s * T + f * SLOTS : s * T + (f + 1) * SLOTS],
+                                start=(s == 0),
+                                stop=(s == PASSES - 1),
+                            )
+            return sums
+
+        def stage(g, side, dc_sums, gated):
+            staged = keep.tile([P, 2 * PAIR_SLOTS], F32, name="dc_staged", tag=f"staged{g}_{side}", align_bytes=ALIGN)
+            if gated:
+                gate = gate2_all[:, slots(g * PAIR, (g + 1) * PAIR)].unsqueeze(1).to_broadcast([P, 2, PAIR_SLOTS])
+                nc.vector.tensor_tensor(
+                    staged[:].rearrange("p (a j) -> p a j", a=2), dc_sums[:].rearrange("p (a j) -> p a j", a=2), gate, MULT
                 )
-                nc.scalar.copy(dc_staged[:], dc_sums[:])
-                nc.vector.tensor_tensor(dc[t][:].indirect(entries(list2, first, last)), dc_staged[:], gate, MULT)
+            else:
+                nc.scalar.copy(staged[:], dc_sums[:])
+            return staged
 
-        second_layer(0, lead_codes, lead_plane, gate2_lead[:])
-        gate2_rest = keep.tile([P, T - LEAD * SLOTS], F32, name="gate2_rest", tag="lead_codes", align_bytes=ALIGN)
-        nc.sync.dma_start(out=gate2_rest[:], in_=gate2[:, slots(LEAD, EXPERTS)])
-        last_codes = keep.tile(later_codes_shape, U8, name="last_codes", tag="staged0_0", align_bytes=ALIGN)
-        load_w2_codes(*GROUPS[2], last_codes)
-        last_plane = keep.tile(later_plane_shape, U8, name="last_plane", tag="dy_codes", align_bytes=ALIGN)
-        load_w2_scales(*GROUPS[2], last_plane)
-        second_layer(1, middle_codes, middle_plane, gate2_rest[:, slots(0, LATER)])
-        second_layer(2, last_codes, last_plane, gate2_rest[:, slots(LATER, 2 * LATER)])
+        def scatter_dc(g, side, place, staged, how):
+            window = dc[TILE_SETS[side][place]][:].indirect(entries(list2, g * PAIR, (g + 1) * PAIR))
+            values = staged[:, slots(place * PAIR, (place + 1) * PAIR)]
+            if how == "scalar":
+                nc.scalar.activation(window, values, COPY)
+            elif how == "vector":
+                nc.vector.tensor_copy(window, values)
+            else:
+                nc.vector.tensor_tensor(window, values, gate2_all[:, slots(g * PAIR, (g + 1) * PAIR)], MULT)
+
+        sums = products(0, lead_codes, lead_plane, lead_words, 0)
+        staged = [stage(0, side, sums[side], True) for side in range(2)]
+        late_words.append(gather_words(2 * PAIR, EXPERTS, 1, "lead_words1"))
+        late_codes = keep.tile(
+            [P, 2 * PAIR * PASSES, FP4_BYTES * H], U8, name="late_codes", tag="lead_codes", align_bytes=ALIGN
+        )
+        load_w2_codes(2 * PAIR, EXPERTS, late_codes)
+        late_plane = keep.tile([P, 2 * PAIR * PASSES * H], U8, name="late_plane", tag="lead_plane", align_bytes=ALIGN)
+        load_w2_scales(2 * PAIR, EXPERTS, late_plane)
+        scatter_dc(0, 0, 0, staged[0], "scalar")
+        scatter_dc(0, 0, 1, staged[0], "scalar")
+        scatter_dc(0, 1, 0, staged[1], "vector")
+        scatter_dc(0, 1, 1, staged[1], "scalar")
+        for g in range(1, PAIRS):
+            if g == 1:
+                sums = products(g, middle_codes, middle_plane, middle_words, PAIR)
+            else:
+                sums = products(g, late_codes, late_plane, late_words, 2 * PAIR)
+            staged = [stage(g, 0, sums[0], True), stage(g, 1, sums[1], g == 1)]
+            for place in range(2):
+                scatter_dc(g, 0, place, staged[0], "scalar")
+                scatter_dc(g, 1, place, staged[1], "vector" if g == 1 else "gated")
 
         gate1_rows = keep.tile([P, SLOTS], F32, name="gate1_rows", tag="staged0_1", align_bytes=ALIGN)
         nc.sync.dma_start(out=gate1_rows[0:EXPERTS, :], in_=gate1[0].rearrange("(e u) -> e u", u=SLOTS))
-        w1_codes = keep.tile([P, EXPERTS, FP4_BYTES * K], U8, name="w1_codes", tag="staged0_3", align_bytes=ALIGN)
+        w1_codes = placed.tile([P, EXPERTS, FP4_BYTES * K], U8, name="w1_codes", offset=0, align_bytes=ALIGN)
         nc.sync.dma_start(out=w1_codes[:].bitcast(I32), in_=w1t_words.bitcast(I32).rearrange("e s p w -> p (e s) w"))
         w1_plane = middle_plane[:, 0 : EXPERTS * K]
         load_scale_rows(nc, w1_plane, w1t_scales.bitcast(I32).rearrange("e s b w -> b (e s) w"), EXPERTS)
-        turned_gate = bank(DC_TILES - 1, SLOTS)
-        nc.tensor.transpose(turned_gate[:], gate1_rows[:], identity[:])
-        gate1_cols = keep.tile([P, EXPERTS], F32, name="gate1_cols")
-        nc.scalar.copy(gate1_cols[:], turned_gate[:, 0:EXPERTS])
+        gate1_cols = gate_columns(gate1_rows, 0, "gate1_cols")
 
         result = [keep.tile([P, T], F32, name=f"result{b}") for b in range(ROW_BLOCKS)]
 
-        def pick(g, picked):
+        def pick(g):
+            picked = []
             for t in range(DC_TILES):
-                nc.vector.tensor_copy(picked[t], dc[t][:].indirect(entries(list1, g * PAIR, (g + 1) * PAIR)))
+                picked.append(keep.tile([P, PAIR_SLOTS], F32, name=f"picked{g}_{t}", align_bytes=ALIGN))
+                window = dc[t][:].indirect(entries(list1, g * PAIR, (g + 1) * PAIR))
+                if t in TILE_SETS[0]:
+                    nc.scalar.activation(picked[t][:], window, COPY)
+                else:
+                    nc.vector.tensor_copy(picked[t][:], window)
+            return picked
 
-        def quantise(g, picked):
-            tile_runs = ((0, DC_TILES // 2), (DC_TILES // 2, DC_TILES)) if g == 0 else ((0, DC_TILES),)
+        def round_pair(g, picked):
             rounded = []
-            for x, number in enumerate(pair_banks(g)):
-                by_slot = bank(number, H)
-                rounded.append(keep.tile([P, H], BF16, name="rounded", tag=f"rounded{g}_{x}"))
-                for low, high in tile_runs:
-                    for t in range(low, high):
-                        nc.tensor.transpose(by_slot[:, t * P : (t + 1) * P], picked[t][:, slots(x, x + 1)], identity[:])
-                    by_word = rounded[x][:].rearrange("j (u p d) -> j u p d", u=2, d=2)
-                    nc.scalar.activation(
-                        by_word[:, :, low * P // PACK : high * P // PACK, :],
-                        by_slot[:, low * P : high * P].rearrange("j (p u d) -> j u p d", u=2, d=2),
-                        COPY,
-                        scale=gate1_cols[:, g * PAIR + x : g * PAIR + x + 1],
-                    )
-            grouped = keep.tile([P, PACK * PAIR_SLOTS], BF16, name=f"grouped{g}", align_bytes=ALIGN)
-            for x, number in enumerate(pair_banks(g + 1)):
-                turned_words = bank(number, 2 * SLOTS)
+            for x in range(PAIR):
+                by_slot = bank((PAIR * g + x) % 4, H)
+                rounded.append(keep.tile([P, H], BF16, name="rounded", tag=f"rounded{g}_{x}", align_bytes=ALIGN))
+                for t in range(DC_TILES):
+                    nc.tensor.transpose(by_slot[:, t * P : (t + 1) * P], picked[t][:, slots(x, x + 1)], identity[:])
+                words = rounded[x][:].rearrange("j (u p d) -> j u p d", u=2, d=2)
+                turned = by_slot[:].rearrange("j (p u d) -> j u p d", u=2, d=2)
+                weight = gate1_cols[:, g * PAIR + x : g * PAIR + x + 1]
+                if x == 0:
+                    nc.scalar.activation(words, turned, COPY, scale=weight)
+                else:
+                    nc.vector.tensor_scalar(words, turned, weight, None, MULT)
+            return rounded
+
+        def quantise(g, rounded):
+            grouped = keep.tile([P, PACK * PAIR_SLOTS], BF16, name="grouped", tag=f"grouped{g}", align_bytes=ALIGN)
+            for x in range(PAIR):
+                turned_words = bank(4 + x, 2 * SLOTS)
                 for u in range(2):
                     nc.tensor.transpose(
                         turned_words[:, slots(u, u + 1)], rounded[x][:].bitcast(F32)[:, u * P : (u + 1) * P], identity[:]
                     )
-                nc.scalar.copy(
+                (nc.scalar.copy if x == 0 else nc.vector.tensor_copy)(
                     grouped[:].bitcast(F32)[:, slots(2 * x, 2 * x + 2)].rearrange("p (j u) -> p j u", u=2),
                     turned_words[:].rearrange("p (u j) -> p j u", u=2),
                 )
@@ -242,12 +284,13 @@ def tile_moe_seb_none_kernel(
             return da_codes, da_scales
 
         def multiply_and_scatter(g, da_codes, da_scales):
-            out_sums = bank(pair_banks(g + 1)[PAIR - 1], ROW_BLOCKS * PAIR_SLOTS)
+            offsets = entries(list1, g * PAIR, (g + 1) * PAIR)
             for b in range(ROW_BLOCKS):
+                out_sums = bank(6 + b, PAIR_SLOTS)
                 for x in range(PAIR):
                     e = g * PAIR + x
                     nc.tensor.matmul_mx(
-                        out=out_sums[:, slots(b * PAIR + x, b * PAIR + x + 1)],
+                        out=out_sums[:, slots(x, x + 1)],
                         lhsT=w1_codes[:, e, FP4_BYTES * P * b : FP4_BYTES * P * (b + 1)].bitcast(FP4X4),
                         lhsT_scale=w1_plane[:, e * K + P * b : e * K + P * (b + 1)],
                         rhs=da_codes[:, slots(x, x + 1)].bitcast(FP8X4),
@@ -255,29 +298,25 @@ def tile_moe_seb_none_kernel(
                         start=True,
                         stop=True,
                     )
-            tag = f"rounded{g + 1}_{PAIR - 1}" if g + 1 < PAIRS else "last_sums"
-            out_staged = keep.tile([P, ROW_BLOCKS * PAIR_SLOTS], F32, name="out_staged", tag=tag)
-            nc.scalar.copy(out_staged[:], out_sums[:])
-            offsets = entries(list1, g * PAIR, (g + 1) * PAIR)
-            for b in range(ROW_BLOCKS):
-                nc.vector.tensor_copy(result[b][:].indirect(offsets), out_staged[:, slots(b * PAIR, (b + 1) * PAIR)])
+                if g + 1 < PAIRS:
+                    tag = f"grouped{g + 1}" if b == 0 else f"rounded{g + 1}_1"
+                else:
+                    tag = f"last_sums{b}"
+                out_staged = keep.tile([P, PAIR_SLOTS], F32, name="out_staged", tag=tag, align_bytes=ALIGN)
+                if b == 0:
+                    nc.vector.tensor_copy(out_staged[:], out_sums[:])
+                    nc.vector.tensor_copy(result[b][:].indirect(offsets), out_staged[:])
+                else:
+                    nc.scalar.copy(out_staged[:], out_sums[:])
+                    nc.scalar.activation(result[b][:].indirect(offsets), out_staged[:], COPY)
 
-        picked_pairs = [
-            [
-                keep.tile([P, PAIR_SLOTS], F32, name="picked_first", tag=tag, align_bytes=ALIGN)[:]
-                for tag in ("got_codes0", "got_codes1", "staged0_1", "picked_first")
-            ]
-        ]
-        last_source = f"staged{len(GROUPS) - 1}_{DC_TILES - 1}"
-        for tag in (last_source, "lead_codes", last_source):
-            picked = keep.tile([P, DC_TILES * PAIR_SLOTS], F32, name="picked", tag=tag, align_bytes=ALIGN)
-            picked_pairs.append([picked[:, slots(t * PAIR, (t + 1) * PAIR)] for t in range(DC_TILES)])
-        for g in range(PAIRS - 1):
-            pick(g, picked_pairs[g])
-        da = [quantise(0, picked_pairs[0])]
-        pick(PAIRS - 1, picked_pairs[PAIRS - 1])
+        picked = [pick(g) for g in range(PAIRS)]
+        rounded = [round_pair(g, picked[g]) for g in range(2)]
+        da = [quantise(0, rounded[0])]
         for g in range(1, PAIRS):
-            da.append(quantise(g, picked_pairs[g]))
+            if g + 1 < PAIRS:
+                rounded.append(round_pair(g + 1, picked[g + 1]))
+            da.append(quantise(g, rounded[g]))
             multiply_and_scatter(g - 1, *da[g - 1])
         multiply_and_scatter(PAIRS - 1, *da[PAIRS - 1])
 

@@ -88,15 +88,14 @@ def tile_moe_seb_none_kernel(
         )
         gate2_rows = keep.tile([P, SLOTS], F32, name="gate2_rows")
         nc.sync.dma_start(out=gate2_rows[0:EXPERTS, :], in_=gate2[0].rearrange("(e u) -> e u", u=SLOTS))
-
+        early_plane = keep.tile([P, 2 * PAIR * PASSES * H], U8, name="early_plane", align_bytes=ALIGN)
+        load_w2_scales(0, 2 * PAIR, early_plane)
         dy_codes = keep.tile([P, PASSES * T], U32, name="dy_codes", tag="dy_codes", align_bytes=ALIGN)
         for s in range(PASSES):
             nc.sync.dma_start(
                 out=dy_codes[:, s * T : (s + 1) * T].bitcast(I32),
                 in_=dy_words[s].rearrange("p t d -> p (t d)").bitcast(I32),
             )
-        lead_plane = keep.tile([P, PAIR * PASSES * H], U8, name="lead_plane", tag="lead_plane", align_bytes=ALIGN)
-        load_w2_scales(0, PAIR, lead_plane)
         lead_codes = keep.tile(
             [P, PAIR * PASSES, FP4_BYTES * H], U8, name="lead_codes", tag="lead_codes", align_bytes=ALIGN
         )
@@ -117,6 +116,8 @@ def tile_moe_seb_none_kernel(
 
         list1 = keep.tile([P, T // STRIPE], U16, name="list1")
         nc.sync.dma_start(list1[:], offs)
+        gate1_rows = keep.tile([P, SLOTS], F32, name="gate1_rows")
+        nc.sync.dma_start(out=gate1_rows[0:EXPERTS, :], in_=gate1[0].rearrange("(e u) -> e u", u=SLOTS))
 
         def gate_columns(rows, number, name):
             turned_gate = bank(number, SLOTS)
@@ -126,7 +127,7 @@ def tile_moe_seb_none_kernel(
             return cols
 
         gate2_cols = gate_columns(gate2_rows, 6, "gate2_cols")
-        gate2_all = keep.tile([P, T], F32, name="gate2_all")
+        gate2_all = keep.tile([P, T], F32, name="gate2_all", tag="gate2_all", align_bytes=ALIGN)
         for half in range(2):
             spread = bank(4 + half, T // 2)
             for x in range(EXPERTS // 2):
@@ -136,129 +137,153 @@ def tile_moe_seb_none_kernel(
                 )
             nc.scalar.copy(gate2_all[:, half * T // 2 : (half + 1) * T // 2], spread[:])
 
-        got_bytes = keep.tile([P, T], U8, name="got_bytes", align_bytes=ALIGN)
+        gate1_cols = gate_columns(gate1_rows, 7, "gate1_cols")
+
+        got_bytes = keep.tile([P, T], U8, name="got_bytes", tag="got_bytes", align_bytes=ALIGN)
         got_planes = keep.tile([P, PASSES * T], U8, name="got_planes", align_bytes=ALIGN)
-        nc.vector.tensor_copy(got_bytes[:], dy_bytes[:].indirect(list2[:]))
-        for q in range(QUADRANTS):
-            source = IDLE_ROWS + q * PASSES * SCALE_ROWS
-            nc.sync.dma_start(
-                out=got_planes[q * QUADRANT : q * QUADRANT + SCALE_ROWS].bitcast(I32).rearrange("r (s w) -> r s w", s=PASSES),
-                in_=got_bytes[source : source + PASSES * SCALE_ROWS].bitcast(I32),
-            )
+
+        def move_scale_rows(first, last, queue):
+            for q in range(QUADRANTS):
+                source = IDLE_ROWS + q * PASSES * SCALE_ROWS
+                by_pass = got_planes[q * QUADRANT : q * QUADRANT + SCALE_ROWS].rearrange("r (s t) -> r s t", s=PASSES)
+                queue.dma_start(
+                    out=by_pass[:, :, slots(first, last)].bitcast(I32),
+                    in_=got_bytes[source : source + PASSES * SCALE_ROWS, slots(first, last)].bitcast(I32),
+                )
+
+        for first, last in ((0, PAIR), (PAIR, EXPERTS)):
+            nc.vector.tensor_copy(got_bytes[:, slots(first, last)], dy_bytes[:].indirect(entries(list2, first, last)))
+        move_scale_rows(0, PAIR, nc.sync)
         middle_codes = placed.tile([P, PAIR * PASSES, FP4_BYTES * H], U8, name="middle_codes", offset=0, align_bytes=ALIGN)
         load_w2_codes(PAIR, 2 * PAIR, middle_codes)
-        middle_plane = placed.tile(
-            [P, PAIR * PASSES * H], U8, name="middle_plane", offset=PAIR_CODE_BYTES + T, align_bytes=ALIGN
-        )
-        load_w2_scales(PAIR, 2 * PAIR, middle_plane)
+        move_scale_rows(PAIR, EXPERTS, nc.sync)
+
+        got_words = {}
 
         def gather_words(first, last, s, tag):
             words = keep.tile([P, (last - first) * SLOTS], U32, name="got_words", tag=tag, align_bytes=ALIGN)
-            nc.vector.tensor_copy(words[:], dy_codes[:, s * T :].indirect(entries(list2, first, last)))
-            return words
+            window = dy_codes[:, s * T : (s + 1) * T] if first == 0 else dy_codes[:, s * T :]
+            nc.vector.tensor_copy(words[:], window.indirect(entries(list2, first, last)))
+            for f in range(first, last):
+                got_words[f, s] = words[:, slots(f - first, f - first + 1)]
 
-        lead_words = [gather_words(0, PAIR, s, f"lead_words{s}") for s in range(PASSES)]
-        middle_words = [gather_words(PAIR, 2 * PAIR, s, f"middle_words{s}") for s in range(PASSES)]
-        late_words = [gather_words(2 * PAIR, EXPERTS, 0, "late_words0")]
+        for s in range(PASSES):
+            gather_words(0, PAIR, s, f"lead_words{s}")
+        gather_words(PAIR, 3 * PAIR, 0, "middle_words0")
+        gather_words(PAIR, 2 * PAIR, 1, "middle_words1")
 
         dc = [keep.tile([P, T], F32, name=f"dc{t}") for t in range(DC_TILES)]
-        TILE_SETS = ((1, 3), (0, 2))
 
-        def products(g, codes, plane, words, base):
-            sums = []
-            for side, tiles in enumerate(TILE_SETS):
-                dc_sums = bank(2 * g + side, 2 * PAIR_SLOTS)
-                sums.append(dc_sums)
-                for place, t in enumerate(tiles):
-                    for x in range(PAIR):
-                        f = g * PAIR + x
-                        for s in range(PASSES):
-                            matrix = (f - base) * PASSES + s
-                            nc.tensor.matmul_mx(
-                                out=dc_sums[:, slots(place * PAIR + x, place * PAIR + x + 1)],
-                                lhsT=codes[:, matrix, FP4_BYTES * P * t : FP4_BYTES * P * (t + 1)].bitcast(FP4X4),
-                                lhsT_scale=plane[:, matrix * H + P * t : matrix * H + P * (t + 1)],
-                                rhs=words[s][:, slots(f - base, f - base + 1)].bitcast(FP8X4),
-                                rhs_scale=got_planes[:, s * T + f * SLOTS : s * T + (f + 1) * SLOTS],
-                                start=(s == 0),
-                                stop=(s == PASSES - 1),
-                            )
-            return sums
-
-        def stage(g, side, dc_sums, gated):
-            staged = keep.tile([P, 2 * PAIR_SLOTS], F32, name="dc_staged", tag=f"staged{g}_{side}", align_bytes=ALIGN)
-            if gated:
-                gate = gate2_all[:, slots(g * PAIR, (g + 1) * PAIR)].unsqueeze(1).to_broadcast([P, 2, PAIR_SLOTS])
-                nc.vector.tensor_tensor(
-                    staged[:].rearrange("p (a j) -> p a j", a=2), dc_sums[:].rearrange("p (a j) -> p a j", a=2), gate, MULT
-                )
+        def products(number, parts, codes, plane, base):
+            dc_sums = bank(number, len(parts) * PAIR_SLOTS)
+            for place, (t, g) in enumerate(parts):
+                for x in range(PAIR):
+                    f = g * PAIR + x
+                    for s in range(PASSES):
+                        matrix = (f - base) * PASSES + s
+                        nc.tensor.matmul_mx(
+                            out=dc_sums[:, slots(place * PAIR + x, place * PAIR + x + 1)],
+                            lhsT=codes[:, matrix, FP4_BYTES * P * t : FP4_BYTES * P * (t + 1)].bitcast(FP4X4),
+                            lhsT_scale=plane[:, matrix * H + P * t : matrix * H + P * (t + 1)],
+                            rhs=got_words[f, s].bitcast(FP8X4),
+                            rhs_scale=got_planes[:, s * T + f * SLOTS : s * T + (f + 1) * SLOTS],
+                            start=(s == 0),
+                            stop=(s == PASSES - 1),
+                        )
+            staged = keep.tile([P, len(parts) * PAIR_SLOTS], F32, name=f"staged{parts[0][0]}_{parts[0][1]}")
+            first, last = parts[0][1] * PAIR, (parts[-1][1] + 1) * PAIR
+            if last - first == PAIR:
+                gate = gate2_all[:, slots(first, last)].unsqueeze(1).to_broadcast([P, len(parts), PAIR_SLOTS])
             else:
-                nc.scalar.copy(staged[:], dc_sums[:])
+                gate = gate2_all[:, slots(first, last)].rearrange("p (a j) -> p a j", j=PAIR_SLOTS)
+            nc.vector.tensor_tensor(
+                staged[:].rearrange("p (a j) -> p a j", j=PAIR_SLOTS),
+                dc_sums[:].rearrange("p (a j) -> p a j", j=PAIR_SLOTS),
+                gate,
+                MULT,
+            )
             return staged
 
-        def scatter_dc(g, side, place, staged, how):
-            window = dc[TILE_SETS[side][place]][:].indirect(entries(list2, g * PAIR, (g + 1) * PAIR))
-            values = staged[:, slots(place * PAIR, (place + 1) * PAIR)]
-            if how == "scalar":
-                nc.scalar.activation(window, values, COPY)
-            elif how == "vector":
-                nc.vector.tensor_copy(window, values)
+        def copy(engine, out, in_):
+            if engine == "scalar":
+                nc.scalar.activation(out, in_, COPY)
             else:
-                nc.vector.tensor_tensor(window, values, gate2_all[:, slots(g * PAIR, (g + 1) * PAIR)], MULT)
+                nc.vector.tensor_copy(out, in_)
 
-        sums = products(0, lead_codes, lead_plane, lead_words, 0)
-        staged = [stage(0, side, sums[side], True) for side in range(2)]
-        late_words.append(gather_words(2 * PAIR, EXPERTS, 1, "lead_words1"))
+        def scatter_dc(engine, t, first, last, values):
+            copy(engine, dc[t][:].indirect(entries(list2, first, last)), values)
+
+        def pick(engine, g, t, tag):
+            picked = keep.tile([P, PAIR_SLOTS], F32, name="picked", tag=tag, align_bytes=ALIGN)
+            copy(engine, picked[:], dc[t][:].indirect(entries(list1, g * PAIR, (g + 1) * PAIR)))
+            return picked
+
+        halves = (slots(0, PAIR), slots(PAIR, 2 * PAIR))
+        lead_sets = ((0,), (2, 1), (3,))
+        staged = [
+            products(side, [(t, 0) for t in tiles], lead_codes, early_plane, 0) for side, tiles in enumerate(lead_sets)
+        ]
+        gather_words(3 * PAIR, EXPERTS, 0, "lead_words0")
+        gather_words(2 * PAIR, EXPERTS, 1, "lead_words1")
         late_codes = keep.tile(
             [P, 2 * PAIR * PASSES, FP4_BYTES * H], U8, name="late_codes", tag="lead_codes", align_bytes=ALIGN
         )
         load_w2_codes(2 * PAIR, EXPERTS, late_codes)
-        late_plane = keep.tile([P, 2 * PAIR * PASSES * H], U8, name="late_plane", tag="lead_plane", align_bytes=ALIGN)
+        late_plane = keep.tile([P, 2 * PAIR * PASSES * H], U8, name="late_plane", tag="got_bytes", align_bytes=ALIGN)
         load_w2_scales(2 * PAIR, EXPERTS, late_plane)
-        scatter_dc(0, 0, 0, staged[0], "scalar")
-        scatter_dc(0, 0, 1, staged[0], "scalar")
-        scatter_dc(0, 1, 0, staged[1], "vector")
-        scatter_dc(0, 1, 1, staged[1], "scalar")
-        for g in range(1, PAIRS):
-            if g == 1:
-                sums = products(g, middle_codes, middle_plane, middle_words, PAIR)
-            else:
-                sums = products(g, late_codes, late_plane, late_words, 2 * PAIR)
-            staged = [stage(g, 0, sums[0], True), stage(g, 1, sums[1], g == 1)]
-            for place in range(2):
-                scatter_dc(g, 0, place, staged[0], "scalar")
-                scatter_dc(g, 1, place, staged[1], "vector" if g == 1 else "gated")
+        for side, tiles in enumerate(lead_sets):
+            for place, t in enumerate(tiles):
+                scatter_dc("scalar", t, 0, PAIR, staged[side][:, halves[place]])
 
-        gate1_rows = keep.tile([P, SLOTS], F32, name="gate1_rows", tag="staged0_1", align_bytes=ALIGN)
-        nc.sync.dma_start(out=gate1_rows[0:EXPERTS, :], in_=gate1[0].rearrange("(e u) -> e u", u=SLOTS))
+        middle_plane = early_plane[:, PAIR * PASSES * H :]
+        staged = [
+            products(3 * (1 - side), [(t, 1) for t in tiles], middle_codes, middle_plane, PAIR)
+            for side, tiles in enumerate(((1, 3), (0, 2)))
+        ]
+        for place in range(2):
+            scatter_dc("scalar", 1 + 2 * place, PAIR, 2 * PAIR, staged[0][:, halves[place]])
+            scatter_dc("vector", 2 * place, PAIR, 2 * PAIR, staged[1][:, halves[place]])
+
+        staged = {
+            t: products(4 + place, [(t, 2), (t, 3)], late_codes, late_plane, 2 * PAIR)
+            for place, t in enumerate((1, 3, 0, 2))
+        }
+        picked = {}
+        for g in (2, 3):
+            scatter_dc("scalar", 1, g * PAIR, (g + 1) * PAIR, staged[1][:, halves[g - 2]])
+        scatter_dc("vector", 0, 2 * PAIR, EXPERTS, staged[0][:])
+        scatter_dc("scalar", 3, 2 * PAIR, 3 * PAIR, staged[3][:, halves[0]])
+        scatter_dc("vector", 2, 2 * PAIR, 3 * PAIR, staged[2][:, halves[0]])
+        for g in range(PAIRS):
+            picked[g, 0] = pick("vector", g, 0, f"picked{g}_0")
+            picked[g, 1] = pick("scalar", g, 1, f"picked{g}_1")
+        scatter_dc("scalar", 3, 3 * PAIR, EXPERTS, staged[3][:, halves[1]])
+        scatter_dc("vector", 2, 3 * PAIR, EXPERTS, staged[2][:, halves[1]])
+
         w1_codes = placed.tile([P, EXPERTS, FP4_BYTES * K], U8, name="w1_codes", offset=0, align_bytes=ALIGN)
         nc.sync.dma_start(out=w1_codes[:].bitcast(I32), in_=w1t_words.bitcast(I32).rearrange("e s p w -> p (e s) w"))
-        w1_plane = middle_plane[:, 0 : EXPERTS * K]
+        w1_plane = early_plane[:, PAIR * PASSES * H :]
         load_scale_rows(nc, w1_plane, w1t_scales.bitcast(I32).rearrange("e s b w -> b (e s) w"), EXPERTS)
-        gate1_cols = gate_columns(gate1_rows, 0, "gate1_cols")
 
         result = [keep.tile([P, T], F32, name=f"result{b}") for b in range(ROW_BLOCKS)]
 
-        def pick(g):
-            picked = []
-            for t in range(DC_TILES):
-                picked.append(keep.tile([P, PAIR_SLOTS], F32, name=f"picked{g}_{t}", align_bytes=ALIGN))
-                window = dc[t][:].indirect(entries(list1, g * PAIR, (g + 1) * PAIR))
-                if t in TILE_SETS[0]:
-                    nc.scalar.activation(picked[t][:], window, COPY)
-                else:
-                    nc.vector.tensor_copy(picked[t][:], window)
-            return picked
+        by_slot = {}
 
-        def round_pair(g, picked):
+        def turn(g, tiles):
+            for x in range(PAIR):
+                if (g, x) not in by_slot:
+                    by_slot[g, x] = bank(PAIR * g + x, H)
+                for t in tiles:
+                    nc.tensor.transpose(
+                        by_slot[g, x][:, t * P : (t + 1) * P], picked[g, t][:, slots(x, x + 1)], identity[:]
+                    )
+
+        def round_pair(g):
             rounded = []
             for x in range(PAIR):
-                by_slot = bank((PAIR * g + x) % 4, H)
                 rounded.append(keep.tile([P, H], BF16, name="rounded", tag=f"rounded{g}_{x}", align_bytes=ALIGN))
-                for t in range(DC_TILES):
-                    nc.tensor.transpose(by_slot[:, t * P : (t + 1) * P], picked[t][:, slots(x, x + 1)], identity[:])
                 words = rounded[x][:].rearrange("j (u p d) -> j u p d", u=2, d=2)
-                turned = by_slot[:].rearrange("j (p u d) -> j u p d", u=2, d=2)
+                turned = by_slot[g, x][:].rearrange("j (p u d) -> j u p d", u=2, d=2)
                 weight = gate1_cols[:, g * PAIR + x : g * PAIR + x + 1]
                 if x == 0:
                     nc.scalar.activation(words, turned, COPY, scale=weight)
@@ -269,7 +294,7 @@ def tile_moe_seb_none_kernel(
         def quantise(g, rounded):
             grouped = keep.tile([P, PACK * PAIR_SLOTS], BF16, name="grouped", tag=f"grouped{g}", align_bytes=ALIGN)
             for x in range(PAIR):
-                turned_words = bank(4 + x, 2 * SLOTS)
+                turned_words = bank(6 * (g % 2) + x, 2 * SLOTS)
                 for u in range(2):
                     nc.tensor.transpose(
                         turned_words[:, slots(u, u + 1)], rounded[x][:].bitcast(F32)[:, u * P : (u + 1) * P], identity[:]
@@ -283,10 +308,11 @@ def tile_moe_seb_none_kernel(
             nc.vector.quantize_mx(out=da_codes[:].bitcast(FP8X4), scales=da_scales[:], in_=grouped[:])
             return da_codes, da_scales
 
-        def multiply_and_scatter(g, da_codes, da_scales):
-            offsets = entries(list1, g * PAIR, (g + 1) * PAIR)
+        def multiply(g, da_codes, da_scales):
+            sums = []
             for b in range(ROW_BLOCKS):
-                out_sums = bank(6 + b, PAIR_SLOTS)
+                out_sums = bank((2 + 2 * g) % BANKS + b if g < 2 else 6 * (g % 2) + b, PAIR_SLOTS)
+                sums.append(out_sums)
                 for x in range(PAIR):
                     e = g * PAIR + x
                     nc.tensor.matmul_mx(
@@ -298,10 +324,12 @@ def tile_moe_seb_none_kernel(
                         start=True,
                         stop=True,
                     )
-                if g + 1 < PAIRS:
-                    tag = f"grouped{g + 1}" if b == 0 else f"rounded{g + 1}_1"
-                else:
-                    tag = f"last_sums{b}"
+            return sums
+
+        def scatter_out(g, sums):
+            offsets = entries(list1, g * PAIR, (g + 1) * PAIR)
+            for b, out_sums in enumerate(sums):
+                tag = f"out_staged{g}_{b}"
                 out_staged = keep.tile([P, PAIR_SLOTS], F32, name="out_staged", tag=tag, align_bytes=ALIGN)
                 if b == 0:
                     nc.vector.tensor_copy(out_staged[:], out_sums[:])
@@ -310,17 +338,20 @@ def tile_moe_seb_none_kernel(
                     nc.scalar.copy(out_staged[:], out_sums[:])
                     nc.scalar.activation(result[b][:].indirect(offsets), out_staged[:], COPY)
 
-        picked = [pick(g) for g in range(PAIRS)]
-        rounded = [round_pair(g, picked[g]) for g in range(2)]
-        da = [quantise(0, rounded[0])]
-        for g in range(1, PAIRS):
-            if g + 1 < PAIRS:
-                rounded.append(round_pair(g + 1, picked[g + 1]))
-            da.append(quantise(g, rounded[g]))
-            multiply_and_scatter(g - 1, *da[g - 1])
-        multiply_and_scatter(PAIRS - 1, *da[PAIRS - 1])
+        for g in range(PAIRS):
+            turn(g, (0, 1))
+        for g in range(PAIRS):
+            picked[g, 2] = pick("vector", g, 2, f"picked{g}_2")
+            picked[g, 3] = pick("scalar", g, 3, f"picked{g}_3")
+        for g in range(PAIRS):
+            turn(g, (2, 3))
+        rounded = [round_pair(g) for g in range(PAIRS)]
+        da = [quantise(g, rounded[g]) for g in range(PAIRS)]
+        sums = [multiply(g, *da[g]) for g in range(PAIRS)]
+        for g in range(PAIRS):
+            scatter_out(g, sums[g])
 
         for b in range(ROW_BLOCKS):
             rows = slice(b * P, (b + 1) * P)
-            nc.sync.dma_start(out=out[rows, 0 : T // 2], in_=result[b][:, 0 : T // 2])
-            nc.scalar.dma_start(out=out[rows, T // 2 : T], in_=result[b][:, T // 2 : T])
+            queue = nc.sync if b == 0 else nc.scalar
+            queue.dma_start(out=out[rows, :], in_=result[b][:])

@@ -254,7 +254,7 @@ def tile_moe_seb_none_kernel(
         scatter_dc("vector", 0, 2 * PAIR, EXPERTS, staged[0][:])
         scatter_dc("scalar", 3, 2 * PAIR, 3 * PAIR, staged[3][:, halves[0]])
         scatter_dc("vector", 2, 2 * PAIR, 3 * PAIR, staged[2][:, halves[0]])
-        for g in range(PAIRS):
+        for g in range(2):
             picked[g, 0] = pick("vector", g, 0, f"picked{g}_0")
             picked[g, 1] = pick("scalar", g, 1, f"picked{g}_1")
         scatter_dc("scalar", 3, 3 * PAIR, EXPERTS, staged[3][:, halves[1]])
@@ -272,13 +272,15 @@ def tile_moe_seb_none_kernel(
         def turn(g, tiles):
             for x in range(PAIR):
                 if (g, x) not in by_slot:
-                    by_slot[g, x] = bank(PAIR * g + x, H)
+                    by_slot[g, x] = bank((PAIR * g + x) % 6, H)
                 for t in tiles:
                     nc.tensor.transpose(
                         by_slot[g, x][:, t * P : (t + 1) * P], picked[g, t][:, slots(x, x + 1)], identity[:]
                     )
 
         def round_pair(g):
+            if g < 3:
+                turn(g, (2, 3))
             rounded = []
             for x in range(PAIR):
                 rounded.append(keep.tile([P, H], BF16, name="rounded", tag=f"rounded{g}_{x}", align_bytes=ALIGN))
@@ -294,7 +296,7 @@ def tile_moe_seb_none_kernel(
         def quantise(g, rounded):
             grouped = keep.tile([P, PACK * PAIR_SLOTS], BF16, name="grouped", tag=f"grouped{g}", align_bytes=ALIGN)
             for x in range(PAIR):
-                turned_words = bank(6 * (g % 2) + x, 2 * SLOTS)
+                turned_words = bank(6 + x, 2 * SLOTS)
                 for u in range(2):
                     nc.tensor.transpose(
                         turned_words[:, slots(u, u + 1)], rounded[x][:].bitcast(F32)[:, u * P : (u + 1) * P], identity[:]
@@ -311,7 +313,7 @@ def tile_moe_seb_none_kernel(
         def multiply(g, da_codes, da_scales):
             sums = []
             for b in range(ROW_BLOCKS):
-                out_sums = bank((2 + 2 * g) % BANKS + b if g < 2 else 6 * (g % 2) + b, PAIR_SLOTS)
+                out_sums = bank(2 + 2 * (g % 2) + b, PAIR_SLOTS)
                 sums.append(out_sums)
                 for x in range(PAIR):
                     e = g * PAIR + x
@@ -329,8 +331,16 @@ def tile_moe_seb_none_kernel(
         def scatter_out(g, sums):
             offsets = entries(list1, g * PAIR, (g + 1) * PAIR)
             for b, out_sums in enumerate(sums):
-                tag = f"out_staged{g}_{b}"
-                out_staged = keep.tile([P, PAIR_SLOTS], F32, name="out_staged", tag=tag, align_bytes=ALIGN)
+                if g == 1:
+                    tag = "rounded0_0" if b == 0 else "picked0_2"
+                elif g + 1 < PAIRS:
+                    tag = f"rounded{g + 1}_{1 - b}"
+                else:
+                    tag = f"last_sums{b}"
+                if (g, b) == (0, 1):
+                    out_staged = shared[:, halves[0]]
+                else:
+                    out_staged = keep.tile([P, PAIR_SLOTS], F32, name="out_staged", tag=tag, align_bytes=ALIGN)
                 if b == 0:
                     nc.vector.tensor_copy(out_staged[:], out_sums[:])
                     nc.vector.tensor_copy(result[b][:].indirect(offsets), out_staged[:])
@@ -338,18 +348,36 @@ def tile_moe_seb_none_kernel(
                     nc.scalar.copy(out_staged[:], out_sums[:])
                     nc.scalar.activation(result[b][:].indirect(offsets), out_staged[:], COPY)
 
-        for g in range(PAIRS):
+        picked[2, 0] = pick("vector", 2, 0, "picked2_0")
+        picked[2, 1] = pick("scalar", 2, 1, "picked2_1")
+        for g in range(3):
             turn(g, (0, 1))
-        for g in range(PAIRS):
+        for g in range(3):
             picked[g, 2] = pick("vector", g, 2, f"picked{g}_2")
             picked[g, 3] = pick("scalar", g, 3, f"picked{g}_3")
-        for g in range(PAIRS):
-            turn(g, (2, 3))
-        rounded = [round_pair(g) for g in range(PAIRS)]
-        da = [quantise(g, rounded[g]) for g in range(PAIRS)]
-        sums = [multiply(g, *da[g]) for g in range(PAIRS)]
-        for g in range(PAIRS):
-            scatter_out(g, sums[g])
+        rounded = [round_pair(0)]
+        picked[3, 2] = pick("vector", 3, 2, "picked0_2")
+        picked[3, 1] = pick("scalar", 3, 1, "picked0_3")
+        rounded.append(round_pair(1))
+        da = [quantise(0, rounded[0])]
+        sums = [multiply(0, *da[0])]
+        picked[3, 3] = pick("scalar", 3, 3, "rounded0_0")
+        rounded.append(round_pair(2))
+        for g in range(1, PAIRS):
+            da.append(quantise(g, rounded[g]))
+            if g == 2:
+                turn(3, (1, 2, 3))
+                turn(3, (0,))
+            sums.append(multiply(g, *da[g]))
+            if g == 1:
+                shared = keep.tile([P, 2 * PAIR_SLOTS], F32, name="shared", tag="rounded1_0", align_bytes=ALIGN)
+            if g == 2:
+                rounded.append(round_pair(3))
+            scatter_out(g - 1, sums[g - 1])
+            if g == 1:
+                picked[3, 0] = shared[:, halves[1]]
+                copy("scalar", picked[3, 0], dc[0][:].indirect(entries(list1, 3 * PAIR, EXPERTS)))
+        scatter_out(PAIRS - 1, sums[PAIRS - 1])
 
         for b in range(ROW_BLOCKS):
             rows = slice(b * P, (b + 1) * P)

@@ -28,22 +28,30 @@ QUADRANTS = 4
 QUADRANT = P // QUADRANTS
 SCALE_ROWS = 4
 FP4_BYTES = 2
-BANKS = 8
 ALIGN = 64
 
 FLOPS = 2 * T * (PASSES * P * PACK * H + H * K)
 
 PAIR = 2
 PAIRS = EXPERTS // PAIR
+LAST = PAIRS - 1
 PAIR_SLOTS = PAIR * SLOTS
 PAIR_CODE_BYTES = PAIR * PASSES * H * FP4_BYTES
 
 BLOCKS = QUADRANTS * SCALE_ROWS
 IDLE_ROWS = P - PASSES * BLOCKS
 
+TURN_BANKS = 6
+WORD_BANK = 6
+OUT_BANK = 2
+
 
 def slots(first, last):
     return slice(first * SLOTS, last * SLOTS)
+
+
+def pair_slots(place):
+    return slots(place * PAIR, (place + 1) * PAIR)
 
 
 def entries(list_tile, first, last):
@@ -78,27 +86,37 @@ def tile_moe_seb_none_kernel(
             rows = w2t_scales.bitcast(I32)[first:last].rearrange("f s b w -> b (f s) w")
             load_scale_rows(nc, plane[:], rows, (last - first) * PASSES)
 
+        def load_gate_rows(gate, name):
+            rows = keep.tile([P, SLOTS], F32, name=name)
+            nc.sync.dma_start(out=rows[0:EXPERTS, :], in_=gate[0].rearrange("(e u) -> e u", u=SLOTS))
+            return rows
+
+        def copy(engine, target, source):
+            if engine is nc.scalar:
+                nc.scalar.activation(target, source, COPY)
+            else:
+                nc.vector.tensor_copy(target, source)
+
         list2 = keep.tile([P, T // STRIPE], U16, name="list2")
         nc.sync.dma_start(list2[:], offs2)
 
-        dy_bytes = placed.tile([P, 2 * T], U8, name="dy_bytes", offset=PAIR_CODE_BYTES - ALIGN, align_bytes=ALIGN)
+        dy_bytes_at = PAIR_CODE_BYTES - ALIGN
+        dy_bytes = placed.tile([P, 2 * T], U8, name="dy_bytes", offset=dy_bytes_at, align_bytes=ALIGN)
         nc.vector.memset(dy_bytes[0:IDLE_ROWS, 0:T].bitcast(I32), 0)
         nc.scalar.dma_start(
             out=dy_bytes[IDLE_ROWS:P, 0:T].bitcast(I32), in_=dy_scales.bitcast(I32).rearrange("s b w -> b s w")
         )
-        gate2_rows = keep.tile([P, SLOTS], F32, name="gate2_rows")
-        nc.sync.dma_start(out=gate2_rows[0:EXPERTS, :], in_=gate2[0].rearrange("(e u) -> e u", u=SLOTS))
+        gate2_rows = load_gate_rows(gate2, "gate2_rows")
         early_plane = keep.tile([P, 2 * PAIR * PASSES * H], U8, name="early_plane", align_bytes=ALIGN)
         load_w2_scales(0, 2 * PAIR, early_plane)
-        dy_codes = keep.tile([P, PASSES * T], U32, name="dy_codes", tag="dy_codes", align_bytes=ALIGN)
+        dy_codes = keep.tile([P, PASSES * T], U32, name="dy_codes", align_bytes=ALIGN)
         for s in range(PASSES):
             nc.sync.dma_start(
                 out=dy_codes[:, s * T : (s + 1) * T].bitcast(I32),
                 in_=dy_words[s].rearrange("p t d -> p (t d)").bitcast(I32),
             )
-        lead_codes = keep.tile(
-            [P, PAIR * PASSES, FP4_BYTES * H], U8, name="lead_codes", tag="lead_codes", align_bytes=ALIGN
-        )
+        pair_codes_shape = [P, PAIR * PASSES, FP4_BYTES * H]
+        lead_codes = keep.tile(pair_codes_shape, U8, name="lead_codes", align_bytes=ALIGN)
         load_w2_codes(0, PAIR, lead_codes)
 
         identity = keep.tile([P, P], F32, name="identity")
@@ -116,8 +134,7 @@ def tile_moe_seb_none_kernel(
 
         list1 = keep.tile([P, T // STRIPE], U16, name="list1")
         nc.sync.dma_start(list1[:], offs)
-        gate1_rows = keep.tile([P, SLOTS], F32, name="gate1_rows")
-        nc.sync.dma_start(out=gate1_rows[0:EXPERTS, :], in_=gate1[0].rearrange("(e u) -> e u", u=SLOTS))
+        gate1_rows = load_gate_rows(gate1, "gate1_rows")
 
         def gate_columns(rows, number, name):
             turned_gate = bank(number, SLOTS)
@@ -127,7 +144,7 @@ def tile_moe_seb_none_kernel(
             return cols
 
         gate2_cols = gate_columns(gate2_rows, 6, "gate2_cols")
-        gate2_all = keep.tile([P, T], F32, name="gate2_all", tag="gate2_all", align_bytes=ALIGN)
+        gate2_all = keep.tile([P, T], F32, name="gate2_all", align_bytes=ALIGN)
         for half in range(2):
             spread = bank(4 + half, T // 2)
             for x in range(EXPERTS // 2):
@@ -136,27 +153,36 @@ def tile_moe_seb_none_kernel(
                     spread[:, slots(x, x + 1)], gate2_cols[:, f : f + 1].to_broadcast([P, P]), identity[:]
                 )
             nc.scalar.copy(gate2_all[:, half * T // 2 : (half + 1) * T // 2], spread[:])
-
         gate1_cols = gate_columns(gate1_rows, 7, "gate1_cols")
 
         got_bytes = keep.tile([P, T], U8, name="got_bytes", tag="got_bytes", align_bytes=ALIGN)
         got_planes = keep.tile([P, PASSES * T], U8, name="got_planes", align_bytes=ALIGN)
 
-        def move_scale_rows(first, last, queue):
+        def move_scale_rows(first, last):
             for q in range(QUADRANTS):
                 source = IDLE_ROWS + q * PASSES * SCALE_ROWS
                 by_pass = got_planes[q * QUADRANT : q * QUADRANT + SCALE_ROWS].rearrange("r (s t) -> r s t", s=PASSES)
-                queue.dma_start(
+                nc.sync.dma_start(
                     out=by_pass[:, :, slots(first, last)].bitcast(I32),
                     in_=got_bytes[source : source + PASSES * SCALE_ROWS, slots(first, last)].bitcast(I32),
                 )
 
         for first, last in ((0, PAIR), (PAIR, EXPERTS)):
             nc.vector.tensor_copy(got_bytes[:, slots(first, last)], dy_bytes[:].indirect(entries(list2, first, last)))
-        move_scale_rows(0, PAIR, nc.sync)
-        middle_codes = placed.tile([P, PAIR * PASSES, FP4_BYTES * H], U8, name="middle_codes", offset=0, align_bytes=ALIGN)
+        move_scale_rows(0, PAIR)
+        middle_codes = placed.tile(pair_codes_shape, U8, name="middle_codes", offset=0, align_bytes=ALIGN)
         load_w2_codes(PAIR, 2 * PAIR, middle_codes)
-        move_scale_rows(PAIR, EXPERTS, nc.sync)
+        move_scale_rows(PAIR, EXPERTS)
+        late_codes = placed.tile(
+            [P, 2 * PAIR * PASSES, FP4_BYTES * H],
+            U8,
+            name="late_codes",
+            offset=dy_bytes_at + 2 * T - ALIGN,
+            align_bytes=ALIGN,
+        )
+        load_w2_codes(2 * PAIR, EXPERTS, late_codes)
+        late_plane = keep.tile([P, 2 * PAIR * PASSES * H], U8, name="late_plane", tag="got_bytes", align_bytes=ALIGN)
+        load_w2_scales(2 * PAIR, EXPERTS, late_plane)
 
         got_words = {}
 
@@ -190,7 +216,7 @@ def tile_moe_seb_none_kernel(
                             start=(s == 0),
                             stop=(s == PASSES - 1),
                         )
-            staged = keep.tile([P, len(parts) * PAIR_SLOTS], F32, name=f"staged{parts[0][0]}_{parts[0][1]}")
+            staged = keep.tile([P, len(parts) * PAIR_SLOTS], F32, name=f"staged{number}_{parts[0][1]}")
             first, last = parts[0][1] * PAIR, (parts[-1][1] + 1) * PAIR
             if last - first == PAIR:
                 gate = gate2_all[:, slots(first, last)].unsqueeze(1).to_broadcast([P, len(parts), PAIR_SLOTS])
@@ -204,104 +230,91 @@ def tile_moe_seb_none_kernel(
             )
             return staged
 
-        def copy(engine, out, in_):
-            if engine == "scalar":
-                nc.scalar.activation(out, in_, COPY)
-            else:
-                nc.vector.tensor_copy(out, in_)
+        def scatter_dc(engine, t, first_pair, last_pair, values):
+            copy(engine, dc[t][:].indirect(entries(list2, first_pair * PAIR, last_pair * PAIR)), values)
 
-        def scatter_dc(engine, t, first, last, values):
-            copy(engine, dc[t][:].indirect(entries(list2, first, last)), values)
+        picked = {}
 
-        def pick(engine, g, t, tag):
-            picked = keep.tile([P, PAIR_SLOTS], F32, name="picked", tag=tag, align_bytes=ALIGN)
-            copy(engine, picked[:], dc[t][:].indirect(entries(list1, g * PAIR, (g + 1) * PAIR)))
-            return picked
+        def pick(engine, g, t, target):
+            picked[g, t] = target
+            copy(engine, target, dc[t][:].indirect(entries(list1, g * PAIR, (g + 1) * PAIR)))
 
-        halves = (slots(0, PAIR), slots(PAIR, 2 * PAIR))
-        lead_sets = ((0,), (2, 1), (3,))
+        def pair_tile(tag):
+            return keep.tile([P, PAIR_SLOTS], F32, name="pair_tile", tag=tag, align_bytes=ALIGN)[:]
+
+        lead_tiles = ((0,), (2, 1), (3,))
         staged = [
-            products(side, [(t, 0) for t in tiles], lead_codes, early_plane, 0) for side, tiles in enumerate(lead_sets)
+            products(number, [(t, 0) for t in tiles], lead_codes, early_plane, 0)
+            for number, tiles in enumerate(lead_tiles)
         ]
         gather_words(3 * PAIR, EXPERTS, 0, "lead_words0")
         gather_words(2 * PAIR, EXPERTS, 1, "lead_words1")
-        late_codes = keep.tile(
-            [P, 2 * PAIR * PASSES, FP4_BYTES * H], U8, name="late_codes", tag="lead_codes", align_bytes=ALIGN
-        )
-        load_w2_codes(2 * PAIR, EXPERTS, late_codes)
-        late_plane = keep.tile([P, 2 * PAIR * PASSES * H], U8, name="late_plane", tag="got_bytes", align_bytes=ALIGN)
-        load_w2_scales(2 * PAIR, EXPERTS, late_plane)
-        for side, tiles in enumerate(lead_sets):
+        for number, tiles in enumerate(lead_tiles):
             for place, t in enumerate(tiles):
-                scatter_dc("scalar", t, 0, PAIR, staged[side][:, halves[place]])
+                scatter_dc(nc.scalar, t, 0, 1, staged[number][:, pair_slots(place)])
 
         middle_plane = early_plane[:, PAIR * PASSES * H :]
-        staged = [
-            products(3 * (1 - side), [(t, 1) for t in tiles], middle_codes, middle_plane, PAIR)
-            for side, tiles in enumerate(((1, 3), (0, 2)))
-        ]
+        for_scalar = products(3, [(1, 1), (3, 1)], middle_codes, middle_plane, PAIR)
+        for_vector = products(0, [(0, 1), (2, 1)], middle_codes, middle_plane, PAIR)
         for place in range(2):
-            scatter_dc("scalar", 1 + 2 * place, PAIR, 2 * PAIR, staged[0][:, halves[place]])
-            scatter_dc("vector", 2 * place, PAIR, 2 * PAIR, staged[1][:, halves[place]])
+            scatter_dc(nc.scalar, 1 + 2 * place, 1, 2, for_scalar[:, pair_slots(place)])
+            scatter_dc(nc.vector, 2 * place, 1, 2, for_vector[:, pair_slots(place)])
 
         staged = {
             t: products(4 + place, [(t, 2), (t, 3)], late_codes, late_plane, 2 * PAIR)
             for place, t in enumerate((1, 3, 0, 2))
         }
-        picked = {}
         for g in (2, 3):
-            scatter_dc("scalar", 1, g * PAIR, (g + 1) * PAIR, staged[1][:, halves[g - 2]])
-        scatter_dc("vector", 0, 2 * PAIR, EXPERTS, staged[0][:])
-        scatter_dc("scalar", 3, 2 * PAIR, 3 * PAIR, staged[3][:, halves[0]])
-        scatter_dc("vector", 2, 2 * PAIR, 3 * PAIR, staged[2][:, halves[0]])
+            scatter_dc(nc.scalar, 1, g, g + 1, staged[1][:, pair_slots(g - 2)])
+        scatter_dc(nc.vector, 0, 2, 4, staged[0][:])
+        scatter_dc(nc.scalar, 3, 2, 3, staged[3][:, pair_slots(0)])
+        scatter_dc(nc.vector, 2, 2, 3, staged[2][:, pair_slots(0)])
         for g in range(2):
-            picked[g, 0] = pick("vector", g, 0, f"picked{g}_0")
-            picked[g, 1] = pick("scalar", g, 1, f"picked{g}_1")
-        scatter_dc("scalar", 3, 3 * PAIR, EXPERTS, staged[3][:, halves[1]])
-        scatter_dc("vector", 2, 3 * PAIR, EXPERTS, staged[2][:, halves[1]])
+            pick(nc.vector, g, 0, pair_tile(f"picked{g}_0"))
+            pick(nc.scalar, g, 1, pair_tile(f"picked{g}_1"))
+        scatter_dc(nc.scalar, 3, 3, 4, staged[3][:, pair_slots(1)])
+        scatter_dc(nc.vector, 2, 3, 4, staged[2][:, pair_slots(1)])
 
         w1_codes = placed.tile([P, EXPERTS, FP4_BYTES * K], U8, name="w1_codes", offset=0, align_bytes=ALIGN)
         nc.sync.dma_start(out=w1_codes[:].bitcast(I32), in_=w1t_words.bitcast(I32).rearrange("e s p w -> p (e s) w"))
-        w1_plane = early_plane[:, PAIR * PASSES * H :]
+        w1_plane = middle_plane
         load_scale_rows(nc, w1_plane, w1t_scales.bitcast(I32).rearrange("e s b w -> b (e s) w"), EXPERTS)
 
         result = [keep.tile([P, T], F32, name=f"result{b}") for b in range(ROW_BLOCKS)]
-
         by_slot = {}
 
         def turn(g, tiles):
             for x in range(PAIR):
                 if (g, x) not in by_slot:
-                    by_slot[g, x] = bank((PAIR * g + x) % 6, H)
+                    by_slot[g, x] = bank((PAIR * g + x) % TURN_BANKS, H)
                 for t in tiles:
                     nc.tensor.transpose(
                         by_slot[g, x][:, t * P : (t + 1) * P], picked[g, t][:, slots(x, x + 1)], identity[:]
                     )
 
         def round_pair(g):
-            if g < 3:
-                turn(g, (2, 3))
             rounded = []
             for x in range(PAIR):
                 rounded.append(keep.tile([P, H], BF16, name="rounded", tag=f"rounded{g}_{x}", align_bytes=ALIGN))
-                words = rounded[x][:].rearrange("j (u p d) -> j u p d", u=2, d=2)
+                by_word = rounded[x][:].rearrange("j (u p d) -> j u p d", u=2, d=2)
                 turned = by_slot[g, x][:].rearrange("j (p u d) -> j u p d", u=2, d=2)
                 weight = gate1_cols[:, g * PAIR + x : g * PAIR + x + 1]
                 if x == 0:
-                    nc.scalar.activation(words, turned, COPY, scale=weight)
+                    nc.scalar.activation(by_word, turned, COPY, scale=weight)
                 else:
-                    nc.vector.tensor_scalar(words, turned, weight, None, MULT)
+                    nc.vector.tensor_scalar(by_word, turned, weight, None, MULT)
             return rounded
 
         def quantise(g, rounded):
-            grouped = keep.tile([P, PACK * PAIR_SLOTS], BF16, name="grouped", tag=f"grouped{g}", align_bytes=ALIGN)
+            grouped = keep.tile([P, PACK * PAIR_SLOTS], BF16, name=f"grouped{g}", align_bytes=ALIGN)
             for x in range(PAIR):
-                turned_words = bank(6 + x, 2 * SLOTS)
+                turned_words = bank(WORD_BANK + x, 2 * SLOTS)
                 for u in range(2):
                     nc.tensor.transpose(
                         turned_words[:, slots(u, u + 1)], rounded[x][:].bitcast(F32)[:, u * P : (u + 1) * P], identity[:]
                     )
-                (nc.scalar.copy if x == 0 else nc.vector.tensor_copy)(
+                move = nc.scalar.copy if x == 0 else nc.vector.tensor_copy
+                move(
                     grouped[:].bitcast(F32)[:, slots(2 * x, 2 * x + 2)].rearrange("p (j u) -> p j u", u=2),
                     turned_words[:].rearrange("p (u j) -> p j u", u=2),
                 )
@@ -313,12 +326,11 @@ def tile_moe_seb_none_kernel(
         def multiply(g, da_codes, da_scales):
             sums = []
             for b in range(ROW_BLOCKS):
-                out_sums = bank(2 + 2 * (g % 2) + b, PAIR_SLOTS)
-                sums.append(out_sums)
+                sums.append(bank(OUT_BANK + ROW_BLOCKS * (g % 2) + b, PAIR_SLOTS))
                 for x in range(PAIR):
                     e = g * PAIR + x
                     nc.tensor.matmul_mx(
-                        out=out_sums[:, slots(x, x + 1)],
+                        out=sums[b][:, slots(x, x + 1)],
                         lhsT=w1_codes[:, e, FP4_BYTES * P * b : FP4_BYTES * P * (b + 1)].bitcast(FP4X4),
                         lhsT_scale=w1_plane[:, e * K + P * b : e * K + P * (b + 1)],
                         rhs=da_codes[:, slots(x, x + 1)].bitcast(FP8X4),
@@ -328,58 +340,47 @@ def tile_moe_seb_none_kernel(
                     )
             return sums
 
-        def scatter_out(g, sums):
+        def scatter_out(g, sums, out_staged):
             offsets = entries(list1, g * PAIR, (g + 1) * PAIR)
-            for b, out_sums in enumerate(sums):
-                if g == 1:
-                    tag = "rounded0_0" if b == 0 else "picked0_2"
-                elif g + 1 < PAIRS:
-                    tag = f"rounded{g + 1}_{1 - b}"
-                else:
-                    tag = f"last_sums{b}"
-                if (g, b) == (0, 1):
-                    out_staged = shared[:, halves[0]]
-                else:
-                    out_staged = keep.tile([P, PAIR_SLOTS], F32, name="out_staged", tag=tag, align_bytes=ALIGN)
-                if b == 0:
-                    nc.vector.tensor_copy(out_staged[:], out_sums[:])
-                    nc.vector.tensor_copy(result[b][:].indirect(offsets), out_staged[:])
-                else:
-                    nc.scalar.copy(out_staged[:], out_sums[:])
-                    nc.scalar.activation(result[b][:].indirect(offsets), out_staged[:], COPY)
+            for b, engine in enumerate((nc.vector, nc.scalar)):
+                move = nc.vector.tensor_copy if engine is nc.vector and g < LAST else nc.scalar.copy
+                move(out_staged[b], sums[b][:])
+                copy(engine, result[b][:].indirect(offsets), out_staged[b])
 
-        picked[2, 0] = pick("vector", 2, 0, "picked2_0")
-        picked[2, 1] = pick("scalar", 2, 1, "picked2_1")
-        for g in range(3):
+        pick(nc.vector, 2, 0, pair_tile("picked2_0"))
+        pick(nc.scalar, 2, 1, pair_tile("picked2_1"))
+        for g in range(LAST):
             turn(g, (0, 1))
-        for g in range(3):
-            picked[g, 2] = pick("vector", g, 2, f"picked{g}_2")
-            picked[g, 3] = pick("scalar", g, 3, f"picked{g}_3")
-        rounded = [round_pair(0)]
-        picked[3, 2] = pick("vector", 3, 2, "picked0_2")
-        picked[3, 1] = pick("scalar", 3, 1, "picked0_3")
-        rounded.append(round_pair(1))
-        da = [quantise(0, rounded[0])]
-        sums = [multiply(0, *da[0])]
-        picked[3, 3] = pick("scalar", 3, 3, "rounded0_0")
-        rounded.append(round_pair(2))
-        for g in range(1, PAIRS):
-            da.append(quantise(g, rounded[g]))
-            if g == 2:
-                turn(3, (1, 2, 3))
-                turn(3, (0,))
-            sums.append(multiply(g, *da[g]))
-            if g == 1:
-                shared = keep.tile([P, 2 * PAIR_SLOTS], F32, name="shared", tag="rounded1_0", align_bytes=ALIGN)
-            if g == 2:
-                rounded.append(round_pair(3))
-            scatter_out(g - 1, sums[g - 1])
-            if g == 1:
-                picked[3, 0] = shared[:, halves[1]]
-                copy("scalar", picked[3, 0], dc[0][:].indirect(entries(list1, 3 * PAIR, EXPERTS)))
-        scatter_out(PAIRS - 1, sums[PAIRS - 1])
+        for g in range(LAST):
+            pick(nc.vector, g, 2, pair_tile(f"picked{g}_2"))
+            pick(nc.scalar, g, 3, pair_tile(f"picked{g}_3"))
 
-        for b in range(ROW_BLOCKS):
-            rows = slice(b * P, (b + 1) * P)
-            queue = nc.sync if b == 0 else nc.scalar
-            queue.dma_start(out=out[rows, :], in_=result[b][:])
+        turn(0, (2, 3))
+        rounded0 = round_pair(0)
+        pick(nc.vector, LAST, 2, pair_tile("picked0_2"))
+        pick(nc.scalar, LAST, 1, pair_tile("picked0_3"))
+        turn(1, (2, 3))
+        rounded1 = round_pair(1)
+        sums0 = multiply(0, *quantise(0, rounded0))
+        pick(nc.scalar, LAST, 3, pair_tile("rounded0_0"))
+        turn(2, (2, 3))
+        rounded2 = round_pair(2)
+
+        sums1 = multiply(1, *quantise(1, rounded1))
+        behind_pair1 = keep.tile([P, 2 * PAIR_SLOTS], F32, name="behind_pair1", tag="rounded1_0", align_bytes=ALIGN)
+        scatter_out(0, sums0, (pair_tile("rounded1_1"), behind_pair1[:, pair_slots(0)]))
+        pick(nc.scalar, LAST, 0, behind_pair1[:, pair_slots(1)])
+
+        da2 = quantise(2, rounded2)
+        turn(LAST, (1, 2, 3))
+        turn(LAST, (0,))
+        sums2 = multiply(2, *da2)
+        rounded3 = round_pair(LAST)
+        scatter_out(1, sums1, (pair_tile("rounded0_0"), pair_tile("picked0_2")))
+
+        sums3 = multiply(LAST, *quantise(LAST, rounded3))
+        scatter_out(2, sums2, (pair_tile("rounded3_1"), pair_tile("rounded3_0")))
+        scatter_out(LAST, sums3, (pair_tile("last_sums0"), pair_tile("last_sums1")))
+
+        for b, queue in enumerate((nc.sync, nc.scalar)):
+            queue.dma_start(out=out[b * P : (b + 1) * P, :], in_=result[b][:])

@@ -357,7 +357,7 @@ def tile_moe_seb_none_kernel(
 
         turn(0, (2, 3))
         rounded0 = round_pair(0)
-        pick(nc.vector, LAST, 2, pair_tile("picked0_2"))
+        pick(nc.scalar, LAST, 2, pair_tile("picked0_2"))
         pick(nc.scalar, LAST, 1, pair_tile("picked0_3"))
         turn(1, (2, 3))
         rounded1 = round_pair(1)

@@ -152,6 +152,9 @@ def tile_moe_seb_none_kernel(
                 nc.tensor.transpose(
                     spread[:, slots(x, x + 1)], gate2_cols[:, f : f + 1].to_broadcast([P, P]), identity[:]
                 )
+            if half == 0:
+                gate2_first = keep.tile([P, PAIR_SLOTS], F32, name="gate2_first", tag="gate2_first", align_bytes=ALIGN)
+                nc.scalar.copy(gate2_first[:], spread[:, 0:PAIR_SLOTS])
             nc.scalar.copy(gate2_all[:, half * T // 2 : (half + 1) * T // 2], spread[:])
         gate1_cols = gate_columns(gate1_rows, 7, "gate1_cols")
 
@@ -188,19 +191,20 @@ def tile_moe_seb_none_kernel(
 
         def gather_words(first, last, s, tag):
             words = keep.tile([P, (last - first) * SLOTS], U32, name="got_words", tag=tag, align_bytes=ALIGN)
-            window = dy_codes[:, s * T : (s + 1) * T] if first == 0 else dy_codes[:, s * T :]
+            window = dy_codes[:, s * T : (s + 1) * T] if first <= PAIR else dy_codes[:, s * T :]
             nc.vector.tensor_copy(words[:], window.indirect(entries(list2, first, last)))
             for f in range(first, last):
                 got_words[f, s] = words[:, slots(f - first, f - first + 1)]
 
         for s in range(PASSES):
             gather_words(0, PAIR, s, f"lead_words{s}")
-        gather_words(PAIR, 3 * PAIR, 0, "middle_words0")
-        gather_words(PAIR, 2 * PAIR, 1, "middle_words1")
+        for s in range(PASSES):
+            gather_words(PAIR, 2 * PAIR, s, f"middle_words{s}")
+        gather_words(2 * PAIR, 3 * PAIR, 0, "third_words0")
 
         dc = [keep.tile([P, T], F32, name=f"dc{t}") for t in range(DC_TILES)]
 
-        def products(number, parts, codes, plane, base):
+        def products(number, parts, codes, plane, base, gates):
             dc_sums = bank(number, len(parts) * PAIR_SLOTS)
             for place, (t, g) in enumerate(parts):
                 for x in range(PAIR):
@@ -219,9 +223,9 @@ def tile_moe_seb_none_kernel(
             staged = keep.tile([P, len(parts) * PAIR_SLOTS], F32, name=f"staged{number}_{parts[0][1]}")
             first, last = parts[0][1] * PAIR, (parts[-1][1] + 1) * PAIR
             if last - first == PAIR:
-                gate = gate2_all[:, slots(first, last)].unsqueeze(1).to_broadcast([P, len(parts), PAIR_SLOTS])
+                gate = gates[:, slots(first, last)].unsqueeze(1).to_broadcast([P, len(parts), PAIR_SLOTS])
             else:
-                gate = gate2_all[:, slots(first, last)].rearrange("p (a j) -> p a j", j=PAIR_SLOTS)
+                gate = gates[:, slots(first, last)].rearrange("p (a j) -> p a j", j=PAIR_SLOTS)
             nc.vector.tensor_tensor(
                 staged[:].rearrange("p (a j) -> p a j", j=PAIR_SLOTS),
                 dc_sums[:].rearrange("p (a j) -> p a j", j=PAIR_SLOTS),
@@ -244,24 +248,28 @@ def tile_moe_seb_none_kernel(
 
         lead_tiles = ((0,), (2, 1), (3,))
         staged = [
-            products(number, [(t, 0) for t in tiles], lead_codes, early_plane, 0)
+            products(number, [(t, 0) for t in tiles], lead_codes, early_plane, 0, gate2_all if number else gate2_first)
             for number, tiles in enumerate(lead_tiles)
         ]
-        gather_words(3 * PAIR, EXPERTS, 0, "lead_words0")
+        gather_words(3 * PAIR, EXPERTS, 0, "gate2_first")
         gather_words(2 * PAIR, EXPERTS, 1, "lead_words1")
         for number, tiles in enumerate(lead_tiles):
             for place, t in enumerate(tiles):
-                scatter_dc(nc.scalar, t, 0, 1, staged[number][:, pair_slots(place)])
+                if t == 0:
+                    copy(nc.scalar, dc[0][:].indirect(entries(list2, 0, 1)), staged[0][:, slots(0, 1)])
+                else:
+                    scatter_dc(nc.scalar, t, 0, 1, staged[number][:, pair_slots(place)])
 
         middle_plane = early_plane[:, PAIR * PASSES * H :]
-        for_scalar = products(3, [(1, 1), (3, 1)], middle_codes, middle_plane, PAIR)
-        for_vector = products(0, [(0, 1), (2, 1)], middle_codes, middle_plane, PAIR)
+        for_scalar = products(3, [(1, 1), (3, 1)], middle_codes, middle_plane, PAIR, gate2_all)
+        for_vector = products(0, [(0, 1), (2, 1)], middle_codes, middle_plane, PAIR, gate2_all)
         for place in range(2):
             scatter_dc(nc.scalar, 1 + 2 * place, 1, 2, for_scalar[:, pair_slots(place)])
             scatter_dc(nc.vector, 2 * place, 1, 2, for_vector[:, pair_slots(place)])
+        copy(nc.vector, dc[0][:].indirect(entries(list2, 1, PAIR)), staged[0][:, slots(1, PAIR)])
 
         staged = {
-            t: products(4 + place, [(t, 2), (t, 3)], late_codes, late_plane, 2 * PAIR)
+            t: products(4 + place, [(t, 2), (t, 3)], late_codes, late_plane, 2 * PAIR, gate2_all)
             for place, t in enumerate((1, 3, 0, 2))
         }
         for g in (2, 3):

@@ -268,20 +268,19 @@ def tile_moe_seb_none_kernel(
             scatter_dc(nc.vector, 2 * place, 1, 2, for_vector[:, pair_slots(place)])
         copy(nc.vector, dc[0][:].indirect(entries(list2, 1, PAIR)), staged[0][:, slots(1, PAIR)])
 
-        staged = {
-            t: products(4 + place, [(t, 2), (t, 3)], late_codes, late_plane, 2 * PAIR, gate2_all)
-            for place, t in enumerate((1, 3, 0, 2))
-        }
-        for g in (2, 3):
-            scatter_dc(nc.scalar, 1, g, g + 1, staged[1][:, pair_slots(g - 2)])
-        scatter_dc(nc.vector, 0, 2, 4, staged[0][:])
-        scatter_dc(nc.scalar, 3, 2, 3, staged[3][:, pair_slots(0)])
-        scatter_dc(nc.vector, 2, 2, 3, staged[2][:, pair_slots(0)])
+        for_scalar = [products(2 + g, [(1, g), (3, g)], late_codes, late_plane, 2 * PAIR, gate2_all) for g in (2, 3)]
+        for_vector = [products(6 + t // 2, [(t, 2), (t, 3)], late_codes, late_plane, 2 * PAIR, gate2_all) for t in (0, 2)]
+        for place in range(2):
+            scatter_dc(nc.scalar, 1 + 2 * place, 2, 3, for_scalar[0][:, pair_slots(place)])
+        scatter_dc(nc.scalar, 1, 3, 4, for_scalar[1][:, pair_slots(0)])
+        copy(nc.scalar, dc[3][:].indirect(entries(list2, 6, 7)), for_scalar[1][:, slots(2, 3)])
+        scatter_dc(nc.vector, 0, 2, 4, for_vector[0][:])
+        scatter_dc(nc.vector, 2, 2, 3, for_vector[1][:, pair_slots(0)])
         for g in range(2):
             pick(nc.vector, g, 0, pair_tile(f"picked{g}_0"))
             pick(nc.scalar, g, 1, pair_tile(f"picked{g}_1"))
-        scatter_dc(nc.scalar, 3, 3, 4, staged[3][:, pair_slots(1)])
-        scatter_dc(nc.vector, 2, 3, 4, staged[2][:, pair_slots(1)])
+        copy(nc.scalar, dc[3][:].indirect(entries(list2, 7, 8)), for_scalar[1][:, slots(3, 4)])
+        scatter_dc(nc.vector, 2, 3, 4, for_vector[1][:, pair_slots(1)])
 
         w1_codes = placed.tile([P, EXPERTS, FP4_BYTES * K], U8, name="w1_codes", offset=0, align_bytes=ALIGN)
         nc.sync.dma_start(out=w1_codes[:].bitcast(I32), in_=w1t_words.bitcast(I32).rearrange("e s p w -> p (e s) w"))
@@ -332,9 +331,9 @@ def tile_moe_seb_none_kernel(
             return da_codes, da_scales
 
         def multiply(g, da_codes, da_scales):
-            sums = []
-            for b in range(ROW_BLOCKS):
-                sums.append(bank(OUT_BANK + ROW_BLOCKS * (g % 2) + b, PAIR_SLOTS))
+            sums = {}
+            for b in reversed(range(ROW_BLOCKS)) if g == LAST else range(ROW_BLOCKS):
+                sums[b] = bank(OUT_BANK + ROW_BLOCKS * (g % 2) + b, PAIR_SLOTS)
                 for x in range(PAIR):
                     e = g * PAIR + x
                     nc.tensor.matmul_mx(
@@ -350,9 +349,10 @@ def tile_moe_seb_none_kernel(
 
         def scatter_out(g, sums, out_staged):
             offsets = entries(list1, g * PAIR, (g + 1) * PAIR)
-            for b, engine in enumerate((nc.vector, nc.scalar)):
-                move = nc.vector.tensor_copy if engine is nc.vector and g < LAST else nc.scalar.copy
+            for b in sums:
+                move = nc.vector.tensor_copy if b == 0 and g < LAST else nc.scalar.copy
                 move(out_staged[b], sums[b][:])
+            for b, engine in enumerate((nc.vector, nc.scalar)):
                 copy(engine, result[b][:].indirect(offsets), out_staged[b])
 
         pick(nc.vector, 2, 0, pair_tile("picked2_0"))

@@ -255,10 +255,7 @@ def tile_moe_seb_none_kernel(
         gather_words(2 * PAIR, EXPERTS, 1, "lead_words1")
         for number, tiles in enumerate(lead_tiles):
             for place, t in enumerate(tiles):
-                if t == 0:
-                    copy(nc.scalar, dc[0][:].indirect(entries(list2, 0, 1)), staged[0][:, slots(0, 1)])
-                else:
-                    scatter_dc(nc.scalar, t, 0, 1, staged[number][:, pair_slots(place)])
+                scatter_dc(nc.scalar, t, 0, 1, staged[number][:, pair_slots(place)])
 
         middle_plane = early_plane[:, PAIR * PASSES * H :]
         for_scalar = products(3, [(1, 1), (3, 1)], middle_codes, middle_plane, PAIR, gate2_all)
@@ -266,7 +263,6 @@ def tile_moe_seb_none_kernel(
         for place in range(2):
             scatter_dc(nc.scalar, 1 + 2 * place, 1, 2, for_scalar[:, pair_slots(place)])
             scatter_dc(nc.vector, 2 * place, 1, 2, for_vector[:, pair_slots(place)])
-        copy(nc.vector, dc[0][:].indirect(entries(list2, 1, PAIR)), staged[0][:, slots(1, PAIR)])
 
         for_scalar = [products(2 + g, [(1, g), (3, g)], late_codes, late_plane, 2 * PAIR, gate2_all) for g in (2, 3)]
         for_vector = [products(6 + t // 2, [(t, 2), (t, 3)], late_codes, late_plane, 2 * PAIR, gate2_all) for t in (0, 2)]
@@ -350,7 +346,7 @@ def tile_moe_seb_none_kernel(
         def scatter_out(g, sums, out_staged):
             offsets = entries(list1, g * PAIR, (g + 1) * PAIR)
             for b in sums:
-                move = nc.vector.tensor_copy if b == 0 and g < LAST else nc.scalar.copy
+                move = nc.vector.tensor_copy if b == 0 and g < 2 else nc.scalar.copy
                 move(out_staged[b], sums[b][:])
             for b, engine in enumerate((nc.vector, nc.scalar)):
                 copy(engine, result[b][:].indirect(offsets), out_staged[b])

from contextlib import ExitStack

import concourse.mybir as mybir

F32 = mybir.dt.float32
BF16 = mybir.dt.bfloat16
I32 = mybir.dt.int32
U32 = mybir.dt.uint32
U16 = mybir.dt.uint16
U8 = mybir.dt.uint8
FP8X4 = mybir.dt.float8_e4m3fn_x4
FP4X4 = mybir.dt.float4_e2m1fn_x4
MULT = mybir.AluOpType.mult
COPY = mybir.ActivationFunctionType.Copy

P = 128
T = 1024
EXPERTS = 8
SLOTS = 128
H = 512
K = 256
PACK = 4
PASSES = 2
DC_TILES = H // P
ROW_BLOCKS = K // P
STRIPE = 16
QUADRANTS = 4
QUADRANT = P // QUADRANTS
SCALE_ROWS = 4
FP4_BYTES = 2
ALIGN = 64

FLOPS = 2 * T * (PASSES * P * PACK * H + H * K)

PAIR = 2
PAIRS = EXPERTS // PAIR
LAST = PAIRS - 1
PAIR_SLOTS = PAIR * SLOTS
PAIR_CODE_BYTES = PAIR * PASSES * H * FP4_BYTES

BLOCKS = QUADRANTS * SCALE_ROWS
IDLE_ROWS = P - PASSES * BLOCKS

TURN_BANKS = 6
WORD_BANK = 6
OUT_BANK = 2


def slots(first, last):
    return slice(first * SLOTS, last * SLOTS)


def pair_slots(place):
    return slots(place * PAIR, (place + 1) * PAIR)


def entries(list_tile, first, last):
    return list_tile[:, first * SLOTS // STRIPE : last * SLOTS // STRIPE]


def load_scale_rows(nc, plane, rows, matrices):
    by_matrix = plane.bitcast(I32).rearrange("p (m w) -> p m w", m=matrices)
    by_place = rows.rearrange("(q r) m w -> r q m w", r=SCALE_ROWS)
    for r in range(SCALE_ROWS):
        nc.sync.dma_start(out=by_matrix[r:P:QUADRANT], in_=by_place[r])


def tile_moe_seb_none_kernel(
    tc, dy_words, dy_scales, w2t_words, w2t_scales, w1t_words, w1t_scales, gate1, gate2, offs, offs2, out
):
    nc = tc.nc
    with ExitStack() as ctx:
        keep = ctx.enter_context(tc.tile_pool(name="keep", bufs=1))
        placed = ctx.enter_context(tc.tile_pool(name="placed", bufs=1))
        psum = ctx.enter_context(tc.psum_pool(name="psum", bufs=1))

        def bank(number, width):
            return psum.tile([P, width], F32, name="bank", tag=f"bank{number}")

        def load_w2_codes(first, last, codes):
            nc.sync.dma_start(
                out=codes[:].bitcast(I32), in_=w2t_words.bitcast(I32)[first:last].rearrange("f s p w -> p (f s) w")
            )

        def load_w2_scales(first, last, plane):
            rows = w2t_scales.bitcast(I32)[first:last].rearrange("f s b w -> b (f s) w")
            load_scale_rows(nc, plane[:], rows, (last - first) * PASSES)

        def load_gate_rows(gate, name):
            rows = keep.tile([P, SLOTS], F32, name=name)
            nc.sync.dma_start(out=rows[0:EXPERTS, :], in_=gate[0].rearrange("(e u) -> e u", u=SLOTS))
            return rows

        def copy(engine, target, source):
            if engine is nc.scalar:
                nc.scalar.activation(target, source, COPY)
            else:
                nc.vector.tensor_copy(target, source)

        list2 = keep.tile([P, T // STRIPE], U16, name="list2")
        nc.sync.dma_start(list2[:], offs2)

        dy_bytes_at = PAIR_CODE_BYTES - ALIGN
        dy_bytes = placed.tile([P, 2 * T], U8, name="dy_bytes", offset=dy_bytes_at, align_bytes=ALIGN)
        nc.vector.memset(dy_bytes[0:IDLE_ROWS, 0:T].bitcast(I32), 0)
        nc.scalar.dma_start(
            out=dy_bytes[IDLE_ROWS:P, 0:T].bitcast(I32), in_=dy_scales.bitcast(I32).rearrange("s b w -> b s w")
        )
        gate2_rows = load_gate_rows(gate2, "gate2_rows")
        early_plane = keep.tile([P, 2 * PAIR * PASSES * H], U8, name="early_plane", align_bytes=ALIGN)
        load_w2_scales(0, 2 * PAIR, early_plane)
        dy_codes = keep.tile([P, PASSES * T], U32, name="dy_codes", align_bytes=ALIGN)
        for s in range(PASSES):
            nc.sync.dma_start(
                out=dy_codes[:, s * T : (s + 1) * T].bitcast(I32),
                in_=dy_words[s].rearrange("p t d -> p (t d)").bitcast(I32),
            )
        pair_codes_shape = [P, PAIR * PASSES, FP4_BYTES * H]
        lead_codes = keep.tile(pair_codes_shape, U8, name="lead_codes", align_bytes=ALIGN)
        load_w2_codes(0, PAIR, lead_codes)

        identity = keep.tile([P, P], F32, name="identity")
        ones = keep.tile([P, P], F32, name="ones")
        nc.gpsimd.memset(ones[:], 1.0)
        nc.gpsimd.affine_select(
            out=identity[:],
            in_=ones[:],
            pattern=[[-1, P]],
            compare_op=mybir.AluOpType.is_equal,
            fill=0.0,
            base=0,
            channel_multiplier=1,
        )

        list1 = keep.tile([P, T // STRIPE], U16, name="list1")
        nc.sync.dma_start(list1[:], offs)
        gate1_rows = load_gate_rows(gate1, "gate1_rows")

        def gate_columns(rows, number, name):
            turned_gate = bank(number, SLOTS)
            nc.tensor.transpose(turned_gate[:], rows[:], identity[:])
            cols = keep.tile([P, EXPERTS], F32, name=name)
            nc.scalar.copy(cols[:], turned_gate[:, 0:EXPERTS])
            return cols

        gate2_cols = gate_columns(gate2_rows, 6, "gate2_cols")
        gate2_all = keep.tile([P, T], F32, name="gate2_all", align_bytes=ALIGN)
        for half in range(2):
            spread = bank(4 + half, T // 2)
            for x in range(EXPERTS // 2):
                f = half * EXPERTS // 2 + x
                nc.tensor.transpose(
                    spread[:, slots(x, x + 1)], gate2_cols[:, f : f + 1].to_broadcast([P, P]), identity[:]
                )
            if half == 0:
                gate2_first = keep.tile([P, PAIR_SLOTS], F32, name="gate2_first", tag="gate2_first", align_bytes=ALIGN)
                nc.scalar.copy(gate2_first[:], spread[:, 0:PAIR_SLOTS])
            nc.scalar.copy(gate2_all[:, half * T // 2 : (half + 1) * T // 2], spread[:])
        gate1_cols = gate_columns(gate1_rows, 7, "gate1_cols")

        got_bytes = keep.tile([P, T], U8, name="got_bytes", tag="got_bytes", align_bytes=ALIGN)
        got_planes = keep.tile([P, PASSES * T], U8, name="got_planes", align_bytes=ALIGN)

        def move_scale_rows(first, last):
            for q in range(QUADRANTS):
                source = IDLE_ROWS + q * PASSES * SCALE_ROWS
                by_pass = got_planes[q * QUADRANT : q * QUADRANT + SCALE_ROWS].rearrange("r (s t) -> r s t", s=PASSES)
                nc.sync.dma_start(
                    out=by_pass[:, :, slots(first, last)].bitcast(I32),
                    in_=got_bytes[source : source + PASSES * SCALE_ROWS, slots(first, last)].bitcast(I32),
                )

        for first, last in ((0, PAIR), (PAIR, EXPERTS)):
            nc.vector.tensor_copy(got_bytes[:, slots(first, last)], dy_bytes[:].indirect(entries(list2, first, last)))
        move_scale_rows(0, PAIR)
        middle_codes = placed.tile(pair_codes_shape, U8, name="middle_codes", offset=0, align_bytes=ALIGN)
        load_w2_codes(PAIR, 2 * PAIR, middle_codes)
        move_scale_rows(PAIR, EXPERTS)
        late_codes = placed.tile(
            [P, 2 * PAIR * PASSES, FP4_BYTES * H],
            U8,
            name="late_codes",
            offset=dy_bytes_at + 2 * T - ALIGN,
            align_bytes=ALIGN,
        )
        load_w2_codes(2 * PAIR, EXPERTS, late_codes)
        late_plane = keep.tile([P, 2 * PAIR * PASSES * H], U8, name="late_plane", tag="got_bytes", align_bytes=ALIGN)
        load_w2_scales(2 * PAIR, EXPERTS, late_plane)

        got_words = {}

        def gather_words(first, last, s, tag):
            words = keep.tile([P, (last - first) * SLOTS], U32, name="got_words", tag=tag, align_bytes=ALIGN)
            window = dy_codes[:, s * T : (s + 1) * T] if first <= PAIR else dy_codes[:, s * T :]
            nc.vector.tensor_copy(words[:], window.indirect(entries(list2, first, last)))
            for f in range(first, last):
                got_words[f, s] = words[:, slots(f - first, f - first + 1)]

        for s in range(PASSES):
            gather_words(0, PAIR, s, f"lead_words{s}")
        for s in range(PASSES):
            gather_words(PAIR, 2 * PAIR, s, f"middle_words{s}")
        gather_words(2 * PAIR, 3 * PAIR, 0, "third_words0")

        dc = [keep.tile([P, T], F32, name=f"dc{t}") for t in range(DC_TILES)]

        def products(number, parts, codes, plane, base, gates):
            dc_sums = bank(number, len(parts) * PAIR_SLOTS)
            for place, (t, g) in enumerate(parts):
                for x in range(PAIR):
                    f = g * PAIR + x
                    for s in range(PASSES):
                        matrix = (f - base) * PASSES + s
                        nc.tensor.matmul_mx(
                            out=dc_sums[:, slots(place * PAIR + x, place * PAIR + x + 1)],
                            lhsT=codes[:, matrix, FP4_BYTES * P * t : FP4_BYTES * P * (t + 1)].bitcast(FP4X4),
                            lhsT_scale=plane[:, matrix * H + P * t : matrix * H + P * (t + 1)],
                            rhs=got_words[f, s].bitcast(FP8X4),
                            rhs_scale=got_planes[:, s * T + f * SLOTS : s * T + (f + 1) * SLOTS],
                            start=(s == 0),
                            stop=(s == PASSES - 1),
                        )
            staged = keep.tile([P, len(parts) * PAIR_SLOTS], F32, name=f"staged{number}_{parts[0][1]}")
            first, last = parts[0][1] * PAIR, (parts[-1][1] + 1) * PAIR
            if last - first == PAIR:
                gate = gates[:, slots(first, last)].unsqueeze(1).to_broadcast([P, len(parts), PAIR_SLOTS])
            else:
                gate = gates[:, slots(first, last)].rearrange("p (a j) -> p a j", j=PAIR_SLOTS)
            nc.vector.tensor_tensor(
                staged[:].rearrange("p (a j) -> p a j", j=PAIR_SLOTS),
                dc_sums[:].rearrange("p (a j) -> p a j", j=PAIR_SLOTS),
                gate,
                MULT,
            )
            return staged

        def scatter_dc(engine, t, first_pair, last_pair, values):
            copy(engine, dc[t][:].indirect(entries(list2, first_pair * PAIR, last_pair * PAIR)), values)

        picked = {}

        def pick(engine, g, t, target):
            picked[g, t] = target
            copy(engine, target, dc[t][:].indirect(entries(list1, g * PAIR, (g + 1) * PAIR)))

        def pair_tile(tag):
            return keep.tile([P, PAIR_SLOTS], F32, name="pair_tile", tag=tag, align_bytes=ALIGN)[:]

        lead_tiles = ((0,), (2, 1), (3,))
        staged = [
            products(number, [(t, 0) for t in tiles], lead_codes, early_plane, 0, gate2_all if number else gate2_first)
            for number, tiles in enumerate(lead_tiles)
        ]
        gather_words(3 * PAIR, EXPERTS, 0, "gate2_first")
        gather_words(2 * PAIR, EXPERTS, 1, "lead_words1")
        for number, tiles in enumerate(lead_tiles):
            for place, t in enumerate(tiles):
                scatter_dc(nc.scalar, t, 0, 1, staged[number][:, pair_slots(place)])

        middle_plane = early_plane[:, PAIR * PASSES * H :]
        for_scalar = products(3, [(1, 1), (3, 1)], middle_codes, middle_plane, PAIR, gate2_all)
        for_vector = products(0, [(0, 1), (2, 1)], middle_codes, middle_plane, PAIR, gate2_all)
        for place in range(2):
            scatter_dc(nc.scalar, 1 + 2 * place, 1, 2, for_scalar[:, pair_slots(place)])
            scatter_dc(nc.vector, 2 * place, 1, 2, for_vector[:, pair_slots(place)])

        for_scalar = [products(2 + g, [(1, g), (3, g)], late_codes, late_plane, 2 * PAIR, gate2_all) for g in (2, 3)]
        for_vector = [products(6 + t // 2, [(t, 2), (t, 3)], late_codes, late_plane, 2 * PAIR, gate2_all) for t in (0, 2)]
        for place in range(2):
            scatter_dc(nc.scalar, 1 + 2 * place, 2, 3, for_scalar[0][:, pair_slots(place)])
        scatter_dc(nc.scalar, 1, 3, 4, for_scalar[1][:, pair_slots(0)])
        copy(nc.scalar, dc[3][:].indirect(entries(list2, 6, 7)), for_scalar[1][:, slots(2, 3)])
        scatter_dc(nc.vector, 0, 2, 4, for_vector[0][:])
        scatter_dc(nc.vector, 2, 2, 3, for_vector[1][:, pair_slots(0)])
        for g in range(2):
            pick(nc.vector, g, 0, pair_tile(f"picked{g}_0"))
            pick(nc.scalar, g, 1, pair_tile(f"picked{g}_1"))
        copy(nc.scalar, dc[3][:].indirect(entries(list2, 7, 8)), for_scalar[1][:, slots(3, 4)])
        scatter_dc(nc.vector, 2, 3, 4, for_vector[1][:, pair_slots(1)])

        w1_codes = placed.tile([P, EXPERTS, FP4_BYTES * K], U8, name="w1_codes", offset=0, align_bytes=ALIGN)
        nc.sync.dma_start(out=w1_codes[:].bitcast(I32), in_=w1t_words.bitcast(I32).rearrange("e s p w -> p (e s) w"))
        w1_plane = middle_plane
        load_scale_rows(nc, w1_plane, w1t_scales.bitcast(I32).rearrange("e s b w -> b (e s) w"), EXPERTS)

        result = [keep.tile([P, T], F32, name=f"result{b}") for b in range(ROW_BLOCKS)]
        by_slot = {}

        def turn(g, tiles):
            for x in range(PAIR):
                if (g, x) not in by_slot:
                    by_slot[g, x] = bank((PAIR * g + x) % TURN_BANKS, H)
                for t in tiles:
                    nc.tensor.transpose(
                        by_slot[g, x][:, t * P : (t + 1) * P], picked[g, t][:, slots(x, x + 1)], identity[:]
                    )

        def round_pair(g):
            rounded = []
            for x in range(PAIR):
                rounded.append(keep.tile([P, H], BF16, name="rounded", tag=f"rounded{g}_{x}", align_bytes=ALIGN))
                by_word = rounded[x][:].rearrange("j (u p d) -> j u p d", u=2, d=2)
                turned = by_slot[g, x][:].rearrange("j (p u d) -> j u p d", u=2, d=2)
                weight = gate1_cols[:, g * PAIR + x : g * PAIR + x + 1]
                if x == 0:
                    nc.scalar.activation(by_word, turned, COPY, scale=weight)
                else:
                    nc.vector.tensor_scalar(by_word, turned, weight, None, MULT)
            return rounded

        def quantise(g, rounded):
            grouped = keep.tile([P, PACK * PAIR_SLOTS], BF16, name=f"grouped{g}", align_bytes=ALIGN)
            for x in range(PAIR):
                turned_words = bank(WORD_BANK + x, 2 * SLOTS)
                for u in range(2):
                    nc.tensor.transpose(
                        turned_words[:, slots(u, u + 1)], rounded[x][:].bitcast(F32)[:, u * P : (u + 1) * P], identity[:]
                    )
                move = nc.scalar.copy if x == 0 else nc.vector.tensor_copy
                move(
                    grouped[:].bitcast(F32)[:, slots(2 * x, 2 * x + 2)].rearrange("p (j u) -> p j u", u=2),
                    turned_words[:].rearrange("p (u j) -> p j u", u=2),
                )
            da_codes = keep.tile([P, PAIR_SLOTS], U32, name=f"da_codes{g}", align_bytes=ALIGN)
            da_scales = keep.tile([P, PAIR_SLOTS], U8, name=f"da_scales{g}", align_bytes=ALIGN)
            nc.vector.quantize_mx(out=da_codes[:].bitcast(FP8X4), scales=da_scales[:], in_=grouped[:])
            return da_codes, da_scales

        def multiply(g, da_codes, da_scales):
            sums = {}
            for b in reversed(range(ROW_BLOCKS)) if g == LAST else range(ROW_BLOCKS):
                sums[b] = bank(OUT_BANK + ROW_BLOCKS * (g % 2) + b, PAIR_SLOTS)
                for x in range(PAIR):
                    e = g * PAIR + x
                    nc.tensor.matmul_mx(
                        out=sums[b][:, slots(x, x + 1)],
                        lhsT=w1_codes[:, e, FP4_BYTES * P * b : FP4_BYTES * P * (b + 1)].bitcast(FP4X4),
                        lhsT_scale=w1_plane[:, e * K + P * b : e * K + P * (b + 1)],
                        rhs=da_codes[:, slots(x, x + 1)].bitcast(FP8X4),
                        rhs_scale=da_scales[:, slots(x, x + 1)],
                        start=True,
                        stop=True,
                    )
            return sums

        def scatter_out(g, sums, out_staged):
            offsets = entries(list1, g * PAIR, (g + 1) * PAIR)
            for b in sums:
                move = nc.vector.tensor_copy if b == 0 and g < 2 else nc.scalar.copy
                move(out_staged[b], sums[b][:])
            for b, engine in enumerate((nc.vector, nc.scalar)):
                copy(engine, result[b][:].indirect(offsets), out_staged[b])

        pick(nc.vector, 2, 0, pair_tile("picked2_0"))
        pick(nc.scalar, 2, 1, pair_tile("picked2_1"))
        for g in range(LAST):
            turn(g, (0, 1))
        for g in range(LAST):
            pick(nc.vector, g, 2, pair_tile(f"picked{g}_2"))
            pick(nc.scalar, g, 3, pair_tile(f"picked{g}_3"))

        turn(0, (2, 3))
        rounded0 = round_pair(0)
        pick(nc.scalar, LAST, 2, pair_tile("picked0_2"))
        pick(nc.scalar, LAST, 1, pair_tile("picked0_3"))
        turn(1, (2, 3))
        rounded1 = round_pair(1)
        sums0 = multiply(0, *quantise(0, rounded0))
        pick(nc.scalar, LAST, 3, pair_tile("rounded0_0"))
        turn(2, (2, 3))
        rounded2 = round_pair(2)

        sums1 = multiply(1, *quantise(1, rounded1))
        behind_pair1 = keep.tile([P, 2 * PAIR_SLOTS], F32, name="behind_pair1", tag="rounded1_0", align_bytes=ALIGN)
        scatter_out(0, sums0, (pair_tile("rounded1_1"), behind_pair1[:, pair_slots(0)]))
        pick(nc.scalar, LAST, 0, behind_pair1[:, pair_slots(1)])

        da2 = quantise(2, rounded2)
        turn(LAST, (1, 2, 3))
        turn(LAST, (0,))
        sums2 = multiply(2, *da2)
        rounded3 = round_pair(LAST)
        scatter_out(1, sums1, (pair_tile("rounded0_0"), pair_tile("picked0_2")))

        sums3 = multiply(LAST, *quantise(LAST, rounded3))
        scatter_out(2, sums2, (pair_tile("rounded3_1"), pair_tile("rounded3_0")))
        scatter_out(LAST, sums3, (pair_tile("last_sums0"), pair_tile("last_sums1")))

        for b, queue in enumerate((nc.sync, nc.scalar)):
            queue.dma_start(out=out[b * P : (b + 1) * P, :], in_=result[b][:])
